import numpy as np
import ml_dtypes


def mxq(x, axis, fmt="e4m3"):
    dtype, down = {"e4m3": (ml_dtypes.float8_e4m3fn, 7), "e5m2": (ml_dtypes.float8_e5m2, 14)}[fmt]
    v = np.moveaxis(np.asarray(x, np.float32).astype(ml_dtypes.bfloat16).astype(np.float64), axis, -1)
    blocks = v.reshape(v.shape[:-1] + (-1, 32))
    amax = np.abs(blocks).max(-1, keepdims=True)
    byte = np.maximum(np.where(amax > 0, np.frexp(amax)[1] - 1 + 127, 0) - down, 1)
    scale = np.exp2(byte - 127.0)
    codes = (blocks / scale).astype(np.float32).astype(dtype).astype(np.float64)
    return np.moveaxis((codes * scale).reshape(v.shape), -1, axis)


WIDE = False


def mx_kscale(k):
    if not WIDE:
        return np.ones(k)
    levels = np.array([10, -10, 5, -5, 0])
    if k % 512:
        return np.exp2(np.random.permutation(np.resize(levels, k // 32))).repeat(32)
    a = np.empty((k // 512, 16))
    for p in range(k // 512):
        a[p, :8] = np.random.permutation(np.resize(levels, 8))
        for g in range(8):
            far = levels[np.abs(levels - a[p, g]) >= 10]
            a[p, g + 8] = far[np.random.randint(len(far))]
    return np.exp2(a.ravel()).repeat(32)


def f64(x):
    return np.asarray(x).astype(np.float64)


def striped(idx):
    return np.tile(idx.reshape(-1, 16).T, (8, 1)).astype(np.uint16)


def unstriped(offs):
    return offs[:16].T.reshape(-1).astype(np.int64)


E2M1 = np.array([0.0, 0.5, 1.0, 1.5, 2.0, 3.0, 4.0, 6.0, -0.0, -0.5, -1.0, -1.5, -2.0, -3.0, -4.0, -6.0])


def pack_weight(w, fmt):
    k, n = w.shape
    w = f64(np.asarray(w, np.float32).astype(ml_dtypes.bfloat16)).reshape(k // 32, 32, n)
    amax = np.abs(w).max(1)
    if fmt == "e4m3":
        byte = np.frexp(amax)[1] - 1 + 127 - 7
    else:
        mant, ex = np.frexp(amax / 6.0)
        byte = np.where(mant > 0.5, ex, ex - 1) + 127
    byte = np.clip(np.where(amax > 0, byte, 1), 1, 254)
    scaled = (w * np.exp2(127.0 - byte)[:, None, :]).reshape(k, n).astype(np.float32)
    by_word = np.ascontiguousarray(scaled.reshape(k // 512, 128, 4, n).transpose(0, 1, 3, 2))
    if fmt == "e4m3":
        words = by_word.astype(ml_dtypes.float8_e4m3fn).view(np.uint8)
    else:
        c = by_word.astype(ml_dtypes.float4_e2m1fn).view(np.uint8) & 0xF
        words = (c[..., 0::2] | (c[..., 1::2] << 4)).reshape(k // 512, 128, 2 * n)
    return np.ascontiguousarray(words), np.ascontiguousarray(byte.astype(np.uint8).reshape(k // 512, 16, n))


def unpack_weight(words, scales, fmt):
    g, _, n = scales.shape
    words = np.ascontiguousarray(words).reshape(g, 128, n, -1)
    if fmt == "e4m3":
        vals = words.view(ml_dtypes.float8_e4m3fn).astype(np.float64)
    else:
        nib = np.empty((g, 128, n, 4), np.uint8)
        nib[..., 0::2] = words & 0xF
        nib[..., 1::2] = words >> 4
        vals = E2M1[nib]
    vals = vals * np.repeat(np.exp2(scales.astype(np.float64) - 127.0), 8, axis=1)[..., None]
    return vals.transpose(0, 1, 3, 2).reshape(g * 512, n)


def sigmoid(v):
    return 1.0 / (1.0 + np.exp(-np.maximum(v, -700.0)))


K, T, E, C, H, N = 512, 512, 4, 256, 512, 512


def by_expert(wq, xq):
    return np.concatenate([wq[e].T @ xq[:, e * C:(e + 1) * C] for e in range(E)], axis=1)


def setup_inputs():
    n = np.random.standard_normal
    s = mx_kscale(K)[:, None]
    u = mx_kscale(H)
    first = np.random.permutation(np.repeat(np.arange(E), T // E))
    second = (first + 1 + np.random.permutation(np.repeat(np.arange(E - 1), -(-T // (E - 1)))[:T])) % E
    while np.bincount(second, minlength=E).max() != T // E:
        load = np.bincount(second, minlength=E); hi, lo = int(load.argmax()), int(load.argmin())
        t = np.flatnonzero((second == hi) & (first != lo))[0]; second[t] = lo
    slot_token = np.empty(E * C, np.int64); pos = np.empty((2, T), np.int64); fill = np.zeros(E, np.int64)
    place = np.stack([np.random.permutation(C) for _ in range(E)])
    for r, deal in enumerate((first, second)):
        for t in np.random.permutation(T):
            e = deal[t]; j = e * C + place[e, fill[e]]; fill[e] += 1; slot_token[j] = t; pos[r, t] = j
    g = np.random.uniform(0.2, 0.8, T)
    w1 = [pack_weight(m, "e2m1") for m in n((E, K, H)) / np.sqrt(K) / s[None]]
    w3 = [pack_weight(m, "e2m1") for m in n((E, K, H)) / np.sqrt(K) / s[None] * u[None, None, :]]
    w2 = [pack_weight(m, "e2m1") for m in n((E, H, N)) / np.sqrt(H) / u[None, :, None]]
    w_slot = np.empty(E * C); w_slot[pos[0]] = g; w_slot[pos[1]] = 1.0 - g
    return {
        "xT": (n((K, T)) * s).astype(np.float32),
        "w1_words": np.stack([m[0] for m in w1]),
        "w1_scales": np.stack([m[1] for m in w1]),
        "w3_words": np.stack([m[0] for m in w3]),
        "w3_scales": np.stack([m[1] for m in w3]),
        "w2_words": np.stack([m[0] for m in w2]),
        "w2_scales": np.stack([m[1] for m in w2]),
        "gate": np.tile(w_slot, (K, 1)).astype(np.float32),
        "offs": striped(slot_token),
        "pos1": striped(pos[0]),
        "pos2": striped(pos[1]),
    }


def reference(xT, w1_words, w1_scales, w3_words, w3_scales, w2_words, w2_scales, gate, offs, pos1, pos2):
    idx = unstriped(offs)
    w1 = np.stack([unpack_weight(w1_words[e], w1_scales[e], "e2m1") for e in range(E)])
    w3 = np.stack([unpack_weight(w3_words[e], w3_scales[e], "e2m1") for e in range(E)])
    w2 = np.stack([unpack_weight(w2_words[e], w2_scales[e], "e2m1") for e in range(E)])
    xq = mxq(f64(gate) * f64(xT)[:, idx], 0, "e4m3")
    h = sigmoid(by_expert(w1, xq))
    h = h * by_expert(w3, xq)
    y = by_expert(w2, mxq(h, 0, "e4m3"))
    return y[:, unstriped(pos1)] + y[:, unstriped(pos2)]

@@ -1,0 +1,252 @@
+from contextlib import ExitStack
+
+import concourse.mybir as mybir
+from concourse.masks import make_identity
+
+K, T, E, C, H, N = 512, 512, 4, 256, 512, 512
+S = E * C
+FLOPS = 2 * S * (2 * K * H + H * N)
+
+F32 = mybir.dt.float32
+BF16 = mybir.dt.bfloat16
+I32 = mybir.dt.int32
+U32 = mybir.dt.uint32
+U16 = mybir.dt.uint16
+U8 = mybir.dt.uint8
+FP8X4 = mybir.dt.float8_e4m3fn_x4
+FP4X4 = mybir.dt.float4_e2m1fn_x4
+MULT = mybir.AluOpType.mult
+ADD = mybir.AluOpType.add
+SIGMOID = mybir.ActivationFunctionType.Sigmoid
+
+P = 128
+PACK = 4
+CH = 128
+STRIPE = 16
+
+
+PAD = 16
+GROUPS = [512, 256, 256]
+LOADS = [
+    ('sync', 'offs'),
+    ('sync', 'x', 0),
+    ('scalar', 'gate', 0, 0, 1),
+    ('sync', 'x', 1),
+    ('scalar', 'gate', 0, 1, 2),
+    ('sync', 'x', 2),
+    ('scalar', 'gate', 0, 2, 3),
+    ('sync', 'x', 3),
+    ('scalar', 'gate', 0, 3, 4),
+    ('sync', 'gate', 1, 0, 2),
+    ('sync', 'gate', 1, 2, 4),
+    ('sync', 'scales', 'w1', 0, 2),
+    ('sync', 'gate', 2, 0, 2),
+    ('sync', 'scales', 'w1', 2, 4),
+    ('gpsimd', 'scales', 'w3', 0, 2),
+    ('gpsimd', 'scales', 'w3', 2, 4),
+    ('sync', 'words', 'w1', 0, 4),
+    ('gpsimd', 'scales', 'w2', 0, 2),
+    ('gpsimd', 'scales', 'w2', 2, 4),
+    ('sync', 'gate', 2, 2, 4),
+    ('sync', 'words', 'w3', 0, 4),
+    ('sync', 'words', 'w2', 0, 4),
+    ('sync', 'pos1'),
+    ('sync', 'pos2'),
+]
+LEAD = {'gather': -3.566, 'first': 0.0, 'mult': 0.89, 'turn': 1.158, 'quant': 2.167, 'second': 3.44}
+A_BUFS, B_BUFS, T_BUFS = 3, 2, 2
+Y_PIECES = [256, 256, 256, 128, 128]
+ZERO_ON = 'gpsimd'
+ADD_ON = ["vector", "vector", "vector", "vector", "vector"]
+PIECES = [(0, 0, T), (1, 0, T), (2, 0, T), (3, 0, T // 2), (3, T // 2, T // 2)]
+
+
+def tile_moe_pre_glu_sigmoid_kernel(
+    tc, xT, w1_words, w1_scales, w3_words, w3_scales, w2_words, w2_scales, gate, offs, pos1, pos2, out
+):
+    nc = tc.nc
+    engines = {"sync": nc.sync, "scalar": nc.scalar, "gpsimd": nc.gpsimd, "vector": nc.vector}
+    starts = [sum(GROUPS[:g]) for g in range(len(GROUPS))]
+    pad = PAD if max(GROUPS) >= T else 0
+    with ExitStack() as ctx:
+        keep = ctx.enter_context(tc.tile_pool(name="keep", bufs=1))
+        work = ctx.enter_context(tc.tile_pool(name="work", bufs=4))
+        psum = ctx.enter_context(tc.psum_pool(name="psum", bufs=1))
+
+        lists = {
+            "offs": (keep.tile([P, S // STRIPE], U16, name="offs_sb"), offs),
+            "pos1": (keep.tile([P, T // STRIPE], U16, name="pos1_sb"), pos1),
+            "pos2": (keep.tile([P, T // STRIPE], U16, name="pos2_sb"), pos2),
+        }
+        x_plane = [keep.tile([P, T + pad], F32, name=f"x_plane{t}") for t in range(PACK)]
+        gate_sb = [keep.tile([P, PACK, w], F32, name=f"gate{g}") for g, w in enumerate(GROUPS)]
+        xg = [keep.tile([P, PACK, w], F32, name=f"xg{g}") for g, w in enumerate(GROUPS)]
+        words = {}
+        scales = {}
+        for name in ("w1", "w3", "w2"):
+            words[name] = keep.tile([P, E, 2 * H], U8, name=f"{name}_words_sb", align_bytes=64)
+            scales[name] = keep.tile([P, E, H], U8, name=f"{name}_scales_sb", align_bytes=64)
+        src_words = {"w1": w1_words, "w3": w3_words, "w2": w2_words}
+        src_scales = {"w1": w1_scales, "w3": w3_scales, "w2": w2_scales}
+        ident = keep.tile([P, P], F32, name="ident")
+        warm = keep.tile([P, 8], F32, name="warm")
+        warm_out = keep.tile([P, 8], F32, name="warm_out")
+
+        x_rows = xT.rearrange("(p t) n -> t p n", t=PACK)
+        gate_rows = gate.rearrange("(p t) s -> p t s", t=PACK)
+
+        def load(queue, kind, *args):
+            q = engines[queue]
+            if kind in lists:
+                q.dma_start(lists[kind][0][:], lists[kind][1])
+            elif kind == "x":
+                q.dma_start(x_plane[args[0]][:, 0:T], x_rows[args[0]])
+            elif kind == "gate":
+                g, t0, t1 = args
+                q.dma_start(gate_sb[g][:, t0:t1, :], gate_rows[:, t0:t1, starts[g] : starts[g] + GROUPS[g]])
+            elif kind == "words":
+                name, e0, e1 = args
+                src = src_words[name].rearrange("e s p b -> p (e s) b")
+                q.dma_start(words[name][:, e0:e1, :].bitcast(I32), src[:, e0:e1, :].bitcast(I32))
+            else:
+                name, r0, r1 = args
+                src = src_scales[name].rearrange("e s (q r) n -> r q (e s) n", r=4)
+                for r in range(r0, r1):
+                    q.dma_start(scales[name][r:P:32, :, :].bitcast(I32), src[r].bitcast(I32))
+
+        nc.vector.memset(warm[:], 0.0)
+        for name in ("w1", "w3", "w2"):
+            engines[ZERO_ON].memset(scales[name][:].rearrange("p e n -> p (e n)").bitcast(I32), 0)
+        if pad:
+            for t in range(PACK):
+                nc.vector.memset(x_plane[t][:, T : T + pad], 0.0)
+        for item in LOADS:
+            load(*item)
+        nc.scalar.activation(warm_out[:], warm[:], SIGMOID)
+        make_identity(nc, ident[:])
+
+        h_codes = keep.tile([P, S], U32, name="h_codes", align_bytes=64)
+        h_scales = keep.tile([P, S], U8, name="h_scales", align_bytes=64)
+        y = [keep.tile([P, S], F32, name=f"y{nt}") for nt in range(N // P)]
+        held = {}
+        a_banks = [psum.tile([P, H], F32, name=f"a{j}") for j in range(A_BUFS)]
+        b_banks = [psum.tile([P, H], F32, name=f"b{j}") for j in range(B_BUFS)]
+        t_banks = [psum.tile([P, H], F32, name=f"t{j}") for j in range(T_BUFS)]
+        y_bank = psum.tile([P, H], F32, name="y_bank")
+
+        def gather_x(g):
+            s0, width = starts[g], GROUPS[g]
+            for t in range(PACK):
+                nc.vector.tensor_tensor(
+                    xg[g][:, t, :],
+                    x_plane[t][:].indirect(lists["offs"][0][:, s0 // STRIPE : (s0 + width) // STRIPE]),
+                    gate_sb[g][:, t, :],
+                    MULT,
+                )
+
+        def first_layer(c):
+            s0 = c * CH
+            e = s0 // C
+            g = max(j for j in range(len(GROUPS)) if starts[j] <= s0)
+            c0 = s0 - starts[g]
+            xb = work.tile([P, CH, PACK], BF16, name="xb", align_bytes=64)
+            nc.scalar.copy(
+                xb[:].rearrange("p (c i) t -> p c t i", i=4),
+                xg[g][:, :, c0 : c0 + CH].rearrange("p t (c i) -> p c t i", i=4),
+            )
+            x_codes = work.tile([P, CH], U32, name="x_codes", align_bytes=64, bufs=8)
+            x_scales = work.tile([P, CH], U8, name="x_scales", align_bytes=64, bufs=8)
+            nc.vector.quantize_mx(x_codes[:].bitcast(FP8X4), x_scales[:], xb[:].rearrange("p c t -> p (c t)"))
+            a = a_banks[c % A_BUFS]
+            b = b_banks[c % B_BUFS]
+            for acc, name in ((a, "w1"), (b, "w3")):
+                nc.tensor.matmul_mx(
+                    acc[:],
+                    lhsT=x_codes[:].bitcast(FP8X4),
+                    lhsT_scale=x_scales[:],
+                    rhs=words[name][:, e, :].bitcast(FP4X4),
+                    rhs_scale=scales[name][:, e, :],
+                    start=True,
+                    stop=True,
+                )
+            sig = work.tile([P, H], F32, name="sig", bufs=8)
+            nc.scalar.activation(sig[:], a[:], SIGMOID)
+            held[c] = (sig, b)
+
+        def multiply(c):
+            sig, b = held[c]
+            ht = work.tile([P, H], BF16, name="ht", align_bytes=64)
+            nc.vector.tensor_tensor(ht[:], b[:], sig[:], MULT)
+            held[c] = ht
+
+        def turn(c):
+            pairs = held[c][:].bitcast(F32)
+            turned = t_banks[c % T_BUFS][:, 0 : 2 * CH].rearrange("p (u c) -> p u c", u=2)
+            for u in range(2):
+                nc.tensor.transpose(turned[:, u, :], pairs[:, u : H // 2 : 2], ident[:])
+            hb = work.tile([P, CH * PACK], BF16, name="hb", align_bytes=64, bufs=8)
+            nc.scalar.copy(
+                hb[:].bitcast(F32).rearrange("p (c u) -> p c u", u=2),
+                turned.rearrange("p u c -> p c u"),
+            )
+            held[c] = hb
+
+        def quantize_h(c):
+            s0 = c * CH
+            nc.vector.quantize_mx(h_codes[:, s0 : s0 + CH].bitcast(FP8X4), h_scales[:, s0 : s0 + CH], held[c][:])
+
+        def second_layer(nt, s0, width, bank):
+            step = min(width, C)
+            for lo in range(s0, s0 + width, step):
+                e = lo // C
+                nc.tensor.matmul_mx(
+                    bank[:, lo - s0 : lo - s0 + step],
+                    lhsT=words["w2"][:, e, 2 * P * nt : 2 * P * (nt + 1)].bitcast(FP4X4),
+                    lhsT_scale=scales["w2"][:, e, P * nt : P * (nt + 1)],
+                    rhs=h_codes[:, lo : lo + step].bitcast(FP8X4),
+                    rhs_scale=h_scales[:, lo : lo + step],
+                    start=True,
+                    stop=True,
+                )
+            nc.scalar.copy(y[nt][:, s0 : s0 + width], bank[:, 0:width])
+
+        steps = [(starts[g] // CH + LEAD["gather"], gather_x, (g,)) for g in range(len(GROUPS))]
+        for c in range(S // CH):
+            steps.append((c + LEAD["first"], first_layer, (c,)))
+            steps.append((c + LEAD["mult"], multiply, (c,)))
+            steps.append((c + LEAD["turn"], turn, (c,)))
+            steps.append((c + LEAD["quant"], quantize_h, (c,)))
+        s0 = 0
+        for width in Y_PIECES:
+            steps.append(((s0 + width) // CH - 1 + LEAD["second"], second_layer, (0, s0, width, y_bank if s0 + width < S else a_banks[(S // CH - 2) % A_BUFS])))
+            s0 += width
+        for step in sorted(steps, key=lambda item: item[0]):
+            step[1](*step[2])
+
+        last = S // CH - 1
+        early = [b_banks[last % B_BUFS], t_banks[last % T_BUFS], y_bank]
+        late = [a_banks[last % A_BUFS], b_banks[(last - 1) % B_BUFS], b_banks[(last - 2) % B_BUFS]]
+        for nt in range(1, N // P):
+            second_layer(nt, 0, 2 * C, early[nt - 1])
+            second_layer(nt, 2 * C, 2 * C, late[nt - 1])
+
+        def fetch(nt, t0, width):
+            got = []
+            for name in ("pos1", "pos2"):
+                g = work.tile([P, width], F32, name="got", tag=f"got{width}", bufs=6)
+                nc.vector.tensor_copy(g[:], y[nt][:].indirect(lists[name][0][:, t0 // STRIPE : (t0 + width) // STRIPE]))
+                got.append(g)
+            return got
+
+        def combine(j, nt, t0, width, got):
+            res = work.tile([P, width], F32, name="res", tag=f"res{width}")
+            engines[ADD_ON[j]].tensor_tensor(res[:], got[0][:], got[1][:], ADD)
+            nc.sync.dma_start(out[nt * P : (nt + 1) * P, t0 : t0 + width], res[:])
+
+        last = None
+        for j, piece in enumerate(PIECES):
+            got = fetch(*piece)
+            if last is not None:
+                combine(*last)
+            last = (j,) + piece + (got,)
+        combine(*last)

@@ -30,35 +30,43 @@ GROUPS = [512, 256, 256]
 LOADS = [
     ('sync', 'offs'),
     ('sync', 'x', 0),
-    ('scalar', 'gate', 0, 0, 1),
     ('sync', 'x', 1),
-    ('scalar', 'gate', 0, 1, 2),
+    ('scalar', 'gate', 0, 0, 1),
     ('sync', 'x', 2),
-    ('scalar', 'gate', 0, 2, 3),
     ('sync', 'x', 3),
-    ('scalar', 'gate', 0, 3, 4),
+    ('scalar', 'gate', 0, 1, 2),
     ('sync', 'gate', 1, 0, 2),
+    ('scalar', 'gate', 0, 2, 3),
+    ('scalar', 'gate', 0, 3, 4),
     ('sync', 'gate', 1, 2, 4),
-    ('sync', 'scales', 'w1', 0, 2),
+    ('sync', 'scales', 'w3', 0, 2),
     ('sync', 'gate', 2, 0, 2),
+    ('sync', 'scales', 'w1', 0, 2),
+    ('sync', 'scales', 'w3', 2, 4),
     ('sync', 'scales', 'w1', 2, 4),
-    ('gpsimd', 'scales', 'w3', 0, 2),
-    ('gpsimd', 'scales', 'w3', 2, 4),
-    ('sync', 'words', 'w1', 0, 4),
-    ('gpsimd', 'scales', 'w2', 0, 2),
-    ('gpsimd', 'scales', 'w2', 2, 4),
+    ('sync', 'words', 'w1', 0, 1),
+    ('scalar', 'warm'),
+    ('sync', 'words', 'w3', 1, 2),
+    ('sync', 'words', 'w1', 2, 4),
+    ('sync', 'words', 'w1', 1, 2),
     ('sync', 'gate', 2, 2, 4),
-    ('sync', 'words', 'w3', 0, 4),
+    ('sync', 'words', 'w3', 0, 1),
+    ('sync', 'words', 'w3', 2, 4),
+    ('sync', 'scales', 'w2', 2, 4),
+    ('scalar', 'scales', 'w2', 0, 2),
+    ('sync', 'pos2'),
     ('sync', 'words', 'w2', 0, 4),
     ('sync', 'pos1'),
-    ('sync', 'pos2'),
 ]
-LEAD = {'gather': -3.566, 'first': 0.0, 'mult': 0.89, 'turn': 1.158, 'quant': 2.167, 'second': 3.44}
-A_BUFS, B_BUFS, T_BUFS = 3, 2, 2
-Y_PIECES = [256, 256, 256, 128, 128]
+LEAD = {'gather': -0.01, 'first': 0, 'mult': 2.026, 'turn': 2.325, 'quant': 13.643}
+A_BUFS, B_BUFS, T_BUFS = 2, 4, 2
+Y_PIECES = [512, 384, 128]
 ZERO_ON = 'gpsimd'
+SPLIT = 0
+TURNS = [2, 2, 2, 1, 1]
+QUANTS = [4, 2, 1, 1]
+PIECES = [(0, 0, 512), (1, 0, 512), (2, 0, 512), (3, 0, 256), (3, 256, 256)]
 ADD_ON = ["vector", "vector", "vector", "vector", "vector"]
-PIECES = [(0, 0, T), (1, 0, T), (2, 0, T), (3, 0, T // 2), (3, T // 2, T // 2)]
 
 
 def tile_moe_pre_glu_sigmoid_kernel(
@@ -99,6 +107,8 @@ def tile_moe_pre_glu_sigmoid_kernel(
             q = engines[queue]
             if kind in lists:
                 q.dma_start(lists[kind][0][:], lists[kind][1])
+            elif kind == "warm":
+                nc.scalar.activation(warm_out[:], warm[:], SIGMOID)
             elif kind == "x":
                 q.dma_start(x_plane[args[0]][:, 0:T], x_rows[args[0]])
             elif kind == "gate":
@@ -115,6 +125,7 @@ def tile_moe_pre_glu_sigmoid_kernel(
                     q.dma_start(scales[name][r:P:32, :, :].bitcast(I32), src[r].bitcast(I32))
 
         nc.vector.memset(warm[:], 0.0)
+        make_identity(nc, ident[:])
         for name in ("w1", "w3", "w2"):
             engines[ZERO_ON].memset(scales[name][:].rearrange("p e n -> p (e n)").bitcast(I32), 0)
         if pad:
@@ -122,27 +133,28 @@ def tile_moe_pre_glu_sigmoid_kernel(
                 nc.vector.memset(x_plane[t][:, T : T + pad], 0.0)
         for item in LOADS:
             load(*item)
-        nc.scalar.activation(warm_out[:], warm[:], SIGMOID)
-        make_identity(nc, ident[:])
 
         h_codes = keep.tile([P, S], U32, name="h_codes", align_bytes=64)
         h_scales = keep.tile([P, S], U8, name="h_scales", align_bytes=64)
         y = [keep.tile([P, S], F32, name=f"y{nt}") for nt in range(N // P)]
+        hb = keep.tile([P, S * PACK], BF16, name="hb", align_bytes=64)
         held = {}
         a_banks = [psum.tile([P, H], F32, name=f"a{j}") for j in range(A_BUFS)]
         b_banks = [psum.tile([P, H], F32, name=f"b{j}") for j in range(B_BUFS)]
         t_banks = [psum.tile([P, H], F32, name=f"t{j}") for j in range(T_BUFS)]
-        y_bank = psum.tile([P, H], F32, name="y_bank")
+        y_banks = [psum.tile([P, H], F32, name=f"y{j}_bank") for j in range(8 - A_BUFS - B_BUFS - T_BUFS)]
 
         def gather_x(g):
             s0, width = starts[g], GROUPS[g]
             for t in range(PACK):
-                nc.vector.tensor_tensor(
-                    xg[g][:, t, :],
-                    x_plane[t][:].indirect(lists["offs"][0][:, s0 // STRIPE : (s0 + width) // STRIPE]),
-                    gate_sb[g][:, t, :],
-                    MULT,
-                )
+                cuts = [0, SPLIT, width] if g == 0 and t == PACK - 1 and SPLIT else [0, width]
+                for lo, hi in zip(cuts, cuts[1:]):
+                    nc.vector.tensor_tensor(
+                        xg[g][:, t, lo:hi],
+                        x_plane[t][:].indirect(lists["offs"][0][:, (s0 + lo) // STRIPE : (s0 + hi) // STRIPE]),
+                        gate_sb[g][:, t, lo:hi],
+                        MULT,
+                    )
 
         def first_layer(c):
             s0 = c * CH
@@ -175,30 +187,30 @@ def tile_moe_pre_glu_sigmoid_kernel(
 
         def multiply(c):
             sig, b = held[c]
-            ht = work.tile([P, H], BF16, name="ht", align_bytes=64)
+            ht = work.tile([P, H], BF16, name="ht", align_bytes=64, bufs=8)
             nc.vector.tensor_tensor(ht[:], b[:], sig[:], MULT)
             held[c] = ht
 
-        def turn(c):
-            pairs = held[c][:].bitcast(F32)
-            turned = t_banks[c % T_BUFS][:, 0 : 2 * CH].rearrange("p (u c) -> p u c", u=2)
-            for u in range(2):
-                nc.tensor.transpose(turned[:, u, :], pairs[:, u : H // 2 : 2], ident[:])
-            hb = work.tile([P, CH * PACK], BF16, name="hb", align_bytes=64, bufs=8)
+        def turn(j, c0, count):
+            turned = t_banks[j % T_BUFS][:, 0 : 2 * CH * count].rearrange("p (c u s) -> p c u s", u=2, s=CH)
+            for c in range(count):
+                pairs = held[c0 + c][:].bitcast(F32)
+                for u in range(2):
+                    nc.tensor.transpose(turned[:, c, u, :], pairs[:, u : H // 2 : 2], ident[:])
+            rows = hb[:, c0 * CH * PACK : (c0 + count) * CH * PACK]
             nc.scalar.copy(
-                hb[:].bitcast(F32).rearrange("p (c u) -> p c u", u=2),
-                turned.rearrange("p u c -> p c u"),
+                rows.bitcast(F32).rearrange("p (c s u) -> p c s u", u=2, s=CH),
+                turned.rearrange("p c u s -> p c s u"),
             )
-            held[c] = hb
 
-        def quantize_h(c):
-            s0 = c * CH
-            nc.vector.quantize_mx(h_codes[:, s0 : s0 + CH].bitcast(FP8X4), h_scales[:, s0 : s0 + CH], held[c][:])
+        def quantize_h(c0, count):
+            lo, hi = c0 * CH, (c0 + count) * CH
+            nc.vector.quantize_mx(h_codes[:, lo:hi].bitcast(FP8X4), h_scales[:, lo:hi], hb[:, lo * PACK : hi * PACK])
 
         def second_layer(nt, s0, width, bank):
-            step = min(width, C)
-            for lo in range(s0, s0 + width, step):
-                e = lo // C
+            cuts = sorted({s0, s0 + width} | {lo for lo in range(0, S, C) if s0 < lo < s0 + width})
+            for lo, hi in zip(cuts, cuts[1:]):
+                e, step = lo // C, hi - lo
                 nc.tensor.matmul_mx(
                     bank[:, lo - s0 : lo - s0 + step],
                     lhsT=words["w2"][:, e, 2 * P * nt : 2 * P * (nt + 1)].bitcast(FP4X4),
@@ -214,18 +226,25 @@ def tile_moe_pre_glu_sigmoid_kernel(
         for c in range(S // CH):
             steps.append((c + LEAD["first"], first_layer, (c,)))
             steps.append((c + LEAD["mult"], multiply, (c,)))
-            steps.append((c + LEAD["turn"], turn, (c,)))
-            steps.append((c + LEAD["quant"], quantize_h, (c,)))
-        s0 = 0
-        for width in Y_PIECES:
-            steps.append(((s0 + width) // CH - 1 + LEAD["second"], second_layer, (0, s0, width, y_bank if s0 + width < S else a_banks[(S // CH - 2) % A_BUFS])))
-            s0 += width
+        c0 = 0
+        for j, count in enumerate(TURNS):
+            steps.append((c0 + count - 1 + LEAD["turn"], turn, (j, c0, count)))
+            c0 += count
+        c0 = 0
+        for count in QUANTS:
+            steps.append((c0 + count - 1 + LEAD["quant"], quantize_h, (c0, count)))
+            c0 += count
         for step in sorted(steps, key=lambda item: item[0]):
             step[1](*step[2])
 
         last = S // CH - 1
-        early = [b_banks[last % B_BUFS], t_banks[last % T_BUFS], y_bank]
-        late = [a_banks[last % A_BUFS], b_banks[(last - 1) % B_BUFS], b_banks[(last - 2) % B_BUFS]]
+        spare = y_banks + [a_banks[(last - j) % A_BUFS] for j in reversed(range(A_BUFS))]
+        s0 = 0
+        for j, width in enumerate(Y_PIECES):
+            second_layer(0, s0, width, spare[j % len(spare)])
+            s0 += width
+        early = [b_banks[last % B_BUFS], t_banks[(len(TURNS) - 1) % T_BUFS], spare[(len(Y_PIECES) - 1) % len(spare)]]
+        late = [b_banks[(last - 1) % B_BUFS], t_banks[(len(TURNS) - 2) % T_BUFS], spare[(len(Y_PIECES) - 2) % len(spare)]]
         for nt in range(1, N // P):
             second_layer(nt, 0, 2 * C, early[nt - 1])
             second_layer(nt, 2 * C, 2 * C, late[nt - 1])

@@ -30,43 +30,45 @@ GROUPS = [512, 256, 256]
 LOADS = [
     ('sync', 'offs'),
     ('sync', 'x', 0),
-    ('sync', 'x', 1),
     ('scalar', 'gate', 0, 0, 1),
-    ('sync', 'x', 2),
-    ('sync', 'x', 3),
+    ('sync', 'x', 1),
     ('scalar', 'gate', 0, 1, 2),
-    ('sync', 'gate', 1, 0, 2),
+    ('sync', 'x', 2),
     ('scalar', 'gate', 0, 2, 3),
+    ('sync', 'x', 3),
     ('scalar', 'gate', 0, 3, 4),
-    ('sync', 'gate', 1, 2, 4),
-    ('sync', 'scales', 'w3', 0, 2),
-    ('sync', 'gate', 2, 0, 2),
-    ('sync', 'scales', 'w1', 0, 2),
-    ('sync', 'scales', 'w3', 2, 4),
-    ('sync', 'scales', 'w1', 2, 4),
-    ('sync', 'words', 'w1', 0, 1),
     ('scalar', 'warm'),
-    ('sync', 'words', 'w3', 1, 2),
+    ('sync', 'gate', 1, 0, 4),
+    ('sync', 'gate', 2, 0, 4),
+    ('sync', 'scales', 'w3', 0, 2),
+    ('sync', 'scales', 'w3', 2, 4),
+    ('sync', 'words', 'w3', 0, 2),
+    ('sync', 'scales', 'w1', 0, 2),
+    ('sync', 'scales', 'w1', 2, 4),
+    ('sync', 'words', 'w1', 0, 2),
     ('sync', 'words', 'w1', 2, 4),
-    ('sync', 'words', 'w1', 1, 2),
-    ('sync', 'gate', 2, 2, 4),
-    ('sync', 'words', 'w3', 0, 1),
     ('sync', 'words', 'w3', 2, 4),
-    ('sync', 'scales', 'w2', 2, 4),
-    ('scalar', 'scales', 'w2', 0, 2),
-    ('sync', 'pos2'),
+    ('gpsimd', 'scales', 'w2', 0, 2),
+    ('gpsimd', 'scales', 'w2', 2, 4),
     ('sync', 'words', 'w2', 0, 4),
     ('sync', 'pos1'),
+    ('sync', 'pos2'),
 ]
-LEAD = {'gather': -0.01, 'first': 0, 'mult': 2.026, 'turn': 2.325, 'quant': 13.643}
-A_BUFS, B_BUFS, T_BUFS = 2, 4, 2
-Y_PIECES = [512, 384, 128]
-ZERO_ON = 'gpsimd'
+LEAD = {'gather': -20.5, 'inter': -20, 'quantx': -18, 'sig': -0.1, 'first': 0, 'mult': 0.5, 'turn': 2.5, 'quant': 4.5}
+A_BUFS, B_BUFS, T_BUFS = 3, 3, 2
+Y_PIECES = [256, 256, 256, 128, 128]
+ZERO_ON = {"w1": "vector", "w3": "vector", "w2": "gpsimd"}
+LATE = 6
+QLATE = 6
+CHAIN = 1
+ALIAS = 1
 SPLIT = 0
 TURNS = [2, 2, 2, 1, 1]
-QUANTS = [4, 2, 1, 1]
+QUANTS = [2, 2, 2, 1, 1]
+TURN_ON = ["vector", "scalar", "scalar", "scalar", "scalar"]
+Y_ON = ["scalar"] * 5
 PIECES = [(0, 0, 512), (1, 0, 512), (2, 0, 512), (3, 0, 256), (3, 256, 256)]
-ADD_ON = ["vector", "vector", "vector", "vector", "vector"]
+ADD_ON = ["gpsimd", "gpsimd", "gpsimd", "vector", "vector"]
 
 
 def tile_moe_pre_glu_sigmoid_kernel(
@@ -87,7 +89,7 @@ def tile_moe_pre_glu_sigmoid_kernel(
             "pos2": (keep.tile([P, T // STRIPE], U16, name="pos2_sb"), pos2),
         }
         x_plane = [keep.tile([P, T + pad], F32, name=f"x_plane{t}") for t in range(PACK)]
-        gate_sb = [keep.tile([P, PACK, w], F32, name=f"gate{g}") for g, w in enumerate(GROUPS)]
+        gate_sb = [keep.tile([P, PACK, w], F32, name=f"gate{g}", align_bytes=64) for g, w in enumerate(GROUPS)]
         xg = [keep.tile([P, PACK, w], F32, name=f"xg{g}") for g, w in enumerate(GROUPS)]
         words = {}
         scales = {}
@@ -119,15 +121,15 @@ def tile_moe_pre_glu_sigmoid_kernel(
                 src = src_words[name].rearrange("e s p b -> p (e s) b")
                 q.dma_start(words[name][:, e0:e1, :].bitcast(I32), src[:, e0:e1, :].bitcast(I32))
             else:
-                name, r0, r1 = args
-                src = src_scales[name].rearrange("e s (q r) n -> r q (e s) n", r=4)
-                for r in range(r0, r1):
-                    q.dma_start(scales[name][r:P:32, :, :].bitcast(I32), src[r].bitcast(I32))
+                name, r0 = args[0], args[1]
+                src = src_scales[name].rearrange("e s (q r) n -> q r (e s) n", r=4)
+                for quad in (r0 // 2, r0 // 2 + 2):
+                    q.dma_start(scales[name][32 * quad : 32 * quad + 4, :, :].bitcast(I32), src[quad].bitcast(I32))
 
         nc.vector.memset(warm[:], 0.0)
         make_identity(nc, ident[:])
         for name in ("w1", "w3", "w2"):
-            engines[ZERO_ON].memset(scales[name][:].rearrange("p e n -> p (e n)").bitcast(I32), 0)
+            engines[ZERO_ON[name]].memset(scales[name][:].rearrange("p e n -> p (e n)").bitcast(I32), 0)
         if pad:
             for t in range(PACK):
                 nc.vector.memset(x_plane[t][:, T : T + pad], 0.0)
@@ -138,11 +140,21 @@ def tile_moe_pre_glu_sigmoid_kernel(
         h_scales = keep.tile([P, S], U8, name="h_scales", align_bytes=64)
         y = [keep.tile([P, S], F32, name=f"y{nt}") for nt in range(N // P)]
         hb = keep.tile([P, S * PACK], BF16, name="hb", align_bytes=64)
+        sigs = [keep.tile([P, H], F32, name=f"sig{c}", align_bytes=64) for c in range(S // CH)]
         held = {}
         a_banks = [psum.tile([P, H], F32, name=f"a{j}") for j in range(A_BUFS)]
         b_banks = [psum.tile([P, H], F32, name=f"b{j}") for j in range(B_BUFS)]
         t_banks = [psum.tile([P, H], F32, name=f"t{j}") for j in range(T_BUFS)]
         y_banks = [psum.tile([P, H], F32, name=f"y{j}_bank") for j in range(8 - A_BUFS - B_BUFS - T_BUFS)]
+
+        def split_pairs(bank):
+            return bank[:].rearrange("s (q u e) -> s u q e", u=2, e=2)
+
+        def by_pair(tile):
+            return tile[:].rearrange("s (u q e) -> s u q e", u=2, e=2)
+
+        def move(engine):
+            return nc.scalar.copy if engine == "scalar" else nc.vector.tensor_copy
 
         def gather_x(g):
             s0, width = starts[g], GROUPS[g]
@@ -156,39 +168,54 @@ def tile_moe_pre_glu_sigmoid_kernel(
                         MULT,
                     )
 
-        def first_layer(c):
+        def interleave(c):
             s0 = c * CH
-            e = s0 // C
             g = max(j for j in range(len(GROUPS)) if starts[j] <= s0)
             c0 = s0 - starts[g]
-            xb = work.tile([P, CH, PACK], BF16, name="xb", align_bytes=64)
+            if c >= LATE:
+                half = c - LATE
+                xb = sigs[ALIAS][:, half * H // 2 : (half + 1) * H // 2].bitcast(BF16).rearrange("p (c t) -> p c t", t=PACK)
+            else:
+                xb = work.tile([P, CH, PACK], BF16, name="xb", align_bytes=64, bufs=8)
             nc.scalar.copy(
                 xb[:].rearrange("p (c i) t -> p c t i", i=4),
                 xg[g][:, :, c0 : c0 + CH].rearrange("p t (c i) -> p c t i", i=4),
             )
+            held["xb", c] = xb
+
+        def quantize_x(c):
             x_codes = work.tile([P, CH], U32, name="x_codes", align_bytes=64, bufs=8)
             x_scales = work.tile([P, CH], U8, name="x_scales", align_bytes=64, bufs=8)
-            nc.vector.quantize_mx(x_codes[:].bitcast(FP8X4), x_scales[:], xb[:].rearrange("p c t -> p (c t)"))
+            nc.vector.quantize_mx(x_codes[:].bitcast(FP8X4), x_scales[:], held["xb", c][:].rearrange("p c t -> p (c t)"))
+            held["xq", c] = (x_codes, x_scales)
+
+        def first_layer(c, acc, name):
+            x_codes, x_scales = held["xq", c]
+            e = c * CH // C
+            nc.tensor.matmul_mx(
+                acc[:],
+                lhsT=x_codes[:].bitcast(FP8X4),
+                lhsT_scale=x_scales[:],
+                rhs=words[name][:, e, :].bitcast(FP4X4),
+                rhs_scale=scales[name][:, e, :],
+                start=True,
+                stop=True,
+            )
+
+        def gate_side(c):
             a = a_banks[c % A_BUFS]
-            b = b_banks[c % B_BUFS]
-            for acc, name in ((a, "w1"), (b, "w3")):
-                nc.tensor.matmul_mx(
-                    acc[:],
-                    lhsT=x_codes[:].bitcast(FP8X4),
-                    lhsT_scale=x_scales[:],
-                    rhs=words[name][:, e, :].bitcast(FP4X4),
-                    rhs_scale=scales[name][:, e, :],
-                    start=True,
-                    stop=True,
-                )
-            sig = work.tile([P, H], F32, name="sig", bufs=8)
-            nc.scalar.activation(sig[:], a[:], SIGMOID)
-            held[c] = (sig, b)
+            first_layer(c, a, "w1")
+            sig = sigs[c]
+            nc.scalar.activation(by_pair(sig), split_pairs(a), SIGMOID)
+            held["sig", c] = sig
+
+        def linear_side(c):
+            first_layer(c, b_banks[c % B_BUFS], "w3")
 
         def multiply(c):
-            sig, b = held[c]
-            ht = work.tile([P, H], BF16, name="ht", align_bytes=64, bufs=8)
-            nc.vector.tensor_tensor(ht[:], b[:], sig[:], MULT)
+            sig, b = held["sig", c], b_banks[c % B_BUFS]
+            ht = gate_sb[-1][:, PACK - 1 - c % PACK, :].bitcast(BF16)
+            nc.vector.tensor_tensor(by_pair(ht), split_pairs(b), by_pair(sig), MULT)
             held[c] = ht
 
         def turn(j, c0, count):
@@ -196,9 +223,9 @@ def tile_moe_pre_glu_sigmoid_kernel(
             for c in range(count):
                 pairs = held[c0 + c][:].bitcast(F32)
                 for u in range(2):
-                    nc.tensor.transpose(turned[:, c, u, :], pairs[:, u : H // 2 : 2], ident[:])
+                    nc.tensor.transpose(turned[:, c, u, :], pairs[:, u * P : (u + 1) * P], ident[:])
             rows = hb[:, c0 * CH * PACK : (c0 + count) * CH * PACK]
-            nc.scalar.copy(
+            move(TURN_ON[j])(
                 rows.bitcast(F32).rearrange("p (c s u) -> p c s u", u=2, s=CH),
                 turned.rearrange("p c u s -> p c s u"),
             )
@@ -207,7 +234,7 @@ def tile_moe_pre_glu_sigmoid_kernel(
             lo, hi = c0 * CH, (c0 + count) * CH
             nc.vector.quantize_mx(h_codes[:, lo:hi].bitcast(FP8X4), h_scales[:, lo:hi], hb[:, lo * PACK : hi * PACK])
 
-        def second_layer(nt, s0, width, bank):
+        def second_layer(nt, s0, width, bank, engine="scalar"):
             cuts = sorted({s0, s0 + width} | {lo for lo in range(0, S, C) if s0 < lo < s0 + width})
             for lo, hi in zip(cuts, cuts[1:]):
                 e, step = lo // C, hi - lo
@@ -220,11 +247,15 @@ def tile_moe_pre_glu_sigmoid_kernel(
                     start=True,
                     stop=True,
                 )
-            nc.scalar.copy(y[nt][:, s0 : s0 + width], bank[:, 0:width])
+            move(engine)(y[nt][:, s0 : s0 + width], bank[:, 0:width])
 
         steps = [(starts[g] // CH + LEAD["gather"], gather_x, (g,)) for g in range(len(GROUPS))]
         for c in range(S // CH):
-            steps.append((c + LEAD["first"], first_layer, (c,)))
+            late = c >= LATE
+            steps.append((ALIAS + LEAD["mult"] + 0.001 * (c - LATE + 1) if late else c + LEAD["inter"], interleave, (c,)))
+            steps.append((ALIAS + LEAD["mult"] + 0.003 + 0.001 * c if c >= QLATE else c + LEAD["quantx"], quantize_x, (c,)))
+            steps.append((ALIAS + LEAD["mult"] + 0.02 + 0.001 * c if late and LEAD["sig"] < -5 else c + LEAD["sig"], gate_side, (c,)))
+            steps.append((c + LEAD["first"], linear_side, (c,)))
             steps.append((c + LEAD["mult"], multiply, (c,)))
         c0 = 0
         for j, count in enumerate(TURNS):
@@ -239,15 +270,17 @@ def tile_moe_pre_glu_sigmoid_kernel(
 
         last = S // CH - 1
         spare = y_banks + [a_banks[(last - j) % A_BUFS] for j in reversed(range(A_BUFS))]
+        banks = [spare[j % len(spare)] for j in range(len(Y_PIECES) - 2)]
+        banks += [b_banks[(last - 1) % B_BUFS], b_banks[last % B_BUFS]]
         s0 = 0
-        for j, width in enumerate(Y_PIECES):
-            second_layer(0, s0, width, spare[j % len(spare)])
+        for width, bank, engine in zip(Y_PIECES, banks, Y_ON):
+            second_layer(0, s0, width, bank, engine)
             s0 += width
-        early = [b_banks[last % B_BUFS], t_banks[(len(TURNS) - 1) % T_BUFS], spare[(len(Y_PIECES) - 1) % len(spare)]]
-        late = [b_banks[(last - 1) % B_BUFS], t_banks[(len(TURNS) - 2) % T_BUFS], spare[(len(Y_PIECES) - 2) % len(spare)]]
+        upper = [t_banks[(len(TURNS) - 2) % T_BUFS], t_banks[(len(TURNS) - 1) % T_BUFS], b_banks[(last - 1) % B_BUFS]]
+        lower = [banks[-1], upper[0], upper[1]]
         for nt in range(1, N // P):
-            second_layer(nt, 0, 2 * C, early[nt - 1])
-            second_layer(nt, 2 * C, 2 * C, late[nt - 1])
+            second_layer(nt, 2 * C, 2 * C, banks[-2] if CHAIN else upper[nt - 1])
+            second_layer(nt, 0, 2 * C, banks[-1] if CHAIN else lower[nt - 1])
 
         def fetch(nt, t0, width):
             got = []

@@ -21,284 +21,238 @@ SIGMOID = mybir.ActivationFunctionType.Sigmoid
 
 P = 128
 PACK = 4
-CH = 128
+QUAD = 32
 STRIPE = 16
+MX_ALIGN = 64
+CHUNK = 128
+CHUNKS = S // CHUNK
+BANK = 512
 
-
-PAD = 16
-GROUPS = [512, 256, 256]
-LOADS = [
-    ('sync', 'offs'),
-    ('sync', 'x', 0),
-    ('scalar', 'gate', 0, 0, 1),
-    ('sync', 'x', 1),
-    ('scalar', 'gate', 0, 1, 2),
-    ('sync', 'x', 2),
-    ('scalar', 'gate', 0, 2, 3),
-    ('sync', 'x', 3),
-    ('scalar', 'gate', 0, 3, 4),
-    ('scalar', 'warm'),
-    ('sync', 'gate', 1, 0, 4),
-    ('sync', 'gate', 2, 0, 4),
-    ('sync', 'scales', 'w3', 0, 2),
-    ('sync', 'scales', 'w3', 2, 4),
-    ('sync', 'words', 'w3', 0, 2),
-    ('sync', 'scales', 'w1', 0, 2),
-    ('sync', 'scales', 'w1', 2, 4),
-    ('sync', 'words', 'w1', 0, 2),
-    ('sync', 'words', 'w1', 2, 4),
-    ('sync', 'words', 'w3', 2, 4),
-    ('gpsimd', 'scales', 'w2', 0, 2),
-    ('gpsimd', 'scales', 'w2', 2, 4),
-    ('sync', 'words', 'w2', 0, 4),
-    ('sync', 'pos1'),
-    ('sync', 'pos2'),
-]
-LEAD = {'gather': -20.5, 'inter': -20, 'quantx': -18, 'sig': -0.1, 'first': 0, 'mult': 0.5, 'turn': 2.5, 'quant': 4.5}
-A_BUFS, B_BUFS, T_BUFS = 3, 3, 2
-Y_PIECES = [256, 256, 256, 128, 128]
-ZERO_ON = {"w1": "vector", "w3": "vector", "w2": "gpsimd"}
-LATE = 6
-QLATE = 6
-CHAIN = 1
-ALIAS = 1
-SPLIT = 0
-TURNS = [2, 2, 2, 1, 1]
-QUANTS = [2, 2, 2, 1, 1]
-TURN_ON = ["vector", "scalar", "scalar", "scalar", "scalar"]
-Y_ON = ["scalar"] * 5
-PIECES = [(0, 0, 512), (1, 0, 512), (2, 0, 512), (3, 0, 256), (3, 256, 256)]
-ADD_ON = ["gpsimd", "gpsimd", "gpsimd", "vector", "vector"]
+GROUPS = (512, 256, 256)
+X_TAIL = 16
+LAYER1_BANKS, TURN_BANKS = 3, 2
+H_RUNS = ((0, 2), (2, 2), (4, 2), (6, 1), (7, 1))
+RESULT_PIECES = ((0, 0, T), (1, 0, T), (2, 0, T), (3, 0, T // 2), (3, T // 2, T // 2))
 
 
 def tile_moe_pre_glu_sigmoid_kernel(
     tc, xT, w1_words, w1_scales, w3_words, w3_scales, w2_words, w2_scales, gate, offs, pos1, pos2, out
 ):
     nc = tc.nc
-    engines = {"sync": nc.sync, "scalar": nc.scalar, "gpsimd": nc.gpsimd, "vector": nc.vector}
-    starts = [sum(GROUPS[:g]) for g in range(len(GROUPS))]
-    pad = PAD if max(GROUPS) >= T else 0
+    group_start = [sum(GROUPS[:g]) for g in range(len(GROUPS))]
+    weights = {"w1": (w1_words, w1_scales), "w3": (w3_words, w3_scales), "w2": (w2_words, w2_scales)}
+
     with ExitStack() as ctx:
         keep = ctx.enter_context(tc.tile_pool(name="keep", bufs=1))
-        work = ctx.enter_context(tc.tile_pool(name="work", bufs=4))
+        work = ctx.enter_context(tc.tile_pool(name="work", bufs=CHUNKS))
         psum = ctx.enter_context(tc.psum_pool(name="psum", bufs=1))
 
-        lists = {
-            "offs": (keep.tile([P, S // STRIPE], U16, name="offs_sb"), offs),
-            "pos1": (keep.tile([P, T // STRIPE], U16, name="pos1_sb"), pos1),
-            "pos2": (keep.tile([P, T // STRIPE], U16, name="pos2_sb"), pos2),
-        }
-        x_plane = [keep.tile([P, T + pad], F32, name=f"x_plane{t}") for t in range(PACK)]
-        gate_sb = [keep.tile([P, PACK, w], F32, name=f"gate{g}", align_bytes=64) for g, w in enumerate(GROUPS)]
-        xg = [keep.tile([P, PACK, w], F32, name=f"xg{g}") for g, w in enumerate(GROUPS)]
-        words = {}
-        scales = {}
-        for name in ("w1", "w3", "w2"):
-            words[name] = keep.tile([P, E, 2 * H], U8, name=f"{name}_words_sb", align_bytes=64)
-            scales[name] = keep.tile([P, E, H], U8, name=f"{name}_scales_sb", align_bytes=64)
-        src_words = {"w1": w1_words, "w3": w3_words, "w2": w2_words}
-        src_scales = {"w1": w1_scales, "w3": w3_scales, "w2": w2_scales}
-        ident = keep.tile([P, P], F32, name="ident")
-        warm = keep.tile([P, 8], F32, name="warm")
+        offs_sb = keep.tile([P, S // STRIPE], U16, name="offs_sb")
+        pos1_sb = keep.tile([P, T // STRIPE], U16, name="pos1_sb")
+        pos2_sb = keep.tile([P, T // STRIPE], U16, name="pos2_sb")
+        x_phase = [keep.tile([P, T + X_TAIL], F32, name=f"x_phase{t}") for t in range(PACK)]
+        gate_sb = [keep.tile([P, PACK, w], F32, name=f"gate{g}", align_bytes=MX_ALIGN) for g, w in enumerate(GROUPS)]
+        x_gated = [keep.tile([P, PACK, w], F32, name=f"x_gated{g}") for g, w in enumerate(GROUPS)]
+        w_codes = {m: keep.tile([P, E, 2 * H], U8, name=f"{m}_codes", align_bytes=MX_ALIGN) for m in weights}
+        w_scales = {m: keep.tile([P, E, H], U8, name=f"{m}_scale_bytes", align_bytes=MX_ALIGN) for m in weights}
+        identity = keep.tile([P, P], F32, name="identity")
+        sig = [keep.tile([P, H], F32, name=f"sig{c}", align_bytes=MX_ALIGN) for c in range(CHUNKS)]
+        h_turned = keep.tile([P, S * PACK], BF16, name="h_turned", align_bytes=MX_ALIGN)
+        h_codes = keep.tile([P, S], U32, name="h_codes", align_bytes=MX_ALIGN)
+        h_scales = keep.tile([P, S], U8, name="h_scales", align_bytes=MX_ALIGN)
+        y = [keep.tile([P, S], F32, name=f"y{nt}") for nt in range(N // P)]
+        a_bank = [psum.tile([P, BANK], F32, name=f"a_bank{j}") for j in range(LAYER1_BANKS)]
+        b_bank = [psum.tile([P, BANK], F32, name=f"b_bank{j}") for j in range(LAYER1_BANKS)]
+        turn_bank = [psum.tile([P, BANK], F32, name=f"turn_bank{j}") for j in range(TURN_BANKS)]
+
+        warm_in = keep.tile([P, 8], F32, name="warm_in")
         warm_out = keep.tile([P, 8], F32, name="warm_out")
+        nc.vector.memset(warm_in[:], 0.0)
+        make_identity(nc, identity[:])
+        for m in weights:
+            nc.vector.memset(w_scales[m][:].rearrange("p e n -> p (e n)").bitcast(I32), 0)
+        for t in range(PACK):
+            nc.vector.memset(x_phase[t][:, T : T + X_TAIL], 0.0)
 
         x_rows = xT.rearrange("(p t) n -> t p n", t=PACK)
         gate_rows = gate.rearrange("(p t) s -> p t s", t=PACK)
 
-        def load(queue, kind, *args):
-            q = engines[queue]
-            if kind in lists:
-                q.dma_start(lists[kind][0][:], lists[kind][1])
-            elif kind == "warm":
-                nc.scalar.activation(warm_out[:], warm[:], SIGMOID)
-            elif kind == "x":
-                q.dma_start(x_plane[args[0]][:, 0:T], x_rows[args[0]])
-            elif kind == "gate":
-                g, t0, t1 = args
-                q.dma_start(gate_sb[g][:, t0:t1, :], gate_rows[:, t0:t1, starts[g] : starts[g] + GROUPS[g]])
-            elif kind == "words":
-                name, e0, e1 = args
-                src = src_words[name].rearrange("e s p b -> p (e s) b")
-                q.dma_start(words[name][:, e0:e1, :].bitcast(I32), src[:, e0:e1, :].bitcast(I32))
-            else:
-                name, r0 = args[0], args[1]
-                src = src_scales[name].rearrange("e s (q r) n -> q r (e s) n", r=4)
-                for quad in (r0 // 2, r0 // 2 + 2):
-                    q.dma_start(scales[name][32 * quad : 32 * quad + 4, :, :].bitcast(I32), src[quad].bitcast(I32))
+        def load_gate(queue, g, t0, t1):
+            s0 = group_start[g]
+            queue.dma_start(gate_sb[g][:, t0:t1, :], gate_rows[:, t0:t1, s0 : s0 + GROUPS[g]])
 
-        nc.vector.memset(warm[:], 0.0)
-        make_identity(nc, ident[:])
-        for name in ("w1", "w3", "w2"):
-            engines[ZERO_ON[name]].memset(scales[name][:].rearrange("p e n -> p (e n)").bitcast(I32), 0)
-        if pad:
-            for t in range(PACK):
-                nc.vector.memset(x_plane[t][:, T : T + pad], 0.0)
-        for item in LOADS:
-            load(*item)
+        def load_codes(m, e0, e1):
+            src = weights[m][0].rearrange("e s p b -> p (e s) b")
+            nc.sync.dma_start(w_codes[m][:, e0:e1, :].bitcast(I32), src[:, e0:e1, :].bitcast(I32))
 
-        h_codes = keep.tile([P, S], U32, name="h_codes", align_bytes=64)
-        h_scales = keep.tile([P, S], U8, name="h_scales", align_bytes=64)
-        y = [keep.tile([P, S], F32, name=f"y{nt}") for nt in range(N // P)]
-        hb = keep.tile([P, S * PACK], BF16, name="hb", align_bytes=64)
-        sigs = [keep.tile([P, H], F32, name=f"sig{c}", align_bytes=64) for c in range(S // CH)]
-        held = {}
-        a_banks = [psum.tile([P, H], F32, name=f"a{j}") for j in range(A_BUFS)]
-        b_banks = [psum.tile([P, H], F32, name=f"b{j}") for j in range(B_BUFS)]
-        t_banks = [psum.tile([P, H], F32, name=f"t{j}") for j in range(T_BUFS)]
-        y_banks = [psum.tile([P, H], F32, name=f"y{j}_bank") for j in range(8 - A_BUFS - B_BUFS - T_BUFS)]
+        def load_scales(m):
+            src = weights[m][1].rearrange("e s (q r) n -> q r (e s) n", r=4)
+            for q in (0, 2, 1, 3):
+                nc.sync.dma_start(w_scales[m][QUAD * q : QUAD * q + 4, :, :].bitcast(I32), src[q].bitcast(I32))
 
-        def split_pairs(bank):
-            return bank[:].rearrange("s (q u e) -> s u q e", u=2, e=2)
+        nc.sync.dma_start(offs_sb[:], offs)
+        for t in range(PACK):
+            nc.sync.dma_start(x_phase[t][:, 0:T], x_rows[t])
+            load_gate(nc.scalar, 0, t, t + 1)
+        nc.scalar.activation(warm_out[:], warm_in[:], SIGMOID)
+        for g in range(1, len(GROUPS)):
+            load_gate(nc.sync, g, 0, PACK)
+        for m in ("w3", "w1"):
+            load_scales(m)
+            load_codes(m, 0, E // 2)
+        for m in ("w1", "w3"):
+            load_codes(m, E // 2, E)
+        load_scales("w2")
+        load_codes("w2", 0, E)
+        nc.sync.dma_start(pos1_sb[:], pos1)
+        nc.sync.dma_start(pos2_sb[:], pos2)
 
-        def by_pair(tile):
-            return tile[:].rearrange("s (u q e) -> s u q e", u=2, e=2)
-
-        def move(engine):
-            return nc.scalar.copy if engine == "scalar" else nc.vector.tensor_copy
+        x_rounded = {}
+        x_quant = {}
 
         def gather_x(g):
-            s0, width = starts[g], GROUPS[g]
+            entries = offs_sb[:, group_start[g] // STRIPE : (group_start[g] + GROUPS[g]) // STRIPE]
             for t in range(PACK):
-                cuts = [0, SPLIT, width] if g == 0 and t == PACK - 1 and SPLIT else [0, width]
-                for lo, hi in zip(cuts, cuts[1:]):
-                    nc.vector.tensor_tensor(
-                        xg[g][:, t, lo:hi],
-                        x_plane[t][:].indirect(lists["offs"][0][:, (s0 + lo) // STRIPE : (s0 + hi) // STRIPE]),
-                        gate_sb[g][:, t, lo:hi],
-                        MULT,
-                    )
+                nc.vector.tensor_tensor(x_gated[g][:, t, :], x_phase[t][:].indirect(entries), gate_sb[g][:, t, :], MULT)
 
-        def interleave(c):
-            s0 = c * CH
-            g = max(j for j in range(len(GROUPS)) if starts[j] <= s0)
-            c0 = s0 - starts[g]
-            if c >= LATE:
-                half = c - LATE
-                xb = sigs[ALIAS][:, half * H // 2 : (half + 1) * H // 2].bitcast(BF16).rearrange("p (c t) -> p c t", t=PACK)
-            else:
-                xb = work.tile([P, CH, PACK], BF16, name="xb", align_bytes=64, bufs=8)
+        def round_x(c, dst):
+            g = max(j for j in range(len(GROUPS)) if group_start[j] <= c * CHUNK)
+            s0 = c * CHUNK - group_start[g]
             nc.scalar.copy(
-                xb[:].rearrange("p (c i) t -> p c t i", i=4),
-                xg[g][:, :, c0 : c0 + CH].rearrange("p t (c i) -> p c t i", i=4),
+                dst.rearrange("p (s i t) -> p s t i", i=4, t=PACK),
+                x_gated[g][:, :, s0 : s0 + CHUNK].rearrange("p t (s i) -> p s t i", i=4),
             )
-            held["xb", c] = xb
+            x_rounded[c] = dst
+
+        def round_x_apart(c):
+            dst = work.tile([P, CHUNK * PACK], BF16, name="x_bf16", align_bytes=MX_ALIGN)
+            round_x(c, dst[:])
 
         def quantize_x(c):
-            x_codes = work.tile([P, CH], U32, name="x_codes", align_bytes=64, bufs=8)
-            x_scales = work.tile([P, CH], U8, name="x_scales", align_bytes=64, bufs=8)
-            nc.vector.quantize_mx(x_codes[:].bitcast(FP8X4), x_scales[:], held["xb", c][:].rearrange("p c t -> p (c t)"))
-            held["xq", c] = (x_codes, x_scales)
+            codes = work.tile([P, CHUNK], U32, name="x_codes", align_bytes=MX_ALIGN)
+            scales = work.tile([P, CHUNK], U8, name="x_scales", align_bytes=MX_ALIGN)
+            nc.vector.quantize_mx(codes[:].bitcast(FP8X4), scales[:], x_rounded[c])
+            x_quant[c] = (codes, scales)
 
-        def first_layer(c, acc, name):
-            x_codes, x_scales = held["xq", c]
-            e = c * CH // C
+        def h_rows(c):
+            return gate_sb[-1][:, PACK - 1 - c % PACK, :].bitcast(BF16)
+
+        def pairs_of_bank(bank):
+            return bank[:].rearrange("s (q u e) -> s u q e", u=2, e=2)
+
+        def in_pair_order(rows):
+            return rows.rearrange("s (u q e) -> s u q e", u=2, e=2)
+
+        def first_layer(c, m, bank):
+            codes, scales = x_quant[c]
+            e = c * CHUNK // C
             nc.tensor.matmul_mx(
-                acc[:],
-                lhsT=x_codes[:].bitcast(FP8X4),
-                lhsT_scale=x_scales[:],
-                rhs=words[name][:, e, :].bitcast(FP4X4),
-                rhs_scale=scales[name][:, e, :],
+                bank[:],
+                lhsT=codes[:].bitcast(FP8X4),
+                lhsT_scale=scales[:],
+                rhs=w_codes[m][:, e, :].bitcast(FP4X4),
+                rhs_scale=w_scales[m][:, e, :],
                 start=True,
                 stop=True,
             )
 
-        def gate_side(c):
-            a = a_banks[c % A_BUFS]
-            first_layer(c, a, "w1")
-            sig = sigs[c]
-            nc.scalar.activation(by_pair(sig), split_pairs(a), SIGMOID)
-            held["sig", c] = sig
+        def hidden(c):
+            a, b = a_bank[c % LAYER1_BANKS], b_bank[c % LAYER1_BANKS]
+            first_layer(c, "w1", a)
+            nc.scalar.activation(in_pair_order(sig[c][:]), pairs_of_bank(a), SIGMOID)
+            first_layer(c, "w3", b)
+            nc.vector.tensor_tensor(in_pair_order(h_rows(c)), pairs_of_bank(b), in_pair_order(sig[c][:]), MULT)
 
-        def linear_side(c):
-            first_layer(c, b_banks[c % B_BUFS], "w3")
-
-        def multiply(c):
-            sig, b = held["sig", c], b_banks[c % B_BUFS]
-            ht = gate_sb[-1][:, PACK - 1 - c % PACK, :].bitcast(BF16)
-            nc.vector.tensor_tensor(by_pair(ht), split_pairs(b), by_pair(sig), MULT)
-            held[c] = ht
-
-        def turn(j, c0, count):
-            turned = t_banks[j % T_BUFS][:, 0 : 2 * CH * count].rearrange("p (c u s) -> p c u s", u=2, s=CH)
+        def turn_h(run, copy):
+            c0, count = H_RUNS[run]
+            bank = turn_bank[run % TURN_BANKS][:, 0 : 2 * CHUNK * count].rearrange("q (c u s) -> q c u s", u=2, s=CHUNK)
             for c in range(count):
-                pairs = held[c0 + c][:].bitcast(F32)
+                words = h_rows(c0 + c).bitcast(F32)
                 for u in range(2):
-                    nc.tensor.transpose(turned[:, c, u, :], pairs[:, u * P : (u + 1) * P], ident[:])
-            rows = hb[:, c0 * CH * PACK : (c0 + count) * CH * PACK]
-            move(TURN_ON[j])(
-                rows.bitcast(F32).rearrange("p (c s u) -> p c s u", u=2, s=CH),
-                turned.rearrange("p c u s -> p c s u"),
-            )
+                    nc.tensor.transpose(bank[:, c, u, :], words[:, u * P : (u + 1) * P], identity[:])
+            dst = h_turned[:, c0 * CHUNK * PACK : (c0 + count) * CHUNK * PACK].bitcast(F32)
+            copy(dst.rearrange("q (c s u) -> q c s u", u=2, s=CHUNK), bank.rearrange("q c u s -> q c s u"))
 
-        def quantize_h(c0, count):
-            lo, hi = c0 * CH, (c0 + count) * CH
-            nc.vector.quantize_mx(h_codes[:, lo:hi].bitcast(FP8X4), h_scales[:, lo:hi], hb[:, lo * PACK : hi * PACK])
+        def quantize_h(run):
+            c0, count = H_RUNS[run]
+            lo, hi = c0 * CHUNK, (c0 + count) * CHUNK
+            nc.vector.quantize_mx(h_codes[:, lo:hi].bitcast(FP8X4), h_scales[:, lo:hi], h_turned[:, lo * PACK : hi * PACK])
 
-        def second_layer(nt, s0, width, bank, engine="scalar"):
-            cuts = sorted({s0, s0 + width} | {lo for lo in range(0, S, C) if s0 < lo < s0 + width})
-            for lo, hi in zip(cuts, cuts[1:]):
-                e, step = lo // C, hi - lo
+        gather_x(0)
+        for c in range(0, 4):
+            round_x_apart(c)
+        for c in range(0, 2):
+            quantize_x(c)
+        gather_x(1)
+        for c in range(4, 6):
+            round_x_apart(c)
+        for c in range(2, 4):
+            quantize_x(c)
+        gather_x(2)
+        for c in range(4, 6):
+            quantize_x(c)
+
+        hidden(0)
+        hidden(1)
+        for c in range(6, 8):
+            round_x(c, sig[1][:, (c - 6) * H // 2 : (c - 5) * H // 2].bitcast(BF16))
+        for c in range(6, 8):
+            quantize_x(c)
+        hidden(2)
+        hidden(3)
+        turn_h(0, nc.vector.tensor_copy)
+        hidden(4)
+        hidden(5)
+        turn_h(1, nc.scalar.copy)
+        quantize_h(0)
+        hidden(6)
+        hidden(7)
+        turn_h(2, nc.scalar.copy)
+        quantize_h(1)
+        turn_h(3, nc.scalar.copy)
+        turn_h(4, nc.scalar.copy)
+        for run in range(2, len(H_RUNS)):
+            quantize_h(run)
+
+        def second_layer(nt, s0, width, bank):
+            step = min(width, C)
+            for lo in range(s0, s0 + width, step):
+                e = lo // C
                 nc.tensor.matmul_mx(
                     bank[:, lo - s0 : lo - s0 + step],
-                    lhsT=words["w2"][:, e, 2 * P * nt : 2 * P * (nt + 1)].bitcast(FP4X4),
-                    lhsT_scale=scales["w2"][:, e, P * nt : P * (nt + 1)],
+                    lhsT=w_codes["w2"][:, e, 2 * P * nt : 2 * P * (nt + 1)].bitcast(FP4X4),
+                    lhsT_scale=w_scales["w2"][:, e, P * nt : P * (nt + 1)],
                     rhs=h_codes[:, lo : lo + step].bitcast(FP8X4),
                     rhs_scale=h_scales[:, lo : lo + step],
                     start=True,
                     stop=True,
                 )
-            move(engine)(y[nt][:, s0 : s0 + width], bank[:, 0:width])
+            nc.scalar.copy(y[nt][:, s0 : s0 + width], bank[:, 0:width])
 
-        steps = [(starts[g] // CH + LEAD["gather"], gather_x, (g,)) for g in range(len(GROUPS))]
-        for c in range(S // CH):
-            late = c >= LATE
-            steps.append((ALIAS + LEAD["mult"] + 0.001 * (c - LATE + 1) if late else c + LEAD["inter"], interleave, (c,)))
-            steps.append((ALIAS + LEAD["mult"] + 0.003 + 0.001 * c if c >= QLATE else c + LEAD["quantx"], quantize_x, (c,)))
-            steps.append((ALIAS + LEAD["mult"] + 0.02 + 0.001 * c if late and LEAD["sig"] < -5 else c + LEAD["sig"], gate_side, (c,)))
-            steps.append((c + LEAD["first"], linear_side, (c,)))
-            steps.append((c + LEAD["mult"], multiply, (c,)))
-        c0 = 0
-        for j, count in enumerate(TURNS):
-            steps.append((c0 + count - 1 + LEAD["turn"], turn, (j, c0, count)))
-            c0 += count
-        c0 = 0
-        for count in QUANTS:
-            steps.append((c0 + count - 1 + LEAD["quant"], quantize_h, (c0, count)))
-            c0 += count
-        for step in sorted(steps, key=lambda item: item[0]):
-            step[1](*step[2])
-
-        last = S // CH - 1
-        spare = y_banks + [a_banks[(last - j) % A_BUFS] for j in reversed(range(A_BUFS))]
-        banks = [spare[j % len(spare)] for j in range(len(Y_PIECES) - 2)]
-        banks += [b_banks[(last - 1) % B_BUFS], b_banks[last % B_BUFS]]
-        s0 = 0
-        for width, bank, engine in zip(Y_PIECES, banks, Y_ON):
-            second_layer(0, s0, width, bank, engine)
-            s0 += width
-        upper = [t_banks[(len(TURNS) - 2) % T_BUFS], t_banks[(len(TURNS) - 1) % T_BUFS], b_banks[(last - 1) % B_BUFS]]
-        lower = [banks[-1], upper[0], upper[1]]
+        first_tile_banks = [a_bank[c % LAYER1_BANKS] for c in range(CHUNKS - 3, CHUNKS)]
+        first_tile_banks += [b_bank[c % LAYER1_BANKS] for c in range(CHUNKS - 2, CHUNKS)]
+        for (c0, count), bank in zip(H_RUNS, first_tile_banks):
+            second_layer(0, c0 * CHUNK, count * CHUNK, bank)
         for nt in range(1, N // P):
-            second_layer(nt, 2 * C, 2 * C, banks[-2] if CHAIN else upper[nt - 1])
-            second_layer(nt, 0, 2 * C, banks[-1] if CHAIN else lower[nt - 1])
+            second_layer(nt, S // 2, S // 2, first_tile_banks[-2])
+            second_layer(nt, 0, S // 2, first_tile_banks[-1])
 
         def fetch(nt, t0, width):
-            got = []
-            for name in ("pos1", "pos2"):
-                g = work.tile([P, width], F32, name="got", tag=f"got{width}", bufs=6)
-                nc.vector.tensor_copy(g[:], y[nt][:].indirect(lists[name][0][:, t0 // STRIPE : (t0 + width) // STRIPE]))
-                got.append(g)
-            return got
+            both = []
+            for pos_sb in (pos1_sb, pos2_sb):
+                picked = work.tile([P, width], F32, name="picked", tag=f"picked{width}", bufs=6)
+                nc.vector.tensor_copy(picked[:], y[nt][:].indirect(pos_sb[:, t0 // STRIPE : (t0 + width) // STRIPE]))
+                both.append(picked)
+            return both
 
-        def combine(j, nt, t0, width, got):
-            res = work.tile([P, width], F32, name="res", tag=f"res{width}")
-            engines[ADD_ON[j]].tensor_tensor(res[:], got[0][:], got[1][:], ADD)
-            nc.sync.dma_start(out[nt * P : (nt + 1) * P, t0 : t0 + width], res[:])
+        def combine(nt, t0, width, both):
+            engine = nc.gpsimd if width == T else nc.vector
+            total = work.tile([P, width], F32, name="total", tag=f"total{width}", bufs=4)
+            engine.tensor_tensor(total[:], both[0][:], both[1][:], ADD)
+            nc.sync.dma_start(out[nt * P : (nt + 1) * P, t0 : t0 + width], total[:])
 
-        last = None
-        for j, piece in enumerate(PIECES):
-            got = fetch(*piece)
-            if last is not None:
-                combine(*last)
-            last = (j,) + piece + (got,)
-        combine(*last)
+        fetched = [fetch(*RESULT_PIECES[0])]
+        for before, piece in zip(RESULT_PIECES, RESULT_PIECES[1:]):
+            fetched.append(fetch(*piece))
+            combine(*before, fetched[-2])
+        combine(*RESULT_PIECES[-1], fetched[-1])

@@ -28,11 +28,11 @@ CHUNK = 128
 CHUNKS = S // CHUNK
 BANK = 512
 
-GROUPS = (512, 256, 256)
-X_TAIL = 16
-LAYER1_BANKS, TURN_BANKS = 3, 2
+GROUPS = (384, 384, 256)
+PLANES = ((1920, 384), (1152, 512), (640, 256))
+STAGE_WIDTH = 3456
 H_RUNS = ((0, 2), (2, 2), (4, 2), (6, 1), (7, 1))
-RESULT_PIECES = ((0, 0, T), (1, 0, T), (2, 0, T), (3, 0, T // 2), (3, T // 2, T // 2))
+LAST_PIECES = (384, 128)
 
 
 def tile_moe_pre_glu_sigmoid_kernel(
@@ -44,26 +44,49 @@ def tile_moe_pre_glu_sigmoid_kernel(
 
     with ExitStack() as ctx:
         keep = ctx.enter_context(tc.tile_pool(name="keep", bufs=1))
-        work = ctx.enter_context(tc.tile_pool(name="work", bufs=CHUNKS))
         psum = ctx.enter_context(tc.psum_pool(name="psum", bufs=1))
+
+        def tile(name, width, dtype):
+            return keep.tile([P, width], dtype, name=name, align_bytes=MX_ALIGN)
 
         offs_sb = keep.tile([P, S // STRIPE], U16, name="offs_sb")
         pos1_sb = keep.tile([P, T // STRIPE], U16, name="pos1_sb")
         pos2_sb = keep.tile([P, T // STRIPE], U16, name="pos2_sb")
-        x_phase = [keep.tile([P, T + X_TAIL], F32, name=f"x_phase{t}") for t in range(PACK)]
-        gate_sb = [keep.tile([P, PACK, w], F32, name=f"gate{g}", align_bytes=MX_ALIGN) for g, w in enumerate(GROUPS)]
-        x_gated = [keep.tile([P, PACK, w], F32, name=f"x_gated{g}") for g, w in enumerate(GROUPS)]
+        x_phase = [tile(f"x_phase{t}", T, F32) for t in range(PACK)]
+        gate_first = tile("gate_first", GROUPS[0], F32)
+        gate_rest = tile("gate_rest", S - GROUPS[0], F32)
+        stage = tile("stage", STAGE_WIDTH, F32)
         w_codes = {m: keep.tile([P, E, 2 * H], U8, name=f"{m}_codes", align_bytes=MX_ALIGN) for m in weights}
         w_scales = {m: keep.tile([P, E, H], U8, name=f"{m}_scale_bytes", align_bytes=MX_ALIGN) for m in weights}
-        identity = keep.tile([P, P], F32, name="identity")
-        sig = [keep.tile([P, H], F32, name=f"sig{c}", align_bytes=MX_ALIGN) for c in range(CHUNKS)]
-        h_turned = keep.tile([P, S * PACK], BF16, name="h_turned", align_bytes=MX_ALIGN)
-        h_codes = keep.tile([P, S], U32, name="h_codes", align_bytes=MX_ALIGN)
-        h_scales = keep.tile([P, S], U8, name="h_scales", align_bytes=MX_ALIGN)
-        y = [keep.tile([P, S], F32, name=f"y{nt}") for nt in range(N // P)]
-        a_bank = [psum.tile([P, BANK], F32, name=f"a_bank{j}") for j in range(LAYER1_BANKS)]
-        b_bank = [psum.tile([P, BANK], F32, name=f"b_bank{j}") for j in range(LAYER1_BANKS)]
-        turn_bank = [psum.tile([P, BANK], F32, name=f"turn_bank{j}") for j in range(TURN_BANKS)]
+        identity = tile("identity", P, F32)
+        x_codes = [tile(f"x_codes{c}", CHUNK, U32) for c in range(CHUNKS)]
+        x_scales = [tile(f"x_scales{c}", CHUNK, U8) for c in range(CHUNKS)]
+        h_turned = tile("h_turned", S * PACK, BF16)
+        h_codes = tile("h_codes", S, U32)
+        h_scales = tile("h_scales", S, U8)
+        y = [tile(f"y{nt}", S, F32) for nt in range(N // P)]
+        banks = [psum.tile([P, BANK], F32, name=f"bank{j}") for j in range(8)]
+        a_bank = [banks[j] for j in (0, 1, 2, 4, 1, 2, 4, 1)]
+        b_bank = [banks[j] for j in (3, 0, 3, 0, 5, 3, 0, 5)]
+        run_bank = [banks[j] for j in (6, 7, 6, 2, 4)]
+
+        def gate_of(g):
+            s0 = group_start[g] - GROUPS[0]
+            return gate_first[:] if g == 0 else gate_rest[:, s0 : s0 + GROUPS[g]]
+
+        def plane(g, t, lo, hi):
+            first, step = PLANES[g]
+            return stage[:, first + t * step + lo : first + t * step + hi]
+
+        x_bf16 = {c: tile(f"x_bf16_{c}", CHUNK * PACK, BF16)[:] for c in (0, 1, 2, 6, 7)}
+        x_bf16[3] = plane(2, 0, -H // 2, 0).bitcast(BF16)
+        sig = {c: tile(f"sig{c}", H, F32)[:] for c in range(1, CHUNKS)}
+        sig[0] = plane(2, 0, -CHUNK, H - CHUNK)
+        for c in (4, 5):
+            x_bf16[c] = sig[1][:, (c - 4) * H // 2 : (c - 3) * H // 2].bitcast(BF16)
+        h_rows = {c: tile(f"h_rows{c}", H // 2, F32)[:] for c in (0, 1, 4, 5, 6, 7)}
+        h_rows[2] = plane(1, 1, CHUNK, 3 * CHUNK)
+        h_rows[3] = plane(1, 3, CHUNK, 3 * CHUNK)
 
         warm_in = keep.tile([P, 8], F32, name="warm_in")
         warm_out = keep.tile([P, 8], F32, name="warm_out")
@@ -71,15 +94,8 @@ def tile_moe_pre_glu_sigmoid_kernel(
         make_identity(nc, identity[:])
         for m in weights:
             nc.vector.memset(w_scales[m][:].rearrange("p e n -> p (e n)").bitcast(I32), 0)
-        for t in range(PACK):
-            nc.vector.memset(x_phase[t][:, T : T + X_TAIL], 0.0)
 
         x_rows = xT.rearrange("(p t) n -> t p n", t=PACK)
-        gate_rows = gate.rearrange("(p t) s -> p t s", t=PACK)
-
-        def load_gate(queue, g, t0, t1):
-            s0 = group_start[g]
-            queue.dma_start(gate_sb[g][:, t0:t1, :], gate_rows[:, t0:t1, s0 : s0 + GROUPS[g]])
 
         def load_codes(m, e0, e1):
             src = weights[m][0].rearrange("e s p b -> p (e s) b")
@@ -91,15 +107,15 @@ def tile_moe_pre_glu_sigmoid_kernel(
                 nc.sync.dma_start(w_scales[m][QUAD * q : QUAD * q + 4, :, :].bitcast(I32), src[q].bitcast(I32))
 
         nc.sync.dma_start(offs_sb[:], offs)
+        nc.scalar.dma_start(gate_first[:], gate[0:P, 0 : GROUPS[0]])
         for t in range(PACK):
-            nc.sync.dma_start(x_phase[t][:, 0:T], x_rows[t])
-            load_gate(nc.scalar, 0, t, t + 1)
+            nc.sync.dma_start(x_phase[t][:], x_rows[t])
         nc.scalar.activation(warm_out[:], warm_in[:], SIGMOID)
-        for g in range(1, len(GROUPS)):
-            load_gate(nc.sync, g, 0, PACK)
-        for m in ("w3", "w1"):
-            load_scales(m)
-            load_codes(m, 0, E // 2)
+        nc.sync.dma_start(gate_rest[:], gate[0:P, GROUPS[0] : S])
+        load_codes("w3", 0, E // 2)
+        load_scales("w3")
+        load_scales("w1")
+        load_codes("w1", 0, E // 2)
         for m in ("w1", "w3"):
             load_codes(m, E // 2, E)
         load_scales("w2")
@@ -107,35 +123,21 @@ def tile_moe_pre_glu_sigmoid_kernel(
         nc.sync.dma_start(pos1_sb[:], pos1)
         nc.sync.dma_start(pos2_sb[:], pos2)
 
-        x_rounded = {}
-        x_quant = {}
-
-        def gather_x(g):
+        def gather_x(g, t):
             entries = offs_sb[:, group_start[g] // STRIPE : (group_start[g] + GROUPS[g]) // STRIPE]
-            for t in range(PACK):
-                nc.vector.tensor_tensor(x_gated[g][:, t, :], x_phase[t][:].indirect(entries), gate_sb[g][:, t, :], MULT)
+            nc.vector.tensor_tensor(plane(g, t, 0, GROUPS[g]), x_phase[t][:].indirect(entries), gate_of(g), MULT)
 
-        def round_x(c, dst):
+        def round_x(c):
             g = max(j for j in range(len(GROUPS)) if group_start[j] <= c * CHUNK)
             s0 = c * CHUNK - group_start[g]
+            planes = plane(g, 0, 0, PACK * PLANES[g][1]).rearrange("p (t s) -> p t s", t=PACK)
             nc.scalar.copy(
-                dst.rearrange("p (s i t) -> p s t i", i=4, t=PACK),
-                x_gated[g][:, :, s0 : s0 + CHUNK].rearrange("p t (s i) -> p s t i", i=4),
+                x_bf16[c].rearrange("p (s i t) -> p s t i", i=4, t=PACK),
+                planes[:, :, s0 : s0 + CHUNK].rearrange("p t (s i) -> p s t i", i=4),
             )
-            x_rounded[c] = dst
-
-        def round_x_apart(c):
-            dst = work.tile([P, CHUNK * PACK], BF16, name="x_bf16", align_bytes=MX_ALIGN)
-            round_x(c, dst[:])
 
         def quantize_x(c):
-            codes = work.tile([P, CHUNK], U32, name="x_codes", align_bytes=MX_ALIGN)
-            scales = work.tile([P, CHUNK], U8, name="x_scales", align_bytes=MX_ALIGN)
-            nc.vector.quantize_mx(codes[:].bitcast(FP8X4), scales[:], x_rounded[c])
-            x_quant[c] = (codes, scales)
-
-        def h_rows(c):
-            return gate_sb[-1][:, PACK - 1 - c % PACK, :].bitcast(BF16)
+            nc.vector.quantize_mx(x_codes[c][:].bitcast(FP8X4), x_scales[c][:], x_bf16[c])
 
         def pairs_of_bank(bank):
             return bank[:].rearrange("s (q u e) -> s u q e", u=2, e=2)
@@ -144,115 +146,126 @@ def tile_moe_pre_glu_sigmoid_kernel(
             return rows.rearrange("s (u q e) -> s u q e", u=2, e=2)
 
         def first_layer(c, m, bank):
-            codes, scales = x_quant[c]
             e = c * CHUNK // C
             nc.tensor.matmul_mx(
                 bank[:],
-                lhsT=codes[:].bitcast(FP8X4),
-                lhsT_scale=scales[:],
+                lhsT=x_codes[c][:].bitcast(FP8X4),
+                lhsT_scale=x_scales[c][:],
                 rhs=w_codes[m][:, e, :].bitcast(FP4X4),
                 rhs_scale=w_scales[m][:, e, :],
                 start=True,
                 stop=True,
             )
 
-        def hidden(c):
-            a, b = a_bank[c % LAYER1_BANKS], b_bank[c % LAYER1_BANKS]
-            first_layer(c, "w1", a)
-            nc.scalar.activation(in_pair_order(sig[c][:]), pairs_of_bank(a), SIGMOID)
-            first_layer(c, "w3", b)
-            nc.vector.tensor_tensor(in_pair_order(h_rows(c)), pairs_of_bank(b), in_pair_order(sig[c][:]), MULT)
+        def sigmoid(c):
+            first_layer(c, "w1", a_bank[c])
+            nc.scalar.activation(in_pair_order(sig[c]), pairs_of_bank(a_bank[c]), SIGMOID)
 
-        def turn_h(run, copy):
+        def hidden(c):
+            first_layer(c, "w3", b_bank[c])
+            nc.vector.tensor_tensor(
+                in_pair_order(h_rows[c].bitcast(BF16)), pairs_of_bank(b_bank[c]), in_pair_order(sig[c]), MULT
+            )
+
+        def turn_h(run):
             c0, count = H_RUNS[run]
-            bank = turn_bank[run % TURN_BANKS][:, 0 : 2 * CHUNK * count].rearrange("q (c u s) -> q c u s", u=2, s=CHUNK)
+            bank = run_bank[run][:, 0 : 2 * CHUNK * count].rearrange("q (c u s) -> q c u s", u=2, s=CHUNK)
             for c in range(count):
-                words = h_rows(c0 + c).bitcast(F32)
                 for u in range(2):
-                    nc.tensor.transpose(bank[:, c, u, :], words[:, u * P : (u + 1) * P], identity[:])
+                    nc.tensor.transpose(bank[:, c, u, :], h_rows[c0 + c][:, u * P : (u + 1) * P], identity[:])
             dst = h_turned[:, c0 * CHUNK * PACK : (c0 + count) * CHUNK * PACK].bitcast(F32)
-            copy(dst.rearrange("q (c s u) -> q c s u", u=2, s=CHUNK), bank.rearrange("q c u s -> q c s u"))
+            nc.scalar.copy(dst.rearrange("q (c s u) -> q c s u", u=2, s=CHUNK), bank.rearrange("q c u s -> q c s u"))
 
         def quantize_h(run):
             c0, count = H_RUNS[run]
             lo, hi = c0 * CHUNK, (c0 + count) * CHUNK
             nc.vector.quantize_mx(h_codes[:, lo:hi].bitcast(FP8X4), h_scales[:, lo:hi], h_turned[:, lo * PACK : hi * PACK])
 
-        gather_x(0)
-        for c in range(0, 4):
-            round_x_apart(c)
-        for c in range(0, 2):
-            quantize_x(c)
-        gather_x(1)
-        for c in range(4, 6):
-            round_x_apart(c)
-        for c in range(2, 4):
-            quantize_x(c)
-        gather_x(2)
-        for c in range(4, 6):
-            quantize_x(c)
-
-        hidden(0)
-        hidden(1)
-        for c in range(6, 8):
-            round_x(c, sig[1][:, (c - 6) * H // 2 : (c - 5) * H // 2].bitcast(BF16))
-        for c in range(6, 8):
-            quantize_x(c)
-        hidden(2)
-        hidden(3)
-        turn_h(0, nc.vector.tensor_copy)
-        hidden(4)
-        hidden(5)
-        turn_h(1, nc.scalar.copy)
-        quantize_h(0)
-        hidden(6)
-        hidden(7)
-        turn_h(2, nc.scalar.copy)
-        quantize_h(1)
-        turn_h(3, nc.scalar.copy)
-        turn_h(4, nc.scalar.copy)
-        for run in range(2, len(H_RUNS)):
-            quantize_h(run)
-
-        def second_layer(nt, s0, width, bank):
-            step = min(width, C)
-            for lo in range(s0, s0 + width, step):
+        def second_layer(nt, s0, s1, bank):
+            lo = s0
+            while lo < s1:
+                hi = min(s1, (lo // C + 1) * C)
                 e = lo // C
                 nc.tensor.matmul_mx(
-                    bank[:, lo - s0 : lo - s0 + step],
+                    bank[:, lo - s0 : hi - s0],
                     lhsT=w_codes["w2"][:, e, 2 * P * nt : 2 * P * (nt + 1)].bitcast(FP4X4),
                     lhsT_scale=w_scales["w2"][:, e, P * nt : P * (nt + 1)],
-                    rhs=h_codes[:, lo : lo + step].bitcast(FP8X4),
-                    rhs_scale=h_scales[:, lo : lo + step],
+                    rhs=h_codes[:, lo:hi].bitcast(FP8X4),
+                    rhs_scale=h_scales[:, lo:hi],
                     start=True,
                     stop=True,
                 )
-            nc.scalar.copy(y[nt][:, s0 : s0 + width], bank[:, 0:width])
+                lo = hi
+            nc.scalar.copy(y[nt][:, s0:s1], bank[:, 0 : s1 - s0])
 
-        first_tile_banks = [a_bank[c % LAYER1_BANKS] for c in range(CHUNKS - 3, CHUNKS)]
-        first_tile_banks += [b_bank[c % LAYER1_BANKS] for c in range(CHUNKS - 2, CHUNKS)]
-        for (c0, count), bank in zip(H_RUNS, first_tile_banks):
-            second_layer(0, c0 * CHUNK, count * CHUNK, bank)
+        for t in range(PACK):
+            gather_x(0, t)
+        for c in (0, 1, 2):
+            round_x(c)
+        gather_x(1, 0)
+        quantize_x(0)
+        sigmoid(0)
+        gather_x(1, 1)
+        for c in (1, 2):
+            quantize_x(c)
+            sigmoid(c)
+        gather_x(1, 2)
+        gather_x(1, 3)
+        hidden(0)
+        hidden(1)
+        for c in (3, 4, 5):
+            round_x(c)
+        gather_x(2, 0)
+        gather_x(2, 1)
+        quantize_x(3)
+        for t in (2, 3):
+            quantize_x(2 + t)
+            gather_x(2, t)
+        sigmoid(3)
+        turn_h(0)
+        sigmoid(4)
+        for c in (6, 7):
+            round_x(c)
+            quantize_x(c)
+        for c in (5, 6, 7):
+            sigmoid(c)
+        hidden(2)
+        hidden(3)
+        turn_h(1)
+        hidden(4)
+        hidden(5)
+        turn_h(2)
+        hidden(6)
+        turn_h(3)
+        hidden(7)
+        turn_h(4)
+        for run in range(len(H_RUNS)):
+            quantize_h(run)
+
+        half = S // 2
+        second_layer(0, 0, half, banks[1])
+        second_layer(0, half, S - CHUNK, banks[7])
+        second_layer(0, S - CHUNK, S, banks[3])
         for nt in range(1, N // P):
-            second_layer(nt, S // 2, S // 2, first_tile_banks[-2])
-            second_layer(nt, 0, S // 2, first_tile_banks[-1])
+            second_layer(nt, half, S, banks[6])
+            second_layer(nt, 0, half, banks[3])
 
-        def fetch(nt, t0, width):
-            both = []
-            for pos_sb in (pos1_sb, pos2_sb):
-                picked = work.tile([P, width], F32, name="picked", tag=f"picked{width}", bufs=6)
-                nc.vector.tensor_copy(picked[:], y[nt][:].indirect(pos_sb[:, t0 // STRIPE : (t0 + width) // STRIPE]))
-                both.append(picked)
-            return both
+        first = [tile(f"first{nt}", T, F32) for nt in range(N // P)]
+        second = [tile(f"second{nt}", T, F32) for nt in range(N // P - 1)]
+        total = [tile(f"total{nt}", T, F32) for nt in range(N // P)]
 
-        def combine(nt, t0, width, both):
-            engine = nc.gpsimd if width == T else nc.vector
-            total = work.tile([P, width], F32, name="total", tag=f"total{width}", bufs=4)
-            engine.tensor_tensor(total[:], both[0][:], both[1][:], ADD)
-            nc.sync.dma_start(out[nt * P : (nt + 1) * P, t0 : t0 + width], total[:])
+        def picked(nt, pos_sb, t0, t1):
+            return y[nt][:].indirect(pos_sb[:, t0 // STRIPE : t1 // STRIPE])
 
-        fetched = [fetch(*RESULT_PIECES[0])]
-        for before, piece in zip(RESULT_PIECES, RESULT_PIECES[1:]):
-            fetched.append(fetch(*piece))
-            combine(*before, fetched[-2])
-        combine(*RESULT_PIECES[-1], fetched[-1])
+        for nt in range(N // P - 1):
+            nc.vector.tensor_copy(first[nt][:], picked(nt, pos1_sb, 0, T))
+            nc.vector.tensor_copy(second[nt][:], picked(nt, pos2_sb, 0, T))
+            nc.gpsimd.tensor_tensor(total[nt][:], first[nt][:], second[nt][:], ADD)
+            nc.sync.dma_start(out[nt * P : (nt + 1) * P, :], total[nt][:])
+        nt = N // P - 1
+        pieces = [(sum(LAST_PIECES[:j]), sum(LAST_PIECES[: j + 1])) for j in range(len(LAST_PIECES))]
+        for t0, t1 in pieces:
+            nc.vector.tensor_copy(first[nt][:, t0:t1], picked(nt, pos1_sb, t0, t1))
+        for t0, t1 in pieces:
+            nc.vector.tensor_tensor(total[nt][:, t0:t1], picked(nt, pos2_sb, t0, t1), first[nt][:, t0:t1], ADD)
+            nc.sync.dma_start(out[nt * P : (nt + 1) * P, t0:t1], total[nt][:, t0:t1])

@@ -68,7 +68,7 @@ def tile_moe_pre_glu_sigmoid_kernel(
         banks = [psum.tile([P, BANK], F32, name=f"bank{j}") for j in range(8)]
         a_bank = [banks[j] for j in (0, 1, 2, 4, 1, 2, 4, 1)]
         b_bank = [banks[j] for j in (3, 0, 3, 0, 5, 3, 0, 5)]
-        run_bank = [banks[j] for j in (6, 7, 6, 2, 4)]
+        run_bank = [banks[j] for j in (6, 2, 6, 7, 4)]
 
         def gate_of(g):
             s0 = group_start[g] - GROUPS[0]
@@ -84,9 +84,10 @@ def tile_moe_pre_glu_sigmoid_kernel(
         sig[0] = plane(2, 0, -CHUNK, H - CHUNK)
         for c in (4, 5):
             x_bf16[c] = sig[1][:, (c - 4) * H // 2 : (c - 3) * H // 2].bitcast(BF16)
-        h_rows = {c: tile(f"h_rows{c}", H // 2, F32)[:] for c in (0, 1, 4, 5, 6, 7)}
+        h_rows = {c: tile(f"h_rows{c}", H // 2, F32)[:] for c in (0, 1, 5, 6, 7)}
         h_rows[2] = plane(1, 1, CHUNK, 3 * CHUNK)
         h_rows[3] = plane(1, 3, CHUNK, 3 * CHUNK)
+        h_rows[4] = plane(2, 3, CHUNK, 3 * CHUNK)
 
         warm_in = keep.tile([P, 8], F32, name="warm_in")
         warm_out = keep.tile([P, 8], F32, name="warm_out")
@@ -113,9 +114,9 @@ def tile_moe_pre_glu_sigmoid_kernel(
         nc.scalar.activation(warm_out[:], warm_in[:], SIGMOID)
         nc.sync.dma_start(gate_rest[:], gate[0:P, GROUPS[0] : S])
         load_codes("w3", 0, E // 2)
+        load_codes("w1", 0, E // 2)
         load_scales("w3")
         load_scales("w1")
-        load_codes("w1", 0, E // 2)
         for m in ("w1", "w3"):
             load_codes(m, E // 2, E)
         load_scales("w2")
@@ -161,8 +162,10 @@ def tile_moe_pre_glu_sigmoid_kernel(
             first_layer(c, "w1", a_bank[c])
             nc.scalar.activation(in_pair_order(sig[c]), pairs_of_bank(a_bank[c]), SIGMOID)
 
-        def hidden(c):
+        def linear(c):
             first_layer(c, "w3", b_bank[c])
+
+        def hidden(c):
             nc.vector.tensor_tensor(
                 in_pair_order(h_rows[c].bitcast(BF16)), pairs_of_bank(b_bank[c]), in_pair_order(sig[c]), MULT
             )
@@ -176,12 +179,11 @@ def tile_moe_pre_glu_sigmoid_kernel(
             dst = h_turned[:, c0 * CHUNK * PACK : (c0 + count) * CHUNK * PACK].bitcast(F32)
             nc.scalar.copy(dst.rearrange("q (c s u) -> q c s u", u=2, s=CHUNK), bank.rearrange("q c u s -> q c s u"))
 
-        def quantize_h(run):
-            c0, count = H_RUNS[run]
+        def quantize_h(c0, count):
             lo, hi = c0 * CHUNK, (c0 + count) * CHUNK
             nc.vector.quantize_mx(h_codes[:, lo:hi].bitcast(FP8X4), h_scales[:, lo:hi], h_turned[:, lo * PACK : hi * PACK])
 
-        def second_layer(nt, s0, s1, bank):
+        def second_layer(nt, s0, s1, bank, copy=nc.scalar.copy):
             lo = s0
             while lo < s1:
                 hi = min(s1, (lo // C + 1) * C)
@@ -196,7 +198,7 @@ def tile_moe_pre_glu_sigmoid_kernel(
                     stop=True,
                 )
                 lo = hi
-            nc.scalar.copy(y[nt][:, s0:s1], bank[:, 0 : s1 - s0])
+            copy(y[nt][:, s0:s1], bank[:, 0 : s1 - s0])
 
         for t in range(PACK):
             gather_x(0, t)
@@ -211,8 +213,10 @@ def tile_moe_pre_glu_sigmoid_kernel(
             sigmoid(c)
         gather_x(1, 2)
         gather_x(1, 3)
-        hidden(0)
-        hidden(1)
+        for c in (0, 1):
+            linear(c)
+            hidden(c)
+        linear(2)
         for c in (3, 4, 5):
             round_x(c)
         gather_x(2, 0)
@@ -221,33 +225,34 @@ def tile_moe_pre_glu_sigmoid_kernel(
         for t in (2, 3):
             quantize_x(2 + t)
             gather_x(2, t)
-        sigmoid(3)
         turn_h(0)
-        sigmoid(4)
+        for c in (3, 4):
+            sigmoid(c)
+            linear(c)
         for c in (6, 7):
             round_x(c)
             quantize_x(c)
         for c in (5, 6, 7):
             sigmoid(c)
-        hidden(2)
-        hidden(3)
+        for c in (2, 3, 4):
+            hidden(c)
+            linear(c + 3)
         turn_h(1)
-        hidden(4)
         hidden(5)
         turn_h(2)
         hidden(6)
         turn_h(3)
         hidden(7)
         turn_h(4)
-        for run in range(len(H_RUNS)):
-            quantize_h(run)
+        for c0, count in ((0, 4), (4, 2), (6, 1), (7, 1)):
+            quantize_h(c0, count)
 
         half = S // 2
         second_layer(0, 0, half, banks[1])
-        second_layer(0, half, S - CHUNK, banks[7])
+        second_layer(0, half, S - CHUNK, banks[0], nc.vector.tensor_copy)
         second_layer(0, S - CHUNK, S, banks[3])
         for nt in range(1, N // P):
-            second_layer(nt, half, S, banks[6])
+            second_layer(nt, half, S, banks[7])
             second_layer(nt, 0, half, banks[3])
 
         first = [tile(f"first{nt}", T, F32) for nt in range(N // P)]

@@ -66,9 +66,9 @@ def tile_moe_pre_glu_sigmoid_kernel(
         h_scales = tile("h_scales", S, U8)
         y = [tile(f"y{nt}", S, F32) for nt in range(N // P)]
         banks = [psum.tile([P, BANK], F32, name=f"bank{j}") for j in range(8)]
-        a_bank = [banks[j] for j in (0, 1, 2, 4, 1, 2, 4, 1)]
-        b_bank = [banks[j] for j in (3, 0, 3, 0, 5, 3, 0, 5)]
-        run_bank = [banks[j] for j in (6, 2, 6, 7, 4)]
+        a_bank = [banks[j] for j in (0, 1, 2, 4, 1, 2, 0, 1)]
+        b_bank = [banks[j] for j in (3, 0, 3, 4, 5, 3, 4, 5)]
+        run_bank = [banks[j] for j in (6, 2, 6, 7, 0)]
 
         def gate_of(g):
             s0 = group_start[g] - GROUPS[0]
@@ -107,9 +107,10 @@ def tile_moe_pre_glu_sigmoid_kernel(
             for q in (0, 2, 1, 3):
                 nc.sync.dma_start(w_scales[m][QUAD * q : QUAD * q + 4, :, :].bitcast(I32), src[q].bitcast(I32))
 
-        nc.sync.dma_start(offs_sb[:], offs)
+        nc.sync.dma_start(x_phase[0][:], x_rows[0])
         nc.scalar.dma_start(gate_first[:], gate[0:P, 0 : GROUPS[0]])
-        for t in range(PACK):
+        nc.sync.dma_start(offs_sb[:], offs)
+        for t in range(1, PACK):
             nc.sync.dma_start(x_phase[t][:], x_rows[t])
         nc.scalar.activation(warm_out[:], warm_in[:], SIGMOID)
         nc.sync.dma_start(gate_rest[:], gate[0:P, GROUPS[0] : S])
@@ -216,6 +217,7 @@ def tile_moe_pre_glu_sigmoid_kernel(
         for c in (0, 1):
             linear(c)
             hidden(c)
+        first_layer(0, "w3", b_bank[0])
         linear(2)
         for c in (3, 4, 5):
             round_x(c)
@@ -226,6 +228,7 @@ def tile_moe_pre_glu_sigmoid_kernel(
             quantize_x(2 + t)
             gather_x(2, t)
         turn_h(0)
+        first_layer(1, "w3", b_bank[1])
         for c in (3, 4):
             sigmoid(c)
             linear(c)
@@ -242,14 +245,16 @@ def tile_moe_pre_glu_sigmoid_kernel(
         turn_h(2)
         hidden(6)
         turn_h(3)
+        first_layer(6, "w3", b_bank[6])
         hidden(7)
         turn_h(4)
+        first_layer(7, "w3", b_bank[7])
         for c0, count in ((0, 4), (4, 2), (6, 1), (7, 1)):
             quantize_h(c0, count)
 
         half = S // 2
         second_layer(0, 0, half, banks[1])
-        second_layer(0, half, S - CHUNK, banks[0], nc.vector.tensor_copy)
+        second_layer(0, half, S - CHUNK, banks[4], nc.vector.tensor_copy)
         second_layer(0, S - CHUNK, S, banks[3])
         for nt in range(1, N // P):
             second_layer(nt, half, S, banks[7])

@@ -108,8 +108,9 @@ def tile_moe_pre_glu_sigmoid_kernel(
                 nc.sync.dma_start(w_scales[m][QUAD * q : QUAD * q + 4, :, :].bitcast(I32), src[q].bitcast(I32))
 
         nc.sync.dma_start(x_phase[0][:], x_rows[0])
-        nc.scalar.dma_start(gate_first[:], gate[0:P, 0 : GROUPS[0]])
+        nc.scalar.dma_start(gate_first[:, 0:CHUNK], gate[0:P, 0:CHUNK])
         nc.sync.dma_start(offs_sb[:], offs)
+        nc.sync.dma_start(gate_first[:, CHUNK : GROUPS[0]], gate[0:P, CHUNK : GROUPS[0]])
         for t in range(1, PACK):
             nc.sync.dma_start(x_phase[t][:], x_rows[t])
         nc.scalar.activation(warm_out[:], warm_in[:], SIGMOID)
@@ -125,9 +126,10 @@ def tile_moe_pre_glu_sigmoid_kernel(
         nc.sync.dma_start(pos1_sb[:], pos1)
         nc.sync.dma_start(pos2_sb[:], pos2)
 
-        def gather_x(g, t):
-            entries = offs_sb[:, group_start[g] // STRIPE : (group_start[g] + GROUPS[g]) // STRIPE]
-            nc.vector.tensor_tensor(plane(g, t, 0, GROUPS[g]), x_phase[t][:].indirect(entries), gate_of(g), MULT)
+        def gather_x(g, t, lo=0, hi=None):
+            hi = GROUPS[g] if hi is None else hi
+            entries = offs_sb[:, (group_start[g] + lo) // STRIPE : (group_start[g] + hi) // STRIPE]
+            nc.vector.tensor_tensor(plane(g, t, lo, hi), x_phase[t][:].indirect(entries), gate_of(g)[:, lo:hi], MULT)
 
         def round_x(c):
             g = max(j for j in range(len(GROUPS)) if group_start[j] <= c * CHUNK)
@@ -201,7 +203,9 @@ def tile_moe_pre_glu_sigmoid_kernel(
                 lo = hi
             copy(y[nt][:, s0:s1], bank[:, 0 : s1 - s0])
 
-        for t in range(PACK):
+        gather_x(0, 0, 0, CHUNK)
+        gather_x(0, 0, CHUNK)
+        for t in range(1, PACK):
             gather_x(0, t)
         for c in (0, 1, 2):
             round_x(c)
@@ -243,9 +247,9 @@ def tile_moe_pre_glu_sigmoid_kernel(
         turn_h(1)
         hidden(5)
         turn_h(2)
+        first_layer(5, "w3", b_bank[5])
         hidden(6)
         turn_h(3)
-        first_layer(6, "w3", b_bank[6])
         hidden(7)
         turn_h(4)
         first_layer(7, "w3", b_bank[7])
@@ -269,9 +273,12 @@ def tile_moe_pre_glu_sigmoid_kernel(
 
         for nt in range(N // P - 1):
             nc.vector.tensor_copy(first[nt][:], picked(nt, pos1_sb, 0, T))
-            nc.vector.tensor_copy(second[nt][:], picked(nt, pos2_sb, 0, T))
-            nc.gpsimd.tensor_tensor(total[nt][:], first[nt][:], second[nt][:], ADD)
-            nc.sync.dma_start(out[nt * P : (nt + 1) * P, :], total[nt][:])
+            width = T // 2 if nt == N // P - 2 else T
+            for t0 in range(0, T, width):
+                t1 = t0 + width
+                nc.vector.tensor_copy(second[nt][:, t0:t1], picked(nt, pos2_sb, t0, t1))
+                nc.gpsimd.tensor_tensor(total[nt][:, t0:t1], first[nt][:, t0:t1], second[nt][:, t0:t1], ADD)
+                nc.sync.dma_start(out[nt * P : (nt + 1) * P, t0:t1], total[nt][:, t0:t1])
         nt = N // P - 1
         pieces = [(sum(LAST_PIECES[:j]), sum(LAST_PIECES[: j + 1])) for j in range(len(LAST_PIECES))]
         for t0, t1 in pieces:

@@ -6,6 +6,7 @@ from concourse.masks import make_identity
 K, T, E, C, H, N = 512, 512, 4, 256, 512, 512
 S = E * C
 FLOPS = 2 * S * (2 * K * H + H * N)
+BYTES = 4 * (K * T + N * T + S) + E * (2 * K * H + H * N) * 17 // 32 + 2 * 8 * (S + 2 * T)
 
 F32 = mybir.dt.float32
 BF16 = mybir.dt.bfloat16
@@ -27,12 +28,24 @@ MX_ALIGN = 64
 CHUNK = 128
 CHUNKS = S // CHUNK
 BANK = 512
+BANKS = 8
+WORDS = H // 2
+Y_TILES = N // P
 
-GROUPS = (384, 384, 256)
-PLANES = ((1920, 384), (1152, 512), (640, 256))
-STAGE_WIDTH = 3456
-H_RUNS = ((0, 2), (2, 2), (4, 2), (6, 1), (7, 1))
-LAST_PIECES = (384, 128)
+GROUPS = (3 * CHUNK, 3 * CHUNK, 2 * CHUNK)
+
+GROUP2_AT, GROUP2_STEP = WORDS, GROUPS[2]
+GROUP1_AT, GROUP1_STEP = GROUP2_AT + 2 * GROUP2_STEP, GROUPS[1] + CHUNK
+GROUP0_AT, GROUP0_STEP = GROUP1_AT + GROUP1_STEP + GROUPS[1] - CHUNK, GROUPS[0]
+PHASES_AT = ((GROUP0_AT, GROUP0_STEP), (GROUP1_AT, GROUP1_STEP), (GROUP2_AT, GROUP2_STEP))
+STAGE_WIDTH = GROUP0_AT + PACK * GROUP0_STEP
+
+TURNS = ((0, 2), (2, 2), (4, 2), (6, 1), (7, 1))
+H_QUANT = ((0, 4), (4, 2), (6, 1), (7, 1))
+A_BANKS = (0, 1, 2, 4, 1, 2, 0, 1)
+B_BANKS = (3, 0, 3, 4, 5, 3, 4, 5)
+TURN_BANKS = (6, 2, 6, 7, 0)
+LAST_PIECES = ((0, 3 * T // 4), (3 * T // 4, T))
 
 
 def tile_moe_pre_glu_sigmoid_kernel(
@@ -64,30 +77,27 @@ def tile_moe_pre_glu_sigmoid_kernel(
         h_turned = tile("h_turned", S * PACK, BF16)
         h_codes = tile("h_codes", S, U32)
         h_scales = tile("h_scales", S, U8)
-        y = [tile(f"y{nt}", S, F32) for nt in range(N // P)]
-        banks = [psum.tile([P, BANK], F32, name=f"bank{j}") for j in range(8)]
-        a_bank = [banks[j] for j in (0, 1, 2, 4, 1, 2, 0, 1)]
-        b_bank = [banks[j] for j in (3, 0, 3, 4, 5, 3, 4, 5)]
-        run_bank = [banks[j] for j in (6, 2, 6, 7, 0)]
+        y = [tile(f"y{nt}", S, F32) for nt in range(Y_TILES)]
+        banks = [psum.tile([P, BANK], F32, name=f"bank{j}") for j in range(BANKS)]
 
         def gate_of(g):
             s0 = group_start[g] - GROUPS[0]
             return gate_first[:] if g == 0 else gate_rest[:, s0 : s0 + GROUPS[g]]
 
-        def plane(g, t, lo, hi):
-            first, step = PLANES[g]
-            return stage[:, first + t * step + lo : first + t * step + hi]
+        def staged(g, t, lo, hi):
+            at, step = PHASES_AT[g]
+            return stage[:, at + t * step + lo : at + t * step + hi]
 
         x_bf16 = {c: tile(f"x_bf16_{c}", CHUNK * PACK, BF16)[:] for c in (0, 1, 2, 6, 7)}
-        x_bf16[3] = plane(2, 0, -H // 2, 0).bitcast(BF16)
+        x_bf16[3] = staged(2, 0, -WORDS, 0).bitcast(BF16)
         sig = {c: tile(f"sig{c}", H, F32)[:] for c in range(1, CHUNKS)}
-        sig[0] = plane(2, 0, -CHUNK, H - CHUNK)
+        sig[0] = staged(2, 0, -CHUNK, H - CHUNK)
         for c in (4, 5):
-            x_bf16[c] = sig[1][:, (c - 4) * H // 2 : (c - 3) * H // 2].bitcast(BF16)
-        h_rows = {c: tile(f"h_rows{c}", H // 2, F32)[:] for c in (0, 1, 5, 6, 7)}
-        h_rows[2] = plane(1, 1, CHUNK, 3 * CHUNK)
-        h_rows[3] = plane(1, 3, CHUNK, 3 * CHUNK)
-        h_rows[4] = plane(2, 3, CHUNK, 3 * CHUNK)
+            x_bf16[c] = sig[1][:, (c - 4) * WORDS : (c - 3) * WORDS].bitcast(BF16)
+        h_rows = {c: tile(f"h_rows{c}", WORDS, F32)[:] for c in (0, 1, 5, 6, 7)}
+        h_rows[2] = staged(1, 1, CHUNK, CHUNK + WORDS)
+        h_rows[3] = staged(1, 3, CHUNK, CHUNK + WORDS)
+        h_rows[4] = staged(2, 3, CHUNK, CHUNK + WORDS)
 
         warm_in = keep.tile([P, 8], F32, name="warm_in")
         warm_out = keep.tile([P, 8], F32, name="warm_out")
@@ -115,10 +125,10 @@ def tile_moe_pre_glu_sigmoid_kernel(
             nc.sync.dma_start(x_phase[t][:], x_rows[t])
         nc.scalar.activation(warm_out[:], warm_in[:], SIGMOID)
         nc.sync.dma_start(gate_rest[:], gate[0:P, GROUPS[0] : S])
-        load_codes("w3", 0, E // 2)
-        load_codes("w1", 0, E // 2)
-        load_scales("w3")
-        load_scales("w1")
+        for m in ("w3", "w1"):
+            load_codes(m, 0, E // 2)
+        for m in ("w3", "w1"):
+            load_scales(m)
         for m in ("w1", "w3"):
             load_codes(m, E // 2, E)
         load_scales("w2")
@@ -126,18 +136,20 @@ def tile_moe_pre_glu_sigmoid_kernel(
         nc.sync.dma_start(pos1_sb[:], pos1)
         nc.sync.dma_start(pos2_sb[:], pos2)
 
-        def gather_x(g, t, lo=0, hi=None):
-            hi = GROUPS[g] if hi is None else hi
+        def gather_x(g, t, lo, hi):
             entries = offs_sb[:, (group_start[g] + lo) // STRIPE : (group_start[g] + hi) // STRIPE]
-            nc.vector.tensor_tensor(plane(g, t, lo, hi), x_phase[t][:].indirect(entries), gate_of(g)[:, lo:hi], MULT)
+            nc.vector.tensor_tensor(staged(g, t, lo, hi), x_phase[t][:].indirect(entries), gate_of(g)[:, lo:hi], MULT)
+
+        def gather_phase(g, t):
+            gather_x(g, t, 0, GROUPS[g])
 
         def round_x(c):
             g = max(j for j in range(len(GROUPS)) if group_start[j] <= c * CHUNK)
             s0 = c * CHUNK - group_start[g]
-            planes = plane(g, 0, 0, PACK * PLANES[g][1]).rearrange("p (t s) -> p t s", t=PACK)
+            phases = staged(g, 0, 0, PACK * PHASES_AT[g][1]).rearrange("p (t s) -> p t s", t=PACK)
             nc.scalar.copy(
                 x_bf16[c].rearrange("p (s i t) -> p s t i", i=4, t=PACK),
-                planes[:, :, s0 : s0 + CHUNK].rearrange("p t (s i) -> p s t i", i=4),
+                phases[:, :, s0 : s0 + CHUNK].rearrange("p t (s i) -> p s t i", i=4),
             )
 
         def quantize_x(c):
@@ -150,32 +162,35 @@ def tile_moe_pre_glu_sigmoid_kernel(
             return rows.rearrange("s (u q e) -> s u q e", u=2, e=2)
 
         def first_layer(c, m, bank):
-            e = c * CHUNK // C
+            expert = c * CHUNK // C
             nc.tensor.matmul_mx(
                 bank[:],
                 lhsT=x_codes[c][:].bitcast(FP8X4),
                 lhsT_scale=x_scales[c][:],
-                rhs=w_codes[m][:, e, :].bitcast(FP4X4),
-                rhs_scale=w_scales[m][:, e, :],
+                rhs=w_codes[m][:, expert, :].bitcast(FP4X4),
+                rhs_scale=w_scales[m][:, expert, :],
                 start=True,
                 stop=True,
             )
 
-        def sigmoid(c):
-            first_layer(c, "w1", a_bank[c])
-            nc.scalar.activation(in_pair_order(sig[c]), pairs_of_bank(a_bank[c]), SIGMOID)
+        def sigmoid_of_a(c):
+            first_layer(c, "w1", banks[A_BANKS[c]])
+            nc.scalar.activation(in_pair_order(sig[c]), pairs_of_bank(banks[A_BANKS[c]]), SIGMOID)
 
-        def linear(c):
-            first_layer(c, "w3", b_bank[c])
+        def product_b(c):
+            first_layer(c, "w3", banks[B_BANKS[c]])
 
-        def hidden(c):
+        def multiply(c):
             nc.vector.tensor_tensor(
-                in_pair_order(h_rows[c].bitcast(BF16)), pairs_of_bank(b_bank[c]), in_pair_order(sig[c]), MULT
+                in_pair_order(h_rows[c].bitcast(BF16)), pairs_of_bank(banks[B_BANKS[c]]), in_pair_order(sig[c]), MULT
             )
 
-        def turn_h(run):
-            c0, count = H_RUNS[run]
-            bank = run_bank[run][:, 0 : 2 * CHUNK * count].rearrange("q (c u s) -> q c u s", u=2, s=CHUNK)
+        def keep_clock_up(c):
+            product_b(c)
+
+        def turn_h(turn):
+            c0, count = TURNS[turn]
+            bank = banks[TURN_BANKS[turn]][:, 0 : 2 * CHUNK * count].rearrange("q (c u s) -> q c u s", u=2, s=CHUNK)
             for c in range(count):
                 for u in range(2):
                     nc.tensor.transpose(bank[:, c, u, :], h_rows[c0 + c][:, u * P : (u + 1) * P], identity[:])
@@ -186,103 +201,107 @@ def tile_moe_pre_glu_sigmoid_kernel(
             lo, hi = c0 * CHUNK, (c0 + count) * CHUNK
             nc.vector.quantize_mx(h_codes[:, lo:hi].bitcast(FP8X4), h_scales[:, lo:hi], h_turned[:, lo * PACK : hi * PACK])
 
-        def second_layer(nt, s0, s1, bank, copy=nc.scalar.copy):
-            lo = s0
-            while lo < s1:
-                hi = min(s1, (lo // C + 1) * C)
-                e = lo // C
+        gather_x(0, 0, 0, CHUNK)
+        gather_x(0, 0, CHUNK, GROUPS[0])
+        for t in range(1, PACK):
+            gather_phase(0, t)
+        for c in (0, 1, 2):
+            round_x(c)
+        gather_phase(1, 0)
+        quantize_x(0)
+        sigmoid_of_a(0)
+        gather_phase(1, 1)
+        for c in (1, 2):
+            quantize_x(c)
+            sigmoid_of_a(c)
+        gather_phase(1, 2)
+        gather_phase(1, 3)
+        for c in (0, 1):
+            product_b(c)
+            multiply(c)
+        keep_clock_up(0)
+        product_b(2)
+        for c in (3, 4, 5):
+            round_x(c)
+        gather_phase(2, 0)
+        gather_phase(2, 1)
+        quantize_x(3)
+        quantize_x(4)
+        gather_phase(2, 2)
+        quantize_x(5)
+        gather_phase(2, 3)
+        turn_h(0)
+        keep_clock_up(1)
+        for c in (3, 4):
+            sigmoid_of_a(c)
+            product_b(c)
+        for c in (6, 7):
+            round_x(c)
+            quantize_x(c)
+        for c in (5, 6, 7):
+            sigmoid_of_a(c)
+        multiply(2)
+        product_b(5)
+        multiply(3)
+        product_b(6)
+        turn_h(1)
+        multiply(4)
+        product_b(7)
+        multiply(5)
+        turn_h(2)
+        keep_clock_up(5)
+        multiply(6)
+        turn_h(3)
+        multiply(7)
+        turn_h(4)
+        keep_clock_up(7)
+        for c0, count in H_QUANT:
+            quantize_h(c0, count)
+
+        def second_layer(nt, s0, s1, bank, copy):
+            for expert in range(s0 // C, (s1 - 1) // C + 1):
+                lo, hi = max(s0, expert * C), min(s1, (expert + 1) * C)
                 nc.tensor.matmul_mx(
                     bank[:, lo - s0 : hi - s0],
-                    lhsT=w_codes["w2"][:, e, 2 * P * nt : 2 * P * (nt + 1)].bitcast(FP4X4),
-                    lhsT_scale=w_scales["w2"][:, e, P * nt : P * (nt + 1)],
+                    lhsT=w_codes["w2"][:, expert, 2 * P * nt : 2 * P * (nt + 1)].bitcast(FP4X4),
+                    lhsT_scale=w_scales["w2"][:, expert, P * nt : P * (nt + 1)],
                     rhs=h_codes[:, lo:hi].bitcast(FP8X4),
                     rhs_scale=h_scales[:, lo:hi],
                     start=True,
                     stop=True,
                 )
-                lo = hi
             copy(y[nt][:, s0:s1], bank[:, 0 : s1 - s0])
 
-        gather_x(0, 0, 0, CHUNK)
-        gather_x(0, 0, CHUNK)
-        for t in range(1, PACK):
-            gather_x(0, t)
-        for c in (0, 1, 2):
-            round_x(c)
-        gather_x(1, 0)
-        quantize_x(0)
-        sigmoid(0)
-        gather_x(1, 1)
-        for c in (1, 2):
-            quantize_x(c)
-            sigmoid(c)
-        gather_x(1, 2)
-        gather_x(1, 3)
-        for c in (0, 1):
-            linear(c)
-            hidden(c)
-        first_layer(0, "w3", b_bank[0])
-        linear(2)
-        for c in (3, 4, 5):
-            round_x(c)
-        gather_x(2, 0)
-        gather_x(2, 1)
-        quantize_x(3)
-        for t in (2, 3):
-            quantize_x(2 + t)
-            gather_x(2, t)
-        turn_h(0)
-        first_layer(1, "w3", b_bank[1])
-        for c in (3, 4):
-            sigmoid(c)
-            linear(c)
-        for c in (6, 7):
-            round_x(c)
-            quantize_x(c)
-        for c in (5, 6, 7):
-            sigmoid(c)
-        for c in (2, 3, 4):
-            hidden(c)
-            linear(c + 3)
-        turn_h(1)
-        hidden(5)
-        turn_h(2)
-        first_layer(5, "w3", b_bank[5])
-        hidden(6)
-        turn_h(3)
-        hidden(7)
-        turn_h(4)
-        first_layer(7, "w3", b_bank[7])
-        for c0, count in ((0, 4), (4, 2), (6, 1), (7, 1)):
-            quantize_h(c0, count)
-
         half = S // 2
-        second_layer(0, 0, half, banks[1])
-        second_layer(0, half, S - CHUNK, banks[4], nc.vector.tensor_copy)
-        second_layer(0, S - CHUNK, S, banks[3])
-        for nt in range(1, N // P):
-            second_layer(nt, half, S, banks[7])
-            second_layer(nt, 0, half, banks[3])
+        last_chunk_bank = banks[B_BANKS[5]]
+        second_layer(0, 0, half, banks[A_BANKS[7]], nc.scalar.copy)
+        second_layer(0, half, S - CHUNK, banks[B_BANKS[6]], nc.vector.tensor_copy)
+        second_layer(0, S - CHUNK, S, last_chunk_bank, nc.scalar.copy)
+        for nt in range(1, Y_TILES):
+            second_layer(nt, half, S, banks[TURN_BANKS[3]], nc.scalar.copy)
+            second_layer(nt, 0, half, last_chunk_bank, nc.scalar.copy)
 
-        first = [tile(f"first{nt}", T, F32) for nt in range(N // P)]
-        second = [tile(f"second{nt}", T, F32) for nt in range(N // P - 1)]
-        total = [tile(f"total{nt}", T, F32) for nt in range(N // P)]
+        first = [tile(f"first{nt}", T, F32) for nt in range(Y_TILES)]
+        second = [tile(f"second{nt}", T, F32) for nt in range(Y_TILES - 1)]
+        total = [tile(f"total{nt}", T, F32) for nt in range(Y_TILES)]
 
         def picked(nt, pos_sb, t0, t1):
             return y[nt][:].indirect(pos_sb[:, t0 // STRIPE : t1 // STRIPE])
 
-        for nt in range(N // P - 1):
+        def store(nt, t0, t1):
+            nc.sync.dma_start(out[nt * P : (nt + 1) * P, t0:t1], total[nt][:, t0:t1])
+
+        last = Y_TILES - 1
+        for nt in range(last):
             nc.vector.tensor_copy(first[nt][:], picked(nt, pos1_sb, 0, T))
-            width = T // 2 if nt == N // P - 2 else T
+            width = T // 2 if nt == last - 1 else T
             for t0 in range(0, T, width):
                 t1 = t0 + width
                 nc.vector.tensor_copy(second[nt][:, t0:t1], picked(nt, pos2_sb, t0, t1))
                 nc.gpsimd.tensor_tensor(total[nt][:, t0:t1], first[nt][:, t0:t1], second[nt][:, t0:t1], ADD)
-                nc.sync.dma_start(out[nt * P : (nt + 1) * P, t0:t1], total[nt][:, t0:t1])
-        nt = N // P - 1
-        pieces = [(sum(LAST_PIECES[:j]), sum(LAST_PIECES[: j + 1])) for j in range(len(LAST_PIECES))]
-        for t0, t1 in pieces:
-            nc.vector.tensor_copy(first[nt][:, t0:t1], picked(nt, pos1_sb, t0, t1))
-        for t0, t1 in pieces:
-            nc.vector.tensor_tensor(total[nt][:, t0:t1], picked(nt, pos2_sb, t0, t1), first[nt][:, t0:t1], ADD)
-            nc.sync.dma_start(out[nt * P : (nt + 1) * P, t0:t1], total[nt][:, t0:t1])
+                store(nt, t0, t1)
+        for t0, t1 in LAST_PIECES:
+            nc.vector.tensor_copy(first[last][:, t0:t1], picked(last, pos1_sb, t0, t1))
+        for t0, t1 in LAST_PIECES:
+            nc.vector.tensor_tensor(total[last][:, t0:t1], picked(last, pos2_sb, t0, t1), first[last][:, t0:t1], ADD)
+            store(last, t0, t1)

@@ -45,7 +45,6 @@ H_QUANT = ((0, 4), (4, 2), (6, 1), (7, 1))
 A_BANKS = (0, 1, 2, 4, 1, 2, 0, 1)
 B_BANKS = (3, 0, 3, 4, 5, 3, 4, 5)
 TURN_BANKS = (6, 2, 6, 7, 0)
-LAST_PIECES = ((0, 3 * T // 4), (3 * T // 4, T))
 
 
 def tile_moe_pre_glu_sigmoid_kernel(
@@ -282,8 +281,9 @@ def tile_moe_pre_glu_sigmoid_kernel(
             second_layer(nt, 0, half, last_chunk_bank, nc.scalar.copy)
 
         first = [tile(f"first{nt}", T, F32) for nt in range(Y_TILES)]
-        second = [tile(f"second{nt}", T, F32) for nt in range(Y_TILES - 1)]
-        total = [tile(f"total{nt}", T, F32) for nt in range(Y_TILES)]
+        second = [tile(f"second{nt}", T, F32) for nt in range(2)]
+        sums = tile("sums", 2 * T, F32)
+        total = [sums[:, T // 2 : T // 2 + T], tile("total1", T, F32)[:], sums[:, 0:T], sums[:, T : 2 * T]]
 
         def picked(nt, pos_sb, t0, t1):
             return y[nt][:].indirect(pos_sb[:, t0 // STRIPE : t1 // STRIPE])
@@ -291,17 +291,13 @@ def tile_moe_pre_glu_sigmoid_kernel(
         def store(nt, t0, t1):
             nc.sync.dma_start(out[nt * P : (nt + 1) * P, t0:t1], total[nt][:, t0:t1])
 
-        last = Y_TILES - 1
-        for nt in range(last):
+        for nt in range(2):
             nc.vector.tensor_copy(first[nt][:], picked(nt, pos1_sb, 0, T))
-            width = T // 2 if nt == last - 1 else T
-            for t0 in range(0, T, width):
-                t1 = t0 + width
-                nc.vector.tensor_copy(second[nt][:, t0:t1], picked(nt, pos2_sb, t0, t1))
-                nc.gpsimd.tensor_tensor(total[nt][:, t0:t1], first[nt][:, t0:t1], second[nt][:, t0:t1], ADD)
-                store(nt, t0, t1)
-        for t0, t1 in LAST_PIECES:
-            nc.vector.tensor_copy(first[last][:, t0:t1], picked(last, pos1_sb, t0, t1))
-        for t0, t1 in LAST_PIECES:
-            nc.vector.tensor_tensor(total[last][:, t0:t1], picked(last, pos2_sb, t0, t1), first[last][:, t0:t1], ADD)
-            store(last, t0, t1)
+            nc.vector.tensor_copy(second[nt][:], picked(nt, pos2_sb, 0, T))
+            nc.gpsimd.tensor_tensor(total[nt], first[nt][:], second[nt][:], ADD)
+            store(nt, 0, T)
+        for nt in (2, 3):
+            nc.vector.tensor_copy(first[nt][:], picked(nt, pos1_sb, 0, T))
+        for nt, t0, t1 in ((2, 0, T), (3, T // 4, T), (3, 0, T // 4)):
+            nc.vector.tensor_tensor(total[nt][:, t0:t1], picked(nt, pos2_sb, t0, t1), first[nt][:, t0:t1], ADD)
+            store(nt, t0, t1)

@@ -34,17 +34,17 @@ Y_TILES = N // P
 
 GROUPS = (3 * CHUNK, 3 * CHUNK, 2 * CHUNK)
 
-GROUP2_AT, GROUP2_STEP = WORDS, GROUPS[2]
-GROUP1_AT, GROUP1_STEP = GROUP2_AT + 2 * GROUP2_STEP, GROUPS[1] + CHUNK
-GROUP0_AT, GROUP0_STEP = GROUP1_AT + GROUP1_STEP + GROUPS[1] - CHUNK, GROUPS[0]
+GROUP2_AT, GROUP2_STEP = 0, 8 * CHUNK
+GROUP1_AT, GROUP1_STEP = CHUNK, 4 * CHUNK
+GROUP0_AT, GROUP0_STEP = 7 * CHUNK, GROUPS[0]
 PHASES_AT = ((GROUP0_AT, GROUP0_STEP), (GROUP1_AT, GROUP1_STEP), (GROUP2_AT, GROUP2_STEP))
-STAGE_WIDTH = GROUP0_AT + PACK * GROUP0_STEP
+STAGE_WIDTH = PACK * GROUP2_STEP
 
-TURNS = ((0, 2), (2, 2), (4, 2), (6, 1), (7, 1))
+TURNS = ((0, 1), (2, 3), (4, 5), (6,), (7,))
 H_QUANT = ((0, 4), (4, 2), (6, 1), (7, 1))
-A_BANKS = (0, 1, 2, 4, 1, 2, 0, 1)
-B_BANKS = (3, 0, 3, 4, 5, 3, 4, 5)
-TURN_BANKS = (6, 2, 6, 7, 0)
+A_BANKS = (0, 1, 2, 0, 1, 2, 0, 1)
+B_BANKS = (3, 4, 5, 6, 7, 3, 5, 2)
+TURN_BANKS = (4, 6, 4, 7, 0)
 
 
 def tile_moe_pre_glu_sigmoid_kernel(
@@ -58,8 +58,8 @@ def tile_moe_pre_glu_sigmoid_kernel(
         keep = ctx.enter_context(tc.tile_pool(name="keep", bufs=1))
         psum = ctx.enter_context(tc.psum_pool(name="psum", bufs=1))
 
-        def tile(name, width, dtype):
-            return keep.tile([P, width], dtype, name=name, align_bytes=MX_ALIGN)
+        def tile(name, width, dtype, tag=None):
+            return keep.tile([P, width], dtype, name=name, tag=tag or name, align_bytes=MX_ALIGN)
 
         offs_sb = keep.tile([P, S // STRIPE], U16, name="offs_sb")
         pos1_sb = keep.tile([P, T // STRIPE], U16, name="pos1_sb")
@@ -71,8 +71,12 @@ def tile_moe_pre_glu_sigmoid_kernel(
         w_codes = {m: keep.tile([P, E, 2 * H], U8, name=f"{m}_codes", align_bytes=MX_ALIGN) for m in weights}
         w_scales = {m: keep.tile([P, E, H], U8, name=f"{m}_scale_bytes", align_bytes=MX_ALIGN) for m in weights}
         identity = tile("identity", P, F32)
-        x_codes = [tile(f"x_codes{c}", CHUNK, U32) for c in range(CHUNKS)]
-        x_scales = [tile(f"x_scales{c}", CHUNK, U8) for c in range(CHUNKS)]
+        x_codes = [tile(f"x_codes{c}", CHUNK, U32)[:] for c in range(6)]
+        x_scales = [tile(f"x_scales{c}", CHUNK, U8)[:] for c in range(6)]
+        last_codes = tile("last_codes", GROUPS[2], U32)
+        last_scales = tile("last_scales", GROUPS[2], U8)
+        x_codes = x_codes + [last_codes[:, 0:CHUNK], last_codes[:, CHUNK:]]
+        x_scales = x_scales + [last_scales[:, 0:CHUNK], last_scales[:, CHUNK:]]
         h_turned = tile("h_turned", S * PACK, BF16)
         h_codes = tile("h_codes", S, U32)
         h_scales = tile("h_scales", S, U8)
@@ -87,16 +91,11 @@ def tile_moe_pre_glu_sigmoid_kernel(
             at, step = PHASES_AT[g]
             return stage[:, at + t * step + lo : at + t * step + hi]
 
-        x_bf16 = {c: tile(f"x_bf16_{c}", CHUNK * PACK, BF16)[:] for c in (0, 1, 2, 6, 7)}
-        x_bf16[3] = staged(2, 0, -WORDS, 0).bitcast(BF16)
-        sig = {c: tile(f"sig{c}", H, F32)[:] for c in range(1, CHUNKS)}
-        sig[0] = staged(2, 0, -CHUNK, H - CHUNK)
-        for c in (4, 5):
-            x_bf16[c] = sig[1][:, (c - 4) * WORDS : (c - 3) * WORDS].bitcast(BF16)
-        h_rows = {c: tile(f"h_rows{c}", WORDS, F32)[:] for c in (0, 1, 5, 6, 7)}
-        h_rows[2] = staged(1, 1, CHUNK, CHUNK + WORDS)
-        h_rows[3] = staged(1, 3, CHUNK, CHUNK + WORDS)
-        h_rows[4] = staged(2, 3, CHUNK, CHUNK + WORDS)
+        x_bf16 = {c: tile(f"x_bf16_{c}", CHUNK * PACK, BF16)[:] for c in (0, 1)}
+        x_bf16[2] = staged(2, 3, 0, WORDS).bitcast(BF16)
+        sig = {c: tile(f"sig{c}", H, F32)[:] for c in range(CHUNKS)}
+        h_rows = {c: tile(f"h_rows{c}", WORDS, F32)[:] for c in (3, 4, 5, 6, 7)}
+        h_rows[2] = staged(2, 0, 0, WORDS)
 
         warm_in = keep.tile([P, 8], F32, name="warm_in")
         warm_out = keep.tile([P, 8], F32, name="warm_out")
@@ -124,9 +123,8 @@ def tile_moe_pre_glu_sigmoid_kernel(
             nc.sync.dma_start(x_phase[t][:], x_rows[t])
         nc.scalar.activation(warm_out[:], warm_in[:], SIGMOID)
         nc.sync.dma_start(gate_rest[:], gate[0:P, GROUPS[0] : S])
-        for m in ("w3", "w1"):
+        for m in ("w1", "w3"):
             load_codes(m, 0, E // 2)
-        for m in ("w3", "w1"):
             load_scales(m)
         for m in ("w1", "w3"):
             load_codes(m, E // 2, E)
@@ -152,7 +150,7 @@ def tile_moe_pre_glu_sigmoid_kernel(
             )
 
         def quantize_x(c):
-            nc.vector.quantize_mx(x_codes[c][:].bitcast(FP8X4), x_scales[c][:], x_bf16[c])
+            nc.vector.quantize_mx(x_codes[c].bitcast(FP8X4), x_scales[c], x_bf16[c])
 
         def pairs_of_bank(bank):
             return bank[:].rearrange("s (q u e) -> s u q e", u=2, e=2)
@@ -164,16 +162,18 @@ def tile_moe_pre_glu_sigmoid_kernel(
             expert = c * CHUNK // C
             nc.tensor.matmul_mx(
                 bank[:],
-                lhsT=x_codes[c][:].bitcast(FP8X4),
-                lhsT_scale=x_scales[c][:],
+                lhsT=x_codes[c].bitcast(FP8X4),
+                lhsT_scale=x_scales[c],
                 rhs=w_codes[m][:, expert, :].bitcast(FP4X4),
                 rhs_scale=w_scales[m][:, expert, :],
                 start=True,
                 stop=True,
             )
 
-        def sigmoid_of_a(c):
+        def product_a(c):
             first_layer(c, "w1", banks[A_BANKS[c]])
+
+        def sigmoid(c):
             nc.scalar.activation(in_pair_order(sig[c]), pairs_of_bank(banks[A_BANKS[c]]), SIGMOID)
 
         def product_b(c):
@@ -184,17 +184,18 @@ def tile_moe_pre_glu_sigmoid_kernel(
                 in_pair_order(h_rows[c].bitcast(BF16)), pairs_of_bank(banks[B_BANKS[c]]), in_pair_order(sig[c]), MULT
             )
 
-        def keep_clock_up(c):
-            product_b(c)
+        def keep_clock_up(product, c):
+            product(c)
 
-        def turn_h(turn):
-            c0, count = TURNS[turn]
-            bank = banks[TURN_BANKS[turn]][:, 0 : 2 * CHUNK * count].rearrange("q (c u s) -> q c u s", u=2, s=CHUNK)
-            for c in range(count):
+        def turn_h(turn, copy=nc.scalar.copy):
+            chunks = TURNS[turn]
+            bank = banks[TURN_BANKS[turn]][:, 0 : 2 * CHUNK * len(chunks)].rearrange("q (c u s) -> q c u s", u=2, s=CHUNK)
+            for j, c in enumerate(chunks):
                 for u in range(2):
-                    nc.tensor.transpose(bank[:, c, u, :], h_rows[c0 + c][:, u * P : (u + 1) * P], identity[:])
-            dst = h_turned[:, c0 * CHUNK * PACK : (c0 + count) * CHUNK * PACK].bitcast(F32)
-            nc.scalar.copy(dst.rearrange("q (c s u) -> q c s u", u=2, s=CHUNK), bank.rearrange("q c u s -> q c s u"))
+                    nc.tensor.transpose(bank[:, j, u, :], h_rows[c][:, u * P : (u + 1) * P], identity[:])
+            dst = h_turned[:].bitcast(F32).rearrange("q (c s u) -> q c s u", u=2, s=CHUNK)
+            step = max(chunks[-1] - chunks[0], 1)
+            copy(dst[:, chunks[0] : chunks[-1] + 1 : step], bank.rearrange("q c u s -> q c s u"))
 
         def quantize_h(c0, count):
             lo, hi = c0 * CHUNK, (c0 + count) * CHUNK
@@ -208,52 +209,64 @@ def tile_moe_pre_glu_sigmoid_kernel(
             round_x(c)
         gather_phase(1, 0)
         quantize_x(0)
-        sigmoid_of_a(0)
+        product_a(0)
+        sigmoid(0)
         gather_phase(1, 1)
         for c in (1, 2):
             quantize_x(c)
-            sigmoid_of_a(c)
+            product_a(c)
+            sigmoid(c)
+        for c in (0, 1, 2):
+            product_b(c)
         gather_phase(1, 2)
         gather_phase(1, 3)
-        for c in (0, 1):
-            product_b(c)
-            multiply(c)
-        keep_clock_up(0)
-        product_b(2)
-        for c in (3, 4, 5):
-            round_x(c)
-        gather_phase(2, 0)
-        gather_phase(2, 1)
-        quantize_x(3)
-        quantize_x(4)
         gather_phase(2, 2)
-        quantize_x(5)
         gather_phase(2, 3)
-        turn_h(0)
-        keep_clock_up(1)
-        for c in (3, 4):
-            sigmoid_of_a(c)
-            product_b(c)
-        for c in (6, 7):
+        mid_rounded = tile("mid_rounded", 5 * WORDS, F32, tag="x_codes0")
+        for c in (3, 4, 5):
+            x_bf16[c] = mid_rounded[:, (c - 3) * WORDS : (c - 2) * WORDS].bitcast(BF16)
             round_x(c)
-            quantize_x(c)
-        for c in (5, 6, 7):
-            sigmoid_of_a(c)
-        multiply(2)
+        h_rows[0] = mid_rounded[:, WORDS + CHUNK : 2 * WORDS + CHUNK]
+        h_rows[1] = mid_rounded[:, 2 * WORDS + CHUNK : 3 * WORDS + CHUNK]
+        quantize_x(3)
+        gather_phase(2, 0)
+        quantize_x(4)
+        quantize_x(5)
+        gather_phase(2, 1)
+        product_a(3)
+        sigmoid(3)
+        last_rounded = tile("last_rounded", GROUPS[2] * PACK, BF16)
+        for c in (6, 7):
+            x_bf16[c] = last_rounded[:, (c - 6) * CHUNK * PACK : (c - 5) * CHUNK * PACK]
+            round_x(c)
+        product_a(4)
+        product_a(5)
+        product_b(3)
+        product_b(4)
+        multiply(0)
         product_b(5)
-        multiply(3)
+        multiply(1)
+        nc.vector.quantize_mx(last_codes[:].bitcast(FP8X4), last_scales[:], last_rounded[:])
+        sigmoid(4)
+        product_a(6)
+        product_a(7)
+        for c in (5, 6, 7):
+            sigmoid(c)
+        turn_h(0)
+        multiply(2)
         product_b(6)
+        product_b(7)
+        multiply(3)
         turn_h(1)
         multiply(4)
-        product_b(7)
         multiply(5)
         turn_h(2)
-        keep_clock_up(5)
+        keep_clock_up(product_b, 5)
         multiply(6)
         turn_h(3)
         multiply(7)
         turn_h(4)
-        keep_clock_up(7)
+        keep_clock_up(product_b, 7)
         for c0, count in H_QUANT:
             quantize_h(c0, count)
 
@@ -272,12 +285,12 @@ def tile_moe_pre_glu_sigmoid_kernel(
             copy(y[nt][:, s0:s1], bank[:, 0 : s1 - s0])
 
         half = S // 2
-        last_chunk_bank = banks[B_BANKS[5]]
-        second_layer(0, 0, half, banks[A_BANKS[7]], nc.scalar.copy)
-        second_layer(0, half, S - CHUNK, banks[B_BANKS[6]], nc.vector.tensor_copy)
+        last_chunk_bank = banks[3]
+        second_layer(0, 0, half, banks[1], nc.scalar.copy)
+        second_layer(0, half, S - CHUNK, banks[6], nc.vector.tensor_copy)
         second_layer(0, S - CHUNK, S, last_chunk_bank, nc.scalar.copy)
         for nt in range(1, Y_TILES):
-            second_layer(nt, half, S, banks[TURN_BANKS[3]], nc.scalar.copy)
+            second_layer(nt, half, S, banks[5], nc.scalar.copy)
             second_layer(nt, 0, half, last_chunk_bank, nc.scalar.copy)
 
         first = [tile(f"first{nt}", T, F32) for nt in range(Y_TILES)]

@@ -34,7 +34,7 @@ Y_TILES = N // P
 
 GROUPS = (3 * CHUNK, 3 * CHUNK, 2 * CHUNK)
 
-GROUP2_AT, GROUP2_STEP = 0, 8 * CHUNK
+GROUP2_AT, GROUP2_STEP = 0, 9 * CHUNK + 32
 GROUP1_AT, GROUP1_STEP = CHUNK, 4 * CHUNK
 GROUP0_AT, GROUP0_STEP = 7 * CHUNK, GROUPS[0]
 PHASES_AT = ((GROUP0_AT, GROUP0_STEP), (GROUP1_AT, GROUP1_STEP), (GROUP2_AT, GROUP2_STEP))
@@ -42,9 +42,9 @@ STAGE_WIDTH = PACK * GROUP2_STEP
 
 TURNS = ((0, 1), (2, 3), (4, 5), (6,), (7,))
 H_QUANT = ((0, 4), (4, 2), (6, 1), (7, 1))
-A_BANKS = (0, 1, 2, 0, 1, 2, 0, 1)
+A_BANKS = (0, 1, 2, 0, 1, 2, 0, 4)
 B_BANKS = (3, 4, 5, 6, 7, 3, 5, 2)
-TURN_BANKS = (4, 6, 4, 7, 0)
+TURN_BANKS = (1, 6, 1, 7, 0)
 
 
 def tile_moe_pre_glu_sigmoid_kernel(
@@ -71,12 +71,8 @@ def tile_moe_pre_glu_sigmoid_kernel(
         w_codes = {m: keep.tile([P, E, 2 * H], U8, name=f"{m}_codes", align_bytes=MX_ALIGN) for m in weights}
         w_scales = {m: keep.tile([P, E, H], U8, name=f"{m}_scale_bytes", align_bytes=MX_ALIGN) for m in weights}
         identity = tile("identity", P, F32)
-        x_codes = [tile(f"x_codes{c}", CHUNK, U32)[:] for c in range(6)]
-        x_scales = [tile(f"x_scales{c}", CHUNK, U8)[:] for c in range(6)]
-        last_codes = tile("last_codes", GROUPS[2], U32)
-        last_scales = tile("last_scales", GROUPS[2], U8)
-        x_codes = x_codes + [last_codes[:, 0:CHUNK], last_codes[:, CHUNK:]]
-        x_scales = x_scales + [last_scales[:, 0:CHUNK], last_scales[:, CHUNK:]]
+        x_codes = [tile(f"x_codes{c}", CHUNK, U32)[:] for c in range(CHUNKS)]
+        x_scales = [tile(f"x_scales{c}", CHUNK, U8)[:] for c in range(CHUNKS)]
         h_turned = tile("h_turned", S * PACK, BF16)
         h_codes = tile("h_codes", S, U32)
         h_scales = tile("h_scales", S, U8)
@@ -94,8 +90,10 @@ def tile_moe_pre_glu_sigmoid_kernel(
         x_bf16 = {c: tile(f"x_bf16_{c}", CHUNK * PACK, BF16)[:] for c in (0, 1)}
         x_bf16[2] = staged(2, 3, 0, WORDS).bitcast(BF16)
         sig = {c: tile(f"sig{c}", H, F32)[:] for c in range(CHUNKS)}
-        h_rows = {c: tile(f"h_rows{c}", WORDS, F32)[:] for c in (3, 4, 5, 6, 7)}
-        h_rows[2] = staged(2, 0, 0, WORDS)
+        h_rows = {c: tile(f"h_rows{c}", WORDS, F32)[:] for c in (5, 6, 7)}
+        h_rows[3] = staged(2, 0, 0, WORDS)
+        h_rows[2] = gate_of(2)
+        h_rows[4] = staged(2, 1, 0, WORDS)
 
         warm_in = keep.tile([P, 8], F32, name="warm_in")
         warm_out = keep.tile([P, 8], F32, name="warm_out")
@@ -125,6 +123,7 @@ def tile_moe_pre_glu_sigmoid_kernel(
         nc.sync.dma_start(gate_rest[:], gate[0:P, GROUPS[0] : S])
         for m in ("w1", "w3"):
             load_codes(m, 0, E // 2)
+        for m in ("w1", "w3"):
             load_scales(m)
         for m in ("w1", "w3"):
             load_codes(m, E // 2, E)
@@ -239,21 +238,22 @@ def tile_moe_pre_glu_sigmoid_kernel(
         for c in (6, 7):
             x_bf16[c] = last_rounded[:, (c - 6) * CHUNK * PACK : (c - 5) * CHUNK * PACK]
             round_x(c)
+        product_b(3)
         product_a(4)
         product_a(5)
-        product_b(3)
         product_b(4)
         multiply(0)
         product_b(5)
         multiply(1)
-        nc.vector.quantize_mx(last_codes[:].bitcast(FP8X4), last_scales[:], last_rounded[:])
-        sigmoid(4)
+        quantize_x(6)
         product_a(6)
-        product_a(7)
-        for c in (5, 6, 7):
+        multiply(2)
+        quantize_x(7)
+        for c in (4, 5, 6):
             sigmoid(c)
         turn_h(0)
-        multiply(2)
+        product_a(7)
+        sigmoid(7)
         product_b(6)
         product_b(7)
         multiply(3)
@@ -286,11 +286,11 @@ def tile_moe_pre_glu_sigmoid_kernel(
 
         half = S // 2
         last_chunk_bank = banks[3]
-        second_layer(0, 0, half, banks[1], nc.scalar.copy)
+        second_layer(0, 0, half, banks[4], nc.scalar.copy)
         second_layer(0, half, S - CHUNK, banks[6], nc.vector.tensor_copy)
         second_layer(0, S - CHUNK, S, last_chunk_bank, nc.scalar.copy)
         for nt in range(1, Y_TILES):
-            second_layer(nt, half, S, banks[5], nc.scalar.copy)
+            second_layer(nt, half, S, banks[6], nc.scalar.copy)
             second_layer(nt, 0, half, last_chunk_bank, nc.scalar.copy)
 
         first = [tile(f"first{nt}", T, F32) for nt in range(Y_TILES)]

@@ -41,7 +41,7 @@ PHASES_AT = ((GROUP0_AT, GROUP0_STEP), (GROUP1_AT, GROUP1_STEP), (GROUP2_AT, GRO
 STAGE_WIDTH = PACK * GROUP2_STEP
 
 TURNS = ((0, 1), (2, 3), (4, 5), (6,), (7,))
-H_QUANT = ((0, 4), (4, 2), (6, 1), (7, 1))
+H_QUANT = ((0, 2), (2, 2), (4, 2), (6, 1), (7, 1))
 A_BANKS = (0, 1, 2, 0, 1, 2, 0, 4)
 B_BANKS = (3, 4, 5, 6, 7, 3, 5, 2)
 TURN_BANKS = (1, 6, 1, 7, 0)
@@ -74,7 +74,7 @@ def tile_moe_pre_glu_sigmoid_kernel(
         x_codes = [tile(f"x_codes{c}", CHUNK, U32)[:] for c in range(CHUNKS)]
         x_scales = [tile(f"x_scales{c}", CHUNK, U8)[:] for c in range(CHUNKS)]
         h_turned = tile("h_turned", S * PACK, BF16)
-        h_codes = tile("h_codes", S, U32)
+        h_codes = tile("h_codes", S - C, U32)
         h_scales = tile("h_scales", S, U8)
         y = [tile(f"y{nt}", S, F32) for nt in range(Y_TILES)]
         banks = [psum.tile([P, BANK], F32, name=f"bank{j}") for j in range(BANKS)]
@@ -91,7 +91,6 @@ def tile_moe_pre_glu_sigmoid_kernel(
         x_bf16[2] = staged(2, 3, 0, WORDS).bitcast(BF16)
         sig = {c: tile(f"sig{c}", H, F32)[:] for c in range(CHUNKS)}
         h_rows = {c: tile(f"h_rows{c}", WORDS, F32)[:] for c in (5, 6, 7)}
-        h_rows[3] = staged(2, 0, 0, WORDS)
         h_rows[2] = gate_of(2)
         h_rows[4] = staged(2, 1, 0, WORDS)
 
@@ -196,9 +195,12 @@ def tile_moe_pre_glu_sigmoid_kernel(
             step = max(chunks[-1] - chunks[0], 1)
             copy(dst[:, chunks[0] : chunks[-1] + 1 : step], bank.rearrange("q c u s -> q c s u"))
 
+        def codes_of_h(lo, hi):
+            return first_h_codes[:, lo:hi] if hi <= C else h_codes[:, lo - C : hi - C]
+
         def quantize_h(c0, count):
             lo, hi = c0 * CHUNK, (c0 + count) * CHUNK
-            nc.vector.quantize_mx(h_codes[:, lo:hi].bitcast(FP8X4), h_scales[:, lo:hi], h_turned[:, lo * PACK : hi * PACK])
+            nc.vector.quantize_mx(codes_of_h(lo, hi).bitcast(FP8X4), h_scales[:, lo:hi], h_turned[:, lo * PACK : hi * PACK])
 
         gather_x(0, 0, 0, CHUNK)
         gather_x(0, 0, CHUNK, GROUPS[0])
@@ -223,42 +225,47 @@ def tile_moe_pre_glu_sigmoid_kernel(
         gather_phase(2, 3)
         mid_rounded = tile("mid_rounded", 5 * WORDS, F32, tag="x_codes0")
         for c in (3, 4, 5):
-            x_bf16[c] = mid_rounded[:, (c - 3) * WORDS : (c - 2) * WORDS].bitcast(BF16)
+            x_bf16[c] = mid_rounded[:, (c - 2) * WORDS : (c - 1) * WORDS].bitcast(BF16)
             round_x(c)
-        h_rows[0] = mid_rounded[:, WORDS + CHUNK : 2 * WORDS + CHUNK]
-        h_rows[1] = mid_rounded[:, 2 * WORDS + CHUNK : 3 * WORDS + CHUNK]
+        h_rows[0] = mid_rounded[:, 2 * WORDS + CHUNK : 3 * WORDS + CHUNK]
+        h_rows[1] = mid_rounded[:, 3 * WORDS + CHUNK : 4 * WORDS + CHUNK]
+        h_rows[3] = tile("h_rows3", WORDS, F32)[:]
         quantize_x(3)
+        b_rows = mid_rounded[:, 0:H]
+        nc.scalar.copy(in_pair_order(b_rows), pairs_of_bank(banks[B_BANKS[2]]))
         gather_phase(2, 0)
         quantize_x(4)
         quantize_x(5)
         gather_phase(2, 1)
         product_a(3)
         sigmoid(3)
+        product_b(3)
+        product_a(4)
+        sigmoid(4)
+        product_a(5)
+        product_b(4)
         last_rounded = tile("last_rounded", GROUPS[2] * PACK, BF16)
         for c in (6, 7):
             x_bf16[c] = last_rounded[:, (c - 6) * CHUNK * PACK : (c - 5) * CHUNK * PACK]
-            round_x(c)
-        product_b(3)
-        product_a(4)
-        product_a(5)
-        product_b(4)
+        round_x(6)
+        round_x(7)
+        nc.gpsimd.tensor_tensor(h_rows[2].bitcast(BF16), b_rows, sig[2], MULT)
         multiply(0)
         product_b(5)
         multiply(1)
+        multiply(3)
         quantize_x(6)
-        product_a(6)
-        multiply(2)
         quantize_x(7)
-        for c in (4, 5, 6):
-            sigmoid(c)
+        sigmoid(5)
         turn_h(0)
+        product_a(6)
         product_a(7)
+        sigmoid(6)
         sigmoid(7)
         product_b(6)
         product_b(7)
-        multiply(3)
-        turn_h(1)
         multiply(4)
+        turn_h(1)
         multiply(5)
         turn_h(2)
         keep_clock_up(product_b, 5)
@@ -267,6 +274,7 @@ def tile_moe_pre_glu_sigmoid_kernel(
         multiply(7)
         turn_h(4)
         keep_clock_up(product_b, 7)
+        first_h_codes = tile("first_h_codes", C, U32, tag="sig6")
         for c0, count in H_QUANT:
             quantize_h(c0, count)
 
@@ -277,7 +285,7 @@ def tile_moe_pre_glu_sigmoid_kernel(
                     bank[:, lo - s0 : hi - s0],
                     lhsT=w_codes["w2"][:, expert, 2 * P * nt : 2 * P * (nt + 1)].bitcast(FP4X4),
                     lhsT_scale=w_scales["w2"][:, expert, P * nt : P * (nt + 1)],
-                    rhs=h_codes[:, lo:hi].bitcast(FP8X4),
+                    rhs=codes_of_h(lo, hi).bitcast(FP8X4),
                     rhs_scale=h_scales[:, lo:hi],
                     start=True,
                     stop=True,
@@ -286,11 +294,13 @@ def tile_moe_pre_glu_sigmoid_kernel(
 
         half = S // 2
         last_chunk_bank = banks[3]
-        second_layer(0, 0, half, banks[4], nc.scalar.copy)
-        second_layer(0, half, S - CHUNK, banks[6], nc.vector.tensor_copy)
+        second_layer(0, 0, C, banks[4], nc.scalar.copy)
+        second_layer(0, C, half, banks[5], nc.scalar.copy)
+        second_layer(0, half, half + C, banks[6], nc.vector.tensor_copy)
+        second_layer(0, half + C, S - CHUNK, banks[1], nc.scalar.copy)
         second_layer(0, S - CHUNK, S, last_chunk_bank, nc.scalar.copy)
         for nt in range(1, Y_TILES):
-            second_layer(nt, half, S, banks[6], nc.scalar.copy)
+            second_layer(nt, half, S, banks[1], nc.scalar.copy)
             second_layer(nt, 0, half, last_chunk_bank, nc.scalar.copy)
 
         first = [tile(f"first{nt}", T, F32) for nt in range(Y_TILES)]

@@ -311,8 +311,8 @@ def tile_moe_pre_glu_sigmoid_kernel(
         def picked(nt, pos_sb, t0, t1):
             return y[nt][:].indirect(pos_sb[:, t0 // STRIPE : t1 // STRIPE])
 
-        def store(nt, t0, t1):
-            nc.sync.dma_start(out[nt * P : (nt + 1) * P, t0:t1], total[nt][:, t0:t1])
+        def store(nt, t0, t1, queue=nc.sync):
+            queue.dma_start(out[nt * P : (nt + 1) * P, t0:t1], total[nt][:, t0:t1])
 
         for nt in range(2):
             nc.vector.tensor_copy(first[nt][:], picked(nt, pos1_sb, 0, T))
@@ -321,6 +321,6 @@ def tile_moe_pre_glu_sigmoid_kernel(
             store(nt, 0, T)
         for nt in (2, 3):
             nc.vector.tensor_copy(first[nt][:], picked(nt, pos1_sb, 0, T))
-        for nt, t0, t1 in ((2, 0, T), (3, T // 4, T), (3, 0, T // 4)):
+        for nt, t0, t1, queue in ((2, 0, T, nc.sync), (3, T // 4, T, nc.sync), (3, 0, T // 4, nc.scalar)):
             nc.vector.tensor_tensor(total[nt][:, t0:t1], picked(nt, pos2_sb, t0, t1), first[nt][:, t0:t1], ADD)
-            store(nt, t0, t1)
+            store(nt, t0, t1, queue)

@@ -19,6 +19,7 @@ FP4X4 = mybir.dt.float4_e2m1fn_x4
 MULT = mybir.AluOpType.mult
 ADD = mybir.AluOpType.add
 SIGMOID = mybir.ActivationFunctionType.Sigmoid
+COPY = mybir.ActivationFunctionType.Copy
 
 P = 128
 PACK = 4
@@ -32,26 +33,20 @@ BANKS = 8
 WORDS = H // 2
 Y_TILES = N // P
 
-GROUPS = (3 * CHUNK, 3 * CHUNK, 2 * CHUNK)
 
-GROUP2_AT, GROUP2_STEP = 0, 9 * CHUNK + 32
-GROUP1_AT, GROUP1_STEP = CHUNK, 4 * CHUNK
-GROUP0_AT, GROUP0_STEP = 7 * CHUNK, GROUPS[0]
-PHASES_AT = ((GROUP0_AT, GROUP0_STEP), (GROUP1_AT, GROUP1_STEP), (GROUP2_AT, GROUP2_STEP))
-STAGE_WIDTH = PACK * GROUP2_STEP
+V_SLOTS = 3 * CHUNK
+S_GROUPS = (2 * CHUNK, 3 * CHUNK)
 
-TURNS = ((0, 1), (2, 3), (4, 5), (6,), (7,))
-H_QUANT = ((0, 2), (2, 2), (4, 2), (6, 1), (7, 1))
-A_BANKS = (0, 1, 2, 0, 1, 2, 0, 4)
-B_BANKS = (3, 4, 5, 6, 7, 3, 5, 2)
-TURN_BANKS = (1, 6, 1, 7, 0)
+TURNS = ((0, 2), (2, 2), (4, 2), (6, 1), (7, 1))
+TURN_BANKS = (6, 7, 6, 7, 6)
 
 
 def tile_moe_pre_glu_sigmoid_kernel(
     tc, xT, w1_words, w1_scales, w3_words, w3_scales, w2_words, w2_scales, gate, offs, pos1, pos2, out
 ):
     nc = tc.nc
-    group_start = [sum(GROUPS[:g]) for g in range(len(GROUPS))]
+    groups = (V_SLOTS,) + S_GROUPS
+    group_start = [sum(groups[:g]) for g in range(len(groups))]
     weights = {"w1": (w1_words, w1_scales), "w3": (w3_words, w3_scales), "w2": (w2_words, w2_scales)}
 
     with ExitStack() as ctx:
@@ -65,34 +60,24 @@ def tile_moe_pre_glu_sigmoid_kernel(
         pos1_sb = keep.tile([P, T // STRIPE], U16, name="pos1_sb")
         pos2_sb = keep.tile([P, T // STRIPE], U16, name="pos2_sb")
         x_phase = [tile(f"x_phase{t}", T, F32) for t in range(PACK)]
-        gate_first = tile("gate_first", GROUPS[0], F32)
-        gate_rest = tile("gate_rest", S - GROUPS[0], F32)
-        stage = tile("stage", STAGE_WIDTH, F32)
+        gate_first = tile("gate_first", V_SLOTS, F32)
+        gate_rest = tile("gate_rest", S - V_SLOTS, F32)
+        stage = [tile(f"stage{g}", PACK * groups[g], F32) for g in range(len(groups))]
         w_codes = {m: keep.tile([P, E, 2 * H], U8, name=f"{m}_codes", align_bytes=MX_ALIGN) for m in weights}
         w_scales = {m: keep.tile([P, E, H], U8, name=f"{m}_scale_bytes", align_bytes=MX_ALIGN) for m in weights}
         identity = tile("identity", P, F32)
+        x_bf16 = [tile(f"x_bf16_{c}", CHUNK * PACK, BF16)[:] for c in range(CHUNKS)]
         x_codes = [tile(f"x_codes{c}", CHUNK, U32)[:] for c in range(CHUNKS)]
         x_scales = [tile(f"x_scales{c}", CHUNK, U8)[:] for c in range(CHUNKS)]
+        sig = [tile(f"sig{c}", H, F32)[:] for c in range(CHUNKS)]
+        h_rows = [tile(f"h_rows{c}", WORDS, F32)[:] for c in range(CHUNKS)]
         h_turned = tile("h_turned", S * PACK, BF16)
-        h_codes = tile("h_codes", S - C, U32)
+        h_codes = tile("h_codes", S, U32)
         h_scales = tile("h_scales", S, U8)
         y = [tile(f"y{nt}", S, F32) for nt in range(Y_TILES)]
+        first = [tile(f"first{nt}", T, F32) for nt in range(Y_TILES)]
+        total = [tile(f"total{nt}", T, F32) for nt in range(Y_TILES)]
         banks = [psum.tile([P, BANK], F32, name=f"bank{j}") for j in range(BANKS)]
-
-        def gate_of(g):
-            s0 = group_start[g] - GROUPS[0]
-            return gate_first[:] if g == 0 else gate_rest[:, s0 : s0 + GROUPS[g]]
-
-        def staged(g, t, lo, hi):
-            at, step = PHASES_AT[g]
-            return stage[:, at + t * step + lo : at + t * step + hi]
-
-        x_bf16 = {c: tile(f"x_bf16_{c}", CHUNK * PACK, BF16)[:] for c in (0, 1)}
-        x_bf16[2] = staged(2, 3, 0, WORDS).bitcast(BF16)
-        sig = {c: tile(f"sig{c}", H, F32)[:] for c in range(CHUNKS)}
-        h_rows = {c: tile(f"h_rows{c}", WORDS, F32)[:] for c in (5, 6, 7)}
-        h_rows[2] = gate_of(2)
-        h_rows[4] = staged(2, 1, 0, WORDS)
 
         warm_in = keep.tile([P, 8], F32, name="warm_in")
         warm_out = keep.tile([P, 8], F32, name="warm_out")
@@ -115,11 +100,11 @@ def tile_moe_pre_glu_sigmoid_kernel(
         nc.sync.dma_start(x_phase[0][:], x_rows[0])
         nc.scalar.dma_start(gate_first[:, 0:CHUNK], gate[0:P, 0:CHUNK])
         nc.sync.dma_start(offs_sb[:], offs)
-        nc.sync.dma_start(gate_first[:, CHUNK : GROUPS[0]], gate[0:P, CHUNK : GROUPS[0]])
+        nc.sync.dma_start(gate_first[:, CHUNK:V_SLOTS], gate[0:P, CHUNK:V_SLOTS])
         for t in range(1, PACK):
             nc.sync.dma_start(x_phase[t][:], x_rows[t])
         nc.scalar.activation(warm_out[:], warm_in[:], SIGMOID)
-        nc.sync.dma_start(gate_rest[:], gate[0:P, GROUPS[0] : S])
+        nc.sync.dma_start(gate_rest[:], gate[0:P, V_SLOTS:S])
         for m in ("w1", "w3"):
             load_codes(m, 0, E // 2)
         for m in ("w1", "w3"):
@@ -131,21 +116,30 @@ def tile_moe_pre_glu_sigmoid_kernel(
         nc.sync.dma_start(pos1_sb[:], pos1)
         nc.sync.dma_start(pos2_sb[:], pos2)
 
-        def gather_x(g, t, lo, hi):
-            entries = offs_sb[:, (group_start[g] + lo) // STRIPE : (group_start[g] + hi) // STRIPE]
-            nc.vector.tensor_tensor(staged(g, t, lo, hi), x_phase[t][:].indirect(entries), gate_of(g)[:, lo:hi], MULT)
+        def picked_x(g, t, lo, hi):
+            return x_phase[t][:].indirect(offs_sb[:, (group_start[g] + lo) // STRIPE : (group_start[g] + hi) // STRIPE])
 
-        def gather_phase(g, t):
-            gather_x(g, t, 0, GROUPS[g])
+        def staged(g, t, lo, hi):
+            return stage[g][:, t * groups[g] + lo : t * groups[g] + hi]
+
+        def gather_gated(t, lo, hi):
+            nc.vector.tensor_tensor(staged(0, t, lo, hi), picked_x(0, t, lo, hi), gate_first[:, lo:hi], MULT)
+
+        def gather_plain(g, t):
+            nc.scalar.activation(staged(g, t, 0, groups[g]), picked_x(g, t, 0, groups[g]), COPY)
 
         def round_x(c):
-            g = max(j for j in range(len(GROUPS)) if group_start[j] <= c * CHUNK)
+            g = max(j for j in range(len(groups)) if group_start[j] <= c * CHUNK)
             s0 = c * CHUNK - group_start[g]
-            phases = staged(g, 0, 0, PACK * PHASES_AT[g][1]).rearrange("p (t s) -> p t s", t=PACK)
-            nc.scalar.copy(
-                x_bf16[c].rearrange("p (s i t) -> p s t i", i=4, t=PACK),
-                phases[:, :, s0 : s0 + CHUNK].rearrange("p t (s i) -> p s t i", i=4),
-            )
+            phases = stage[g][:].rearrange("p (t s) -> p t s", t=PACK)
+            src = phases[:, :, s0 : s0 + CHUNK].rearrange("p t (s i) -> p s t i", i=4)
+            dst = x_bf16[c].rearrange("p (s i t) -> p s t i", i=4, t=PACK)
+            if g == 0:
+                nc.vector.tensor_copy(dst, src)
+            else:
+                lo = c * CHUNK - V_SLOTS
+                weight = gate_rest[:, lo : lo + CHUNK].rearrange("p (s o i) -> p s o i", o=1, i=4)
+                nc.vector.tensor_tensor(dst, src, weight.broadcast_to([P, CHUNK // 4, PACK, 4]), MULT)
 
         def quantize_x(c):
             nc.vector.quantize_mx(x_codes[c].bitcast(FP8X4), x_scales[c], x_bf16[c])
@@ -169,158 +163,134 @@ def tile_moe_pre_glu_sigmoid_kernel(
             )
 
         def product_a(c):
-            first_layer(c, "w1", banks[A_BANKS[c]])
+            first_layer(c, "w1", banks[c % 3])
 
         def sigmoid(c):
-            nc.scalar.activation(in_pair_order(sig[c]), pairs_of_bank(banks[A_BANKS[c]]), SIGMOID)
+            nc.scalar.activation(in_pair_order(sig[c]), pairs_of_bank(banks[c % 3]), SIGMOID)
 
         def product_b(c):
-            first_layer(c, "w3", banks[B_BANKS[c]])
+            first_layer(c, "w3", banks[3 + c % 3])
 
         def multiply(c):
             nc.vector.tensor_tensor(
-                in_pair_order(h_rows[c].bitcast(BF16)), pairs_of_bank(banks[B_BANKS[c]]), in_pair_order(sig[c]), MULT
+                in_pair_order(h_rows[c].bitcast(BF16)), pairs_of_bank(banks[3 + c % 3]), in_pair_order(sig[c]), MULT
             )
 
-        def keep_clock_up(product, c):
-            product(c)
-
-        def turn_h(turn, copy=nc.scalar.copy):
-            chunks = TURNS[turn]
-            bank = banks[TURN_BANKS[turn]][:, 0 : 2 * CHUNK * len(chunks)].rearrange("q (c u s) -> q c u s", u=2, s=CHUNK)
-            for j, c in enumerate(chunks):
+        def turn_h(turn, copy):
+            c0, count = TURNS[turn]
+            bank = banks[TURN_BANKS[turn]][:, 0 : 2 * CHUNK * count].rearrange("q (c u s) -> q c u s", u=2, s=CHUNK)
+            for j in range(count):
                 for u in range(2):
-                    nc.tensor.transpose(bank[:, j, u, :], h_rows[c][:, u * P : (u + 1) * P], identity[:])
+                    nc.tensor.transpose(bank[:, j, u, :], h_rows[c0 + j][:, u * P : (u + 1) * P], identity[:])
             dst = h_turned[:].bitcast(F32).rearrange("q (c s u) -> q c s u", u=2, s=CHUNK)
-            step = max(chunks[-1] - chunks[0], 1)
-            copy(dst[:, chunks[0] : chunks[-1] + 1 : step], bank.rearrange("q c u s -> q c s u"))
+            copy(dst[:, c0 : c0 + count], bank.rearrange("q c u s -> q c s u"))
 
-        def codes_of_h(lo, hi):
-            return first_h_codes[:, lo:hi] if hi <= C else h_codes[:, lo - C : hi - C]
-
-        def quantize_h(c0, count):
+        def quantize_h(turn):
+            c0, count = TURNS[turn]
             lo, hi = c0 * CHUNK, (c0 + count) * CHUNK
-            nc.vector.quantize_mx(codes_of_h(lo, hi).bitcast(FP8X4), h_scales[:, lo:hi], h_turned[:, lo * PACK : hi * PACK])
+            nc.vector.quantize_mx(h_codes[:, lo:hi].bitcast(FP8X4), h_scales[:, lo:hi], h_turned[:, lo * PACK : hi * PACK])
 
-        gather_x(0, 0, 0, CHUNK)
-        gather_x(0, 0, CHUNK, GROUPS[0])
+        def second_layer(pieces, bank, copy):
+            at = 0
+            for nt, s0, s1 in pieces:
+                for lo in range(s0, s1, C):
+                    hi = min(s1, lo + C)
+                    expert = lo // C
+                    nc.tensor.matmul_mx(
+                        bank[:, at + lo - s0 : at + hi - s0],
+                        lhsT=w_codes["w2"][:, expert, 2 * P * nt : 2 * P * (nt + 1)].bitcast(FP4X4),
+                        lhsT_scale=w_scales["w2"][:, expert, P * nt : P * (nt + 1)],
+                        rhs=h_codes[:, lo:hi].bitcast(FP8X4),
+                        rhs_scale=h_scales[:, lo:hi],
+                        start=True,
+                        stop=True,
+                    )
+                at = at + s1 - s0
+            at = 0
+            for nt, s0, s1 in pieces:
+                copy(y[nt][:, s0:s1], bank[:, at : at + s1 - s0])
+                at = at + s1 - s0
+
+        on_s, on_v = nc.scalar.copy, nc.vector.tensor_copy
+
+        gather_gated(0, 0, CHUNK)
+        gather_gated(0, CHUNK, V_SLOTS)
         for t in range(1, PACK):
-            gather_phase(0, t)
-        for c in (0, 1, 2):
-            round_x(c)
-        gather_phase(1, 0)
-        quantize_x(0)
-        product_a(0)
-        sigmoid(0)
-        gather_phase(1, 1)
-        for c in (1, 2):
+            gather_gated(t, 0, V_SLOTS)
+        for t in range(PACK):
+            for g in (1, 2):
+                gather_plain(g, t)
+        round_x(0)
+        round_x(1)
+        for c in range(6):
             quantize_x(c)
             product_a(c)
             sigmoid(c)
-        for c in (0, 1, 2):
-            product_b(c)
-        gather_phase(1, 2)
-        gather_phase(1, 3)
-        gather_phase(2, 2)
-        gather_phase(2, 3)
-        mid_rounded = tile("mid_rounded", 5 * WORDS, F32, tag="x_codes0")
-        for c in (3, 4, 5):
-            x_bf16[c] = mid_rounded[:, (c - 2) * WORDS : (c - 1) * WORDS].bitcast(BF16)
-            round_x(c)
-        h_rows[0] = mid_rounded[:, 2 * WORDS + CHUNK : 3 * WORDS + CHUNK]
-        h_rows[1] = mid_rounded[:, 3 * WORDS + CHUNK : 4 * WORDS + CHUNK]
-        h_rows[3] = tile("h_rows3", WORDS, F32)[:]
-        quantize_x(3)
-        b_rows = mid_rounded[:, 0:H]
-        nc.scalar.copy(in_pair_order(b_rows), pairs_of_bank(banks[B_BANKS[2]]))
-        gather_phase(2, 0)
-        quantize_x(4)
-        quantize_x(5)
-        gather_phase(2, 1)
-        product_a(3)
-        sigmoid(3)
-        product_b(3)
-        product_a(4)
-        sigmoid(4)
-        product_a(5)
+            if c < 3:
+                product_b(c)
+            if c + 2 < 6:
+                round_x(c + 2)
+            if c == 4:
+                multiply(0)
+                product_b(3)
+        multiply(1)
         product_b(4)
-        last_rounded = tile("last_rounded", GROUPS[2] * PACK, BF16)
-        for c in (6, 7):
-            x_bf16[c] = last_rounded[:, (c - 6) * CHUNK * PACK : (c - 5) * CHUNK * PACK]
         round_x(6)
         round_x(7)
-        nc.gpsimd.tensor_tensor(h_rows[2].bitcast(BF16), b_rows, sig[2], MULT)
-        multiply(0)
-        product_b(5)
-        multiply(1)
-        multiply(3)
         quantize_x(6)
-        quantize_x(7)
-        sigmoid(5)
-        turn_h(0)
         product_a(6)
-        product_a(7)
+        turn_h(0, on_s)
         sigmoid(6)
+        multiply(2)
+        product_b(5)
+        quantize_x(7)
+        product_a(7)
         sigmoid(7)
+        quantize_h(0)
+        multiply(3)
         product_b(6)
-        product_b(7)
+        turn_h(1, on_s)
         multiply(4)
-        turn_h(1)
+        product_b(7)
         multiply(5)
-        turn_h(2)
-        keep_clock_up(product_b, 5)
+        turn_h(2, on_s)
+        quantize_h(1)
         multiply(6)
-        turn_h(3)
+        turn_h(3, on_s)
         multiply(7)
-        turn_h(4)
-        keep_clock_up(product_b, 7)
-        first_h_codes = tile("first_h_codes", C, U32, tag="sig6")
-        for c0, count in H_QUANT:
-            quantize_h(c0, count)
-
-        def second_layer(nt, s0, s1, bank, copy):
-            for expert in range(s0 // C, (s1 - 1) // C + 1):
-                lo, hi = max(s0, expert * C), min(s1, (expert + 1) * C)
-                nc.tensor.matmul_mx(
-                    bank[:, lo - s0 : hi - s0],
-                    lhsT=w_codes["w2"][:, expert, 2 * P * nt : 2 * P * (nt + 1)].bitcast(FP4X4),
-                    lhsT_scale=w_scales["w2"][:, expert, P * nt : P * (nt + 1)],
-                    rhs=codes_of_h(lo, hi).bitcast(FP8X4),
-                    rhs_scale=h_scales[:, lo:hi],
-                    start=True,
-                    stop=True,
-                )
-            copy(y[nt][:, s0:s1], bank[:, 0 : s1 - s0])
-
-        half = S // 2
-        last_chunk_bank = banks[3]
-        second_layer(0, 0, C, banks[4], nc.scalar.copy)
-        second_layer(0, C, half, banks[5], nc.scalar.copy)
-        second_layer(0, half, half + C, banks[6], nc.vector.tensor_copy)
-        second_layer(0, half + C, S - CHUNK, banks[1], nc.scalar.copy)
-        second_layer(0, S - CHUNK, S, last_chunk_bank, nc.scalar.copy)
-        for nt in range(1, Y_TILES):
-            second_layer(nt, half, S, banks[1], nc.scalar.copy)
-            second_layer(nt, 0, half, last_chunk_bank, nc.scalar.copy)
-
-        first = [tile(f"first{nt}", T, F32) for nt in range(Y_TILES)]
-        second = [tile(f"second{nt}", T, F32) for nt in range(2)]
-        sums = tile("sums", 2 * T, F32)
-        total = [sums[:, T // 2 : T // 2 + T], tile("total1", T, F32)[:], sums[:, 0:T], sums[:, T : 2 * T]]
+        quantize_h(2)
+        turn_h(4, on_v)
+        quantize_h(3)
+        quantize_h(4)
+        second_layer(((0, 0, C), (1, 0, C)), banks[2], on_s)
+        second_layer(((2, 0, C), (3, 0, C)), banks[0], on_s)
+        second_layer(((0, C, 2 * C), (1, C, 2 * C)), banks[1], on_s)
+        second_layer(((2, C, 2 * C), (3, C, 2 * C)), banks[2], on_s)
+        second_layer(((0, 2 * C, 3 * C), (1, 2 * C, 3 * C)), banks[5], on_v)
+        second_layer(((0, 3 * C, S),), banks[0], on_s)
+        second_layer(((1, 3 * C, S),), banks[1], on_s)
 
         def picked(nt, pos_sb, t0, t1):
             return y[nt][:].indirect(pos_sb[:, t0 // STRIPE : t1 // STRIPE])
 
-        def store(nt, t0, t1, queue=nc.sync):
+        def first_on_s(nt, t0, t1):
+            nc.scalar.activation(first[nt][:, t0:t1], picked(nt, pos1_sb, t0, t1), COPY)
+
+        def add_second(nt, t0, t1, queue=nc.sync):
+            nc.vector.tensor_tensor(total[nt][:, t0:t1], picked(nt, pos2_sb, t0, t1), first[nt][:, t0:t1], ADD)
             queue.dma_start(out[nt * P : (nt + 1) * P, t0:t1], total[nt][:, t0:t1])
 
-        for nt in range(2):
-            nc.vector.tensor_copy(first[nt][:], picked(nt, pos1_sb, 0, T))
-            nc.vector.tensor_copy(second[nt][:], picked(nt, pos2_sb, 0, T))
-            nc.gpsimd.tensor_tensor(total[nt], first[nt][:], second[nt][:], ADD)
-            store(nt, 0, T)
-        for nt in (2, 3):
-            nc.vector.tensor_copy(first[nt][:], picked(nt, pos1_sb, 0, T))
-        for nt, t0, t1, queue in ((2, 0, T, nc.sync), (3, T // 4, T, nc.sync), (3, 0, T // 4, nc.scalar)):
-            nc.vector.tensor_tensor(total[nt][:, t0:t1], picked(nt, pos2_sb, t0, t1), first[nt][:, t0:t1], ADD)
-            store(nt, t0, t1, queue)
+        nc.vector.tensor_copy(first[0][:, 0 : T // 2], picked(0, pos1_sb, 0, T // 2))
+        first_on_s(0, T // 2, T)
+        first_on_s(1, 0, T)
+        second_layer(((3, 2 * C, S),), banks[3], on_s)
+        second_layer(((2, 2 * C, S),), banks[4], on_v)
+        first_on_s(2, 0, T)
+        first_on_s(3, T // 2, T)
+        first_on_s(3, 0, T // 2)
+        add_second(0, 0, T)
+        add_second(1, 0, T)
+        add_second(2, 0, T)
+        add_second(3, T // 2, T)
+        add_second(3, T // 4, T // 2)
+        add_second(3, 0, T // 4, nc.scalar)

@@ -34,11 +34,14 @@ WORDS = H // 2
 Y_TILES = N // P
 
 
-V_SLOTS = 3 * CHUNK
-S_GROUPS = (2 * CHUNK, 3 * CHUNK)
+V_SLOTS = 2 * CHUNK
+S_GROUPS = (3 * CHUNK, 2 * CHUNK, CHUNK)
 
 TURNS = ((0, 2), (2, 2), (4, 2), (6, 1), (7, 1))
-TURN_BANKS = (6, 7, 6, 7, 6)
+ROUNDS = ((0, 1), (1, 1), (2, 2), (4, 1), (5, 2), (7, 1))
+TURN_BANKS = (6, 7, 6, 7, 0)
+A_BANKS = (0, 1, 2, 6, 7, 0, 1, 2)
+B_BANKS = (3, 4, 5, 3, 4, 5, 3, 4)
 
 
 def tile_moe_pre_glu_sigmoid_kernel(
@@ -61,19 +64,26 @@ def tile_moe_pre_glu_sigmoid_kernel(
         pos2_sb = keep.tile([P, T // STRIPE], U16, name="pos2_sb")
         x_phase = [tile(f"x_phase{t}", T, F32) for t in range(PACK)]
         gate_first = tile("gate_first", V_SLOTS, F32)
-        gate_rest = tile("gate_rest", S - V_SLOTS, F32)
-        stage = [tile(f"stage{g}", PACK * groups[g], F32) for g in range(len(groups))]
-        w_codes = {m: keep.tile([P, E, 2 * H], U8, name=f"{m}_codes", align_bytes=MX_ALIGN) for m in weights}
+        gate_mid = tile("gate_mid", groups[1], F32)
+        gate_last = tile("gate_last", groups[2] + groups[3], F32)
+        stage = {g: tile(f"stage{g}", PACK * groups[g], F32)[:] for g in range(2)}
+        w_codes = {
+            (m, e0): keep.tile([P, E // 2, 2 * H], U8, name=f"{m}_codes{e0}", align_bytes=MX_ALIGN)
+            for m in weights
+            for e0 in (0, E // 2)
+        }
         w_scales = {m: keep.tile([P, E, H], U8, name=f"{m}_scale_bytes", align_bytes=MX_ALIGN) for m in weights}
         identity = tile("identity", P, F32)
-        x_bf16 = [tile(f"x_bf16_{c}", CHUNK * PACK, BF16)[:] for c in range(CHUNKS)]
-        x_codes = [tile(f"x_codes{c}", CHUNK, U32)[:] for c in range(CHUNKS)]
-        x_scales = [tile(f"x_scales{c}", CHUNK, U8)[:] for c in range(CHUNKS)]
+        x_bf16 = [tile(f"x_bf16_{c0}", n * CHUNK * PACK, BF16)[:] for c0, n in ROUNDS]
+        run_codes = [tile(f"x_codes{c0}", n * CHUNK, U32)[:] for c0, n in ROUNDS]
+        x_codes = [run_codes[r][:, j * CHUNK : (j + 1) * CHUNK] for r, (c0, n) in enumerate(ROUNDS) for j in range(n)]
+        run_scales = [tile(f"x_scales{c0}", n * CHUNK, U8)[:] for c0, n in ROUNDS]
+        x_scales = [run_scales[r][:, j * CHUNK : (j + 1) * CHUNK] for r, (c0, n) in enumerate(ROUNDS) for j in range(n)]
         sig = [tile(f"sig{c}", H, F32)[:] for c in range(CHUNKS)]
         h_rows = [tile(f"h_rows{c}", WORDS, F32)[:] for c in range(CHUNKS)]
-        h_turned = tile("h_turned", S * PACK, BF16)
-        h_codes = tile("h_codes", S, U32)
-        h_scales = tile("h_scales", S, U8)
+        h_turned = [tile(f"h_turned{j}", count * CHUNK * PACK, BF16) for j, (c0, count) in enumerate(TURNS)]
+        h_codes = {e: tile(f"h_codes{e}", C, U32) for e in (2, 3)}
+        h_scales = [tile(f"h_scales{e}", C, U8) for e in range(E)]
         y = [tile(f"y{nt}", S, F32) for nt in range(Y_TILES)]
         first = [tile(f"first{nt}", T, F32) for nt in range(Y_TILES)]
         total = [tile(f"total{nt}", T, F32) for nt in range(Y_TILES)]
@@ -90,12 +100,13 @@ def tile_moe_pre_glu_sigmoid_kernel(
 
         def load_codes(m, e0, e1):
             src = weights[m][0].rearrange("e s p b -> p (e s) b")
-            nc.sync.dma_start(w_codes[m][:, e0:e1, :].bitcast(I32), src[:, e0:e1, :].bitcast(I32))
+            nc.sync.dma_start(w_codes[m, e0][:].bitcast(I32), src[:, e0:e1, :].bitcast(I32))
 
-        def load_scales(m):
-            src = weights[m][1].rearrange("e s (q r) n -> q r (e s) n", r=4)
+        def load_scales(*names):
             for q in (0, 2, 1, 3):
-                nc.sync.dma_start(w_scales[m][QUAD * q : QUAD * q + 4, :, :].bitcast(I32), src[q].bitcast(I32))
+                for m in names:
+                    src = weights[m][1].rearrange("e s (q r) n -> q r (e s) n", r=4)
+                    nc.sync.dma_start(w_scales[m][QUAD * q : QUAD * q + 4, :, :].bitcast(I32), src[q].bitcast(I32))
 
         nc.sync.dma_start(x_phase[0][:], x_rows[0])
         nc.scalar.dma_start(gate_first[:, 0:CHUNK], gate[0:P, 0:CHUNK])
@@ -104,15 +115,16 @@ def tile_moe_pre_glu_sigmoid_kernel(
         for t in range(1, PACK):
             nc.sync.dma_start(x_phase[t][:], x_rows[t])
         nc.scalar.activation(warm_out[:], warm_in[:], SIGMOID)
-        nc.sync.dma_start(gate_rest[:], gate[0:P, V_SLOTS:S])
-        for m in ("w1", "w3"):
-            load_codes(m, 0, E // 2)
-        for m in ("w1", "w3"):
-            load_scales(m)
-        for m in ("w1", "w3"):
-            load_codes(m, E // 2, E)
+        nc.sync.dma_start(gate_mid[:], gate[0:P, group_start[1] : group_start[2]])
+        load_codes("w1", 0, E // 2)
+        load_scales("w1", "w3")
+        nc.sync.dma_start(gate_last[:], gate[0:P, group_start[2] : S])
+        load_codes("w1", E // 2, E)
+        load_codes("w3", 0, E // 2)
+        load_codes("w3", E // 2, E)
         load_scales("w2")
-        load_codes("w2", 0, E)
+        load_codes("w2", 0, E // 2)
+        load_codes("w2", E // 2, E)
         nc.sync.dma_start(pos1_sb[:], pos1)
         nc.sync.dma_start(pos2_sb[:], pos2)
 
@@ -128,21 +140,24 @@ def tile_moe_pre_glu_sigmoid_kernel(
         def gather_plain(g, t):
             nc.scalar.activation(staged(g, t, 0, groups[g]), picked_x(g, t, 0, groups[g]), COPY)
 
-        def round_x(c):
-            g = max(j for j in range(len(groups)) if group_start[j] <= c * CHUNK)
-            s0 = c * CHUNK - group_start[g]
-            phases = stage[g][:].rearrange("p (t s) -> p t s", t=PACK)
-            src = phases[:, :, s0 : s0 + CHUNK].rearrange("p t (s i) -> p s t i", i=4)
-            dst = x_bf16[c].rearrange("p (s i t) -> p s t i", i=4, t=PACK)
+        def round_x(r):
+            lo, width = ROUNDS[r][0] * CHUNK, ROUNDS[r][1] * CHUNK
+            g = max(j for j in range(len(groups)) if group_start[j] <= lo)
+            s0 = lo - group_start[g]
+            phases = stage[g].rearrange("p (t s) -> p t s", t=PACK)
+            run = 4 if g == 0 else 2
+            src = phases[:, :, s0 : s0 + width].rearrange("p t (s i) -> p s t i", i=run)
+            dst = x_bf16[r].rearrange("p (s i t) -> p s t i", i=run, t=PACK)
             if g == 0:
                 nc.vector.tensor_copy(dst, src)
             else:
-                lo = c * CHUNK - V_SLOTS
-                weight = gate_rest[:, lo : lo + CHUNK].rearrange("p (s o i) -> p s o i", o=1, i=4)
-                nc.vector.tensor_tensor(dst, src, weight.broadcast_to([P, CHUNK // 4, PACK, 4]), MULT)
+                at = lo - group_start[min(g, 2)]
+                row = (gate_mid if g == 1 else gate_last)[:, at : at + width]
+                weight = row.rearrange("p (s o i) -> p s o i", o=1, i=run).broadcast_to([P, width // run, PACK, run])
+                nc.vector.tensor_tensor(dst, src, weight, MULT)
 
-        def quantize_x(c):
-            nc.vector.quantize_mx(x_codes[c].bitcast(FP8X4), x_scales[c], x_bf16[c])
+        def quantize_x(r):
+            nc.vector.quantize_mx(run_codes[r].bitcast(FP8X4), run_scales[r], x_bf16[r])
 
         def pairs_of_bank(bank):
             return bank[:].rearrange("s (q u e) -> s u q e", u=2, e=2)
@@ -156,24 +171,24 @@ def tile_moe_pre_glu_sigmoid_kernel(
                 bank[:],
                 lhsT=x_codes[c].bitcast(FP8X4),
                 lhsT_scale=x_scales[c],
-                rhs=w_codes[m][:, expert, :].bitcast(FP4X4),
+                rhs=w_codes[m, expert // 2 * 2][:, expert % 2, :].bitcast(FP4X4),
                 rhs_scale=w_scales[m][:, expert, :],
                 start=True,
                 stop=True,
             )
 
         def product_a(c):
-            first_layer(c, "w1", banks[c % 3])
+            first_layer(c, "w1", banks[A_BANKS[c]])
 
         def sigmoid(c):
-            nc.scalar.activation(in_pair_order(sig[c]), pairs_of_bank(banks[c % 3]), SIGMOID)
+            nc.scalar.activation(in_pair_order(sig[c]), pairs_of_bank(banks[A_BANKS[c]]), SIGMOID)
 
         def product_b(c):
-            first_layer(c, "w3", banks[3 + c % 3])
+            first_layer(c, "w3", banks[B_BANKS[c]])
 
         def multiply(c):
             nc.vector.tensor_tensor(
-                in_pair_order(h_rows[c].bitcast(BF16)), pairs_of_bank(banks[3 + c % 3]), in_pair_order(sig[c]), MULT
+                in_pair_order(h_rows[c].bitcast(BF16)), pairs_of_bank(banks[B_BANKS[c]]), in_pair_order(sig[c]), MULT
             )
 
         def turn_h(turn, copy):
@@ -182,13 +197,14 @@ def tile_moe_pre_glu_sigmoid_kernel(
             for j in range(count):
                 for u in range(2):
                     nc.tensor.transpose(bank[:, j, u, :], h_rows[c0 + j][:, u * P : (u + 1) * P], identity[:])
-            dst = h_turned[:].bitcast(F32).rearrange("q (c s u) -> q c s u", u=2, s=CHUNK)
-            copy(dst[:, c0 : c0 + count], bank.rearrange("q c u s -> q c s u"))
+            dst = h_turned[turn][:].bitcast(F32).rearrange("q (c s u) -> q c s u", u=2, s=CHUNK)
+            copy(dst, bank.rearrange("q c u s -> q c s u"))
 
         def quantize_h(turn):
             c0, count = TURNS[turn]
-            lo, hi = c0 * CHUNK, (c0 + count) * CHUNK
-            nc.vector.quantize_mx(h_codes[:, lo:hi].bitcast(FP8X4), h_scales[:, lo:hi], h_turned[:, lo * PACK : hi * PACK])
+            expert, lo = divmod(c0 * CHUNK, C)
+            hi = lo + count * CHUNK
+            nc.vector.quantize_mx(h_codes[expert][:, lo:hi].bitcast(FP8X4), h_scales[expert][:, lo:hi], h_turned[turn][:])
 
         def second_layer(pieces, bank, copy):
             at = 0
@@ -198,10 +214,10 @@ def tile_moe_pre_glu_sigmoid_kernel(
                     expert = lo // C
                     nc.tensor.matmul_mx(
                         bank[:, at + lo - s0 : at + hi - s0],
-                        lhsT=w_codes["w2"][:, expert, 2 * P * nt : 2 * P * (nt + 1)].bitcast(FP4X4),
+                        lhsT=w_codes["w2", expert // 2 * 2][:, expert % 2, 2 * P * nt : 2 * P * (nt + 1)].bitcast(FP4X4),
                         lhsT_scale=w_scales["w2"][:, expert, P * nt : P * (nt + 1)],
-                        rhs=h_codes[:, lo:hi].bitcast(FP8X4),
-                        rhs_scale=h_scales[:, lo:hi],
+                        rhs=h_codes[expert][:, lo % C : lo % C + hi - lo].bitcast(FP8X4),
+                        rhs_scale=h_scales[expert][:, lo % C : lo % C + hi - lo],
                         start=True,
                         stop=True,
                     )
@@ -217,58 +233,55 @@ def tile_moe_pre_glu_sigmoid_kernel(
         gather_gated(0, CHUNK, V_SLOTS)
         for t in range(1, PACK):
             gather_gated(t, 0, V_SLOTS)
-        for t in range(PACK):
-            for g in (1, 2):
+        late = tile("late_stage", PACK * (groups[2] + groups[3]), F32, tag="gate_first")
+        stage[2] = late[:, 0 : PACK * groups[2]]
+        stage[3] = late[:, PACK * groups[2] : PACK * (groups[2] + groups[3])]
+        for g in (1, 2, 3):
+            for t in range(PACK):
                 gather_plain(g, t)
         round_x(0)
-        round_x(1)
-        for c in range(6):
-            quantize_x(c)
-            product_a(c)
-            sigmoid(c)
-            if c < 3:
-                product_b(c)
-            if c + 2 < 6:
-                round_x(c + 2)
-            if c == 4:
-                multiply(0)
-                product_b(3)
+        for r, (c0, n) in enumerate(ROUNDS):
+            if r + 1 < len(ROUNDS):
+                round_x(r + 1)
+            quantize_x(r)
+            for c in range(c0, c0 + n):
+                product_a(c)
+                sigmoid(c)
+        for c in range(3):
+            product_b(c)
+        multiply(0)
+        product_b(3)
         multiply(1)
-        product_b(4)
-        round_x(6)
-        round_x(7)
-        quantize_x(6)
-        product_a(6)
         turn_h(0, on_s)
-        sigmoid(6)
+        product_b(4)
         multiply(2)
         product_b(5)
-        quantize_x(7)
-        product_a(7)
-        sigmoid(7)
-        quantize_h(0)
         multiply(3)
-        product_b(6)
         turn_h(1, on_s)
+        product_b(6)
         multiply(4)
         product_b(7)
         multiply(5)
         turn_h(2, on_s)
-        quantize_h(1)
         multiply(6)
         turn_h(3, on_s)
         multiply(7)
+        for e in (0, 1):
+            h_codes[e] = tile(f"h_codes{e}", C, U32, tag=f"sig{6 + e}")
+            quantize_h(e)
+        turn_h(4, on_s)
         quantize_h(2)
-        turn_h(4, on_v)
         quantize_h(3)
         quantize_h(4)
-        second_layer(((0, 0, C), (1, 0, C)), banks[2], on_s)
-        second_layer(((2, 0, C), (3, 0, C)), banks[0], on_s)
-        second_layer(((0, C, 2 * C), (1, C, 2 * C)), banks[1], on_s)
-        second_layer(((2, C, 2 * C), (3, C, 2 * C)), banks[2], on_s)
-        second_layer(((0, 2 * C, 3 * C), (1, 2 * C, 3 * C)), banks[5], on_v)
-        second_layer(((0, 3 * C, S),), banks[0], on_s)
-        second_layer(((1, 3 * C, S),), banks[1], on_s)
+        half = S // 2
+        second_layer(((0, 0, half),), banks[1], on_s)
+        second_layer(((0, half, half + C),), banks[5], on_v)
+        second_layer(((0, half + C, S),), banks[4], on_v)
+        second_layer(((1, 0, half),), banks[2], on_s)
+        second_layer(((1, half, S),), banks[6], on_v)
+        second_layer(((2, half, S),), banks[7], on_v)
+        second_layer(((3, 0, half),), banks[1], on_v)
+        second_layer(((3, half, S),), banks[0], on_v)
 
         def picked(nt, pos_sb, t0, t1):
             return y[nt][:].indirect(pos_sb[:, t0 // STRIPE : t1 // STRIPE])
@@ -280,17 +293,14 @@ def tile_moe_pre_glu_sigmoid_kernel(
             nc.vector.tensor_tensor(total[nt][:, t0:t1], picked(nt, pos2_sb, t0, t1), first[nt][:, t0:t1], ADD)
             queue.dma_start(out[nt * P : (nt + 1) * P, t0:t1], total[nt][:, t0:t1])
 
-        nc.vector.tensor_copy(first[0][:, 0 : T // 2], picked(0, pos1_sb, 0, T // 2))
-        first_on_s(0, T // 2, T)
+        first_on_s(0, 0, T)
+        second_layer(((2, 0, half),), banks[3], on_s)
         first_on_s(1, 0, T)
-        second_layer(((3, 2 * C, S),), banks[3], on_s)
-        second_layer(((2, 2 * C, S),), banks[4], on_v)
         first_on_s(2, 0, T)
         first_on_s(3, T // 2, T)
         first_on_s(3, 0, T // 2)
-        add_second(0, 0, T)
-        add_second(1, 0, T)
-        add_second(2, 0, T)
+        for nt in range(3):
+            add_second(nt, 0, T)
         add_second(3, T // 2, T)
         add_second(3, T // 4, T // 2)
         add_second(3, 0, T // 4, nc.scalar)

@@ -64,8 +64,7 @@ def tile_moe_pre_glu_sigmoid_kernel(
         pos2_sb = keep.tile([P, T // STRIPE], U16, name="pos2_sb")
         x_phase = [tile(f"x_phase{t}", T, F32) for t in range(PACK)]
         gate_first = tile("gate_first", V_SLOTS, F32)
-        gate_mid = tile("gate_mid", groups[1], F32)
-        gate_last = tile("gate_last", groups[2] + groups[3], F32)
+        gate_rest = tile("gate_rest", S - V_SLOTS, F32)
         stage = {g: tile(f"stage{g}", PACK * groups[g], F32)[:] for g in range(2)}
         w_codes = {
             (m, e0): keep.tile([P, E // 2, 2 * H], U8, name=f"{m}_codes{e0}", align_bytes=MX_ALIGN)
@@ -115,12 +114,11 @@ def tile_moe_pre_glu_sigmoid_kernel(
         for t in range(1, PACK):
             nc.sync.dma_start(x_phase[t][:], x_rows[t])
         nc.scalar.activation(warm_out[:], warm_in[:], SIGMOID)
-        nc.sync.dma_start(gate_mid[:], gate[0:P, group_start[1] : group_start[2]])
+        nc.sync.dma_start(gate_rest[:], gate[0:P, V_SLOTS:S])
         load_codes("w1", 0, E // 2)
         load_scales("w1", "w3")
-        nc.sync.dma_start(gate_last[:], gate[0:P, group_start[2] : S])
-        load_codes("w1", E // 2, E)
         load_codes("w3", 0, E // 2)
+        load_codes("w1", E // 2, E)
         load_codes("w3", E // 2, E)
         load_scales("w2")
         load_codes("w2", 0, E // 2)
@@ -151,8 +149,7 @@ def tile_moe_pre_glu_sigmoid_kernel(
             if g == 0:
                 nc.vector.tensor_copy(dst, src)
             else:
-                at = lo - group_start[min(g, 2)]
-                row = (gate_mid if g == 1 else gate_last)[:, at : at + width]
+                row = gate_rest[:, lo - V_SLOTS : lo - V_SLOTS + width]
                 weight = row.rearrange("p (s o i) -> p s o i", o=1, i=run).broadcast_to([P, width // run, PACK, run])
                 nc.vector.tensor_tensor(dst, src, weight, MULT)
 
@@ -297,10 +294,13 @@ def tile_moe_pre_glu_sigmoid_kernel(
         second_layer(((2, 0, half),), banks[3], on_s)
         first_on_s(1, 0, T)
         first_on_s(2, 0, T)
-        first_on_s(3, T // 2, T)
-        first_on_s(3, 0, T // 2)
+        first_on_s(3, 0, T)
+        second = tile("second", T // 2, F32)
+        nc.scalar.activation(second[:], picked(3, pos2_sb, 0, T // 2), COPY)
         for nt in range(3):
             add_second(nt, 0, T)
         add_second(3, T // 2, T)
-        add_second(3, T // 4, T // 2)
-        add_second(3, 0, T // 4, nc.scalar)
+        for t0, queue in ((T // 4, nc.sync), (0, nc.scalar)):
+            cols = slice(t0, t0 + T // 4)
+            nc.vector.tensor_tensor(total[3][:, cols], first[3][:, cols], second[:, cols], ADD)
+            queue.dma_start(out[3 * P : 4 * P, cols], total[3][:, cols])

@@ -34,23 +34,19 @@ WORDS = H // 2
 Y_TILES = N // P
 
 
-V_SLOTS = 2 * CHUNK
-S_GROUPS = (3 * CHUNK, 2 * CHUNK, CHUNK)
+V_END = 352
+S_END = 768
 
-TURNS = ((0, 2), (2, 2), (4, 2), (6, 1), (7, 1))
-ROUNDS = ((0, 1), (1, 1), (2, 2), (4, 1), (5, 2), (7, 1))
-TURN_BANKS = (6, 7, 6, 7, 0)
-A_BANKS = (0, 1, 2, 6, 7, 0, 1, 2)
-B_BANKS = (3, 4, 5, 3, 4, 5, 3, 4)
+A_BANKS = (0, 1, 2, 6, 7, 0, 6, 0)
+B_BANKS = (3, 4, 5, 1, 2, 3, 7, 1)
 
 
 def tile_moe_pre_glu_sigmoid_kernel(
     tc, xT, w1_words, w1_scales, w3_words, w3_scales, w2_words, w2_scales, gate, offs, pos1, pos2, out
 ):
     nc = tc.nc
-    groups = (V_SLOTS,) + S_GROUPS
-    group_start = [sum(groups[:g]) for g in range(len(groups))]
     weights = {"w1": (w1_words, w1_scales), "w3": (w3_words, w3_scales), "w2": (w2_words, w2_scales)}
+    groups = ((0, V_END), (V_END, S_END), (S_END, S))
 
     with ExitStack() as ctx:
         keep = ctx.enter_context(tc.tile_pool(name="keep", bufs=1))
@@ -63,9 +59,9 @@ def tile_moe_pre_glu_sigmoid_kernel(
         pos1_sb = keep.tile([P, T // STRIPE], U16, name="pos1_sb")
         pos2_sb = keep.tile([P, T // STRIPE], U16, name="pos2_sb")
         x_phase = [tile(f"x_phase{t}", T, F32) for t in range(PACK)]
-        gate_first = tile("gate_first", V_SLOTS, F32)
-        gate_rest = tile("gate_rest", S - V_SLOTS, F32)
-        stage = {g: tile(f"stage{g}", PACK * groups[g], F32)[:] for g in range(2)}
+        gate_first = tile("gate_first", V_END, F32)
+        gate_rest = tile("gate_rest", S - V_END, F32)
+        stage = {g: tile(f"stage{g}", PACK * (groups[g][1] - groups[g][0]), F32)[:] for g in range(2)}
         w_codes = {
             (m, e0): keep.tile([P, E // 2, 2 * H], U8, name=f"{m}_codes{e0}", align_bytes=MX_ALIGN)
             for m in weights
@@ -73,17 +69,14 @@ def tile_moe_pre_glu_sigmoid_kernel(
         }
         w_scales = {m: keep.tile([P, E, H], U8, name=f"{m}_scale_bytes", align_bytes=MX_ALIGN) for m in weights}
         identity = tile("identity", P, F32)
-        x_bf16 = [tile(f"x_bf16_{c0}", n * CHUNK * PACK, BF16)[:] for c0, n in ROUNDS]
-        run_codes = [tile(f"x_codes{c0}", n * CHUNK, U32)[:] for c0, n in ROUNDS]
-        x_codes = [run_codes[r][:, j * CHUNK : (j + 1) * CHUNK] for r, (c0, n) in enumerate(ROUNDS) for j in range(n)]
-        run_scales = [tile(f"x_scales{c0}", n * CHUNK, U8)[:] for c0, n in ROUNDS]
-        x_scales = [run_scales[r][:, j * CHUNK : (j + 1) * CHUNK] for r, (c0, n) in enumerate(ROUNDS) for j in range(n)]
+        x_bf16 = tile("x_bf16", PACK * S_END, BF16)
+        x_codes, x_scales = {}, {}
         sig = [tile(f"sig{c}", H, F32)[:] for c in range(CHUNKS)]
         h_rows = [tile(f"h_rows{c}", WORDS, F32)[:] for c in range(CHUNKS)]
-        h_turned = [tile(f"h_turned{j}", count * CHUNK * PACK, BF16) for j, (c0, count) in enumerate(TURNS)]
-        h_codes = {e: tile(f"h_codes{e}", C, U32) for e in (2, 3)}
+        h_turned = {}
+        h_codes = [tile(f"h_codes{e}", C, U32) for e in range(E)]
         h_scales = [tile(f"h_scales{e}", C, U8) for e in range(E)]
-        y = [tile(f"y{nt}", S, F32) for nt in range(Y_TILES)]
+        y = {nt: tile(f"y{nt}", S, F32) for nt in (0, 2)}
         first = [tile(f"first{nt}", T, F32) for nt in range(Y_TILES)]
         total = [tile(f"total{nt}", T, F32) for nt in range(Y_TILES)]
         banks = [psum.tile([P, BANK], F32, name=f"bank{j}") for j in range(BANKS)]
@@ -97,9 +90,9 @@ def tile_moe_pre_glu_sigmoid_kernel(
 
         x_rows = xT.rearrange("(p t) n -> t p n", t=PACK)
 
-        def load_codes(m, e0, e1):
+        def load_codes(m, e0):
             src = weights[m][0].rearrange("e s p b -> p (e s) b")
-            nc.sync.dma_start(w_codes[m, e0][:].bitcast(I32), src[:, e0:e1, :].bitcast(I32))
+            nc.sync.dma_start(w_codes[m, e0][:].bitcast(I32), src[:, e0 : e0 + E // 2, :].bitcast(I32))
 
         def load_scales(*names):
             for q in (0, 2, 1, 3):
@@ -107,54 +100,65 @@ def tile_moe_pre_glu_sigmoid_kernel(
                     src = weights[m][1].rearrange("e s (q r) n -> q r (e s) n", r=4)
                     nc.sync.dma_start(w_scales[m][QUAD * q : QUAD * q + 4, :, :].bitcast(I32), src[q].bitcast(I32))
 
+        nc.scalar.activation(warm_out[:], warm_in[:], SIGMOID)
         nc.sync.dma_start(x_phase[0][:], x_rows[0])
-        nc.scalar.dma_start(gate_first[:, 0:CHUNK], gate[0:P, 0:CHUNK])
         nc.sync.dma_start(offs_sb[:], offs)
-        nc.sync.dma_start(gate_first[:, CHUNK:V_SLOTS], gate[0:P, CHUNK:V_SLOTS])
+        nc.sync.dma_start(gate_first[:], gate[0:P, 0:V_END])
         for t in range(1, PACK):
             nc.sync.dma_start(x_phase[t][:], x_rows[t])
-        nc.scalar.activation(warm_out[:], warm_in[:], SIGMOID)
-        nc.sync.dma_start(gate_rest[:], gate[0:P, V_SLOTS:S])
-        load_codes("w1", 0, E // 2)
+        nc.sync.dma_start(gate_rest[:], gate[0:P, V_END:S])
         load_scales("w1", "w3")
-        load_codes("w3", 0, E // 2)
-        load_codes("w1", E // 2, E)
-        load_codes("w3", E // 2, E)
+        load_codes("w1", 0)
+        load_codes("w3", 0)
+        load_codes("w1", E // 2)
+        load_codes("w3", E // 2)
         load_scales("w2")
-        load_codes("w2", 0, E // 2)
-        load_codes("w2", E // 2, E)
+        load_codes("w2", 0)
+        load_codes("w2", E // 2)
         nc.sync.dma_start(pos1_sb[:], pos1)
         nc.sync.dma_start(pos2_sb[:], pos2)
 
-        def picked_x(g, t, lo, hi):
-            return x_phase[t][:].indirect(offs_sb[:, (group_start[g] + lo) // STRIPE : (group_start[g] + hi) // STRIPE])
+        def picked_x(g, t):
+            return x_phase[t][:].indirect(offs_sb[:, groups[g][0] // STRIPE : groups[g][1] // STRIPE])
 
-        def staged(g, t, lo, hi):
-            return stage[g][:, t * groups[g] + lo : t * groups[g] + hi]
+        def staged(g, t):
+            width = groups[g][1] - groups[g][0]
+            return stage[g][:, t * width : (t + 1) * width]
 
-        def gather_gated(t, lo, hi):
-            nc.vector.tensor_tensor(staged(0, t, lo, hi), picked_x(0, t, lo, hi), gate_first[:, lo:hi], MULT)
+        def staged_slots(lo, hi):
+            g = max(j for j in range(len(groups)) if groups[j][0] <= lo)
+            return stage[g].rearrange("p (t s) -> p t s", t=PACK)[:, :, lo - groups[g][0] : hi - groups[g][0]]
 
-        def gather_plain(g, t):
-            nc.scalar.activation(staged(g, t, 0, groups[g]), picked_x(g, t, 0, groups[g]), COPY)
+        def round_gated(lo, hi):
+            src = staged_slots(lo, hi).rearrange("p t (s i) -> p s t i", i=4)
+            nc.vector.tensor_copy(x_bf16[:, PACK * lo : PACK * hi].rearrange("p (s i t) -> p s t i", i=4, t=PACK), src)
 
-        def round_x(r):
-            lo, width = ROUNDS[r][0] * CHUNK, ROUNDS[r][1] * CHUNK
-            g = max(j for j in range(len(groups)) if group_start[j] <= lo)
-            s0 = lo - group_start[g]
-            phases = stage[g].rearrange("p (t s) -> p t s", t=PACK)
-            run = 4 if g == 0 else 2
-            src = phases[:, :, s0 : s0 + width].rearrange("p t (s i) -> p s t i", i=run)
-            dst = x_bf16[r].rearrange("p (s i t) -> p s t i", i=run, t=PACK)
-            if g == 0:
-                nc.vector.tensor_copy(dst, src)
-            else:
-                row = gate_rest[:, lo - V_SLOTS : lo - V_SLOTS + width]
-                weight = row.rearrange("p (s o i) -> p s o i", o=1, i=run).broadcast_to([P, width // run, PACK, run])
-                nc.vector.tensor_tensor(dst, src, weight, MULT)
+        def gate_and_round(lo, hi):
+            src = staged_slots(lo, hi).rearrange("p t (s i) -> p s t i", i=2)
+            dst = x_bf16[:, PACK * lo : PACK * hi].rearrange("p (s i t) -> p s t i", i=2, t=PACK)
+            row = gate_rest[:, lo - V_END : hi - V_END].rearrange("p (s o i) -> p s o i", o=1, i=2)
+            nc.vector.tensor_tensor(dst, src, row.broadcast_to([P, (hi - lo) // 2, PACK, 2]), MULT)
 
-        def quantize_x(r):
-            nc.vector.quantize_mx(run_codes[r].bitcast(FP8X4), run_scales[r], x_bf16[r])
+        last_room = x_bf16[:, PACK * (S_END - CHUNK) : PACK * S_END]
+
+        def gate_and_round_on_gpsimd(c):
+            lo, hi = c * CHUNK, (c + 1) * CHUNK
+            row = gate_rest[:, lo - V_END : hi - V_END].rearrange("p (s o) -> p s o", o=1)
+            nc.gpsimd.tensor_tensor(
+                last_room.rearrange("p (s t) -> p s t", t=PACK),
+                staged_slots(lo, hi).rearrange("p t s -> p s t"),
+                row.broadcast_to([P, CHUNK, PACK]),
+                MULT,
+            )
+
+        def quantize_x(c0, count, tag=None):
+            codes = tile(f"x_codes{c0}", count * CHUNK, U32, tag=tag)[:]
+            scales = tile(f"x_scales{c0}", count * CHUNK, U8)[:]
+            for j in range(count):
+                x_codes[c0 + j] = codes[:, j * CHUNK : (j + 1) * CHUNK]
+                x_scales[c0 + j] = scales[:, j * CHUNK : (j + 1) * CHUNK]
+            src = last_room if c0 * CHUNK >= S_END else x_bf16[:, PACK * CHUNK * c0 : PACK * CHUNK * (c0 + count)]
+            nc.vector.quantize_mx(codes.bitcast(FP8X4), scales, src)
 
         def pairs_of_bank(bank):
             return bank[:].rearrange("s (q u e) -> s u q e", u=2, e=2)
@@ -177,124 +181,159 @@ def tile_moe_pre_glu_sigmoid_kernel(
         def product_a(c):
             first_layer(c, "w1", banks[A_BANKS[c]])
 
-        def sigmoid(c):
-            nc.scalar.activation(in_pair_order(sig[c]), pairs_of_bank(banks[A_BANKS[c]]), SIGMOID)
-
         def product_b(c):
             first_layer(c, "w3", banks[B_BANKS[c]])
+
+        def sigmoid(c):
+            nc.scalar.activation(in_pair_order(sig[c]), pairs_of_bank(banks[A_BANKS[c]]), SIGMOID)
 
         def multiply(c):
             nc.vector.tensor_tensor(
                 in_pair_order(h_rows[c].bitcast(BF16)), pairs_of_bank(banks[B_BANKS[c]]), in_pair_order(sig[c]), MULT
             )
 
-        def turn_h(turn, copy):
-            c0, count = TURNS[turn]
-            bank = banks[TURN_BANKS[turn]][:, 0 : 2 * CHUNK * count].rearrange("q (c u s) -> q c u s", u=2, s=CHUNK)
+        def turn_view(count, bank):
+            return banks[bank][:, 0 : 2 * CHUNK * count].rearrange("q (c u s) -> q c u s", u=2, s=CHUNK)
+
+        def turn_h(c0, count, bank):
             for j in range(count):
                 for u in range(2):
-                    nc.tensor.transpose(bank[:, j, u, :], h_rows[c0 + j][:, u * P : (u + 1) * P], identity[:])
-            dst = h_turned[turn][:].bitcast(F32).rearrange("q (c s u) -> q c s u", u=2, s=CHUNK)
-            copy(dst, bank.rearrange("q c u s -> q c s u"))
+                    nc.tensor.transpose(turn_view(count, bank)[:, j, u, :], h_rows[c0 + j][:, u * P : (u + 1) * P], identity[:])
 
-        def quantize_h(turn):
-            c0, count = TURNS[turn]
+        def copy_turned(c0, count, bank, tag=None):
+            h_turned[c0] = tile(f"h_turned{c0}", count * CHUNK * PACK, BF16, tag=tag)
+            dst = h_turned[c0][:].bitcast(F32).rearrange("q (c s u) -> q c s u", u=2, s=CHUNK)
+            nc.scalar.copy(dst, turn_view(count, bank).rearrange("q c u s -> q c s u"))
+
+        def quantize_h(c0, count):
             expert, lo = divmod(c0 * CHUNK, C)
             hi = lo + count * CHUNK
-            nc.vector.quantize_mx(h_codes[expert][:, lo:hi].bitcast(FP8X4), h_scales[expert][:, lo:hi], h_turned[turn][:])
+            nc.vector.quantize_mx(h_codes[expert][:, lo:hi].bitcast(FP8X4), h_scales[expert][:, lo:hi], h_turned[c0][:])
 
-        def second_layer(pieces, bank, copy):
-            at = 0
-            for nt, s0, s1 in pieces:
-                for lo in range(s0, s1, C):
-                    hi = min(s1, lo + C)
-                    expert = lo // C
-                    nc.tensor.matmul_mx(
-                        bank[:, at + lo - s0 : at + hi - s0],
-                        lhsT=w_codes["w2", expert // 2 * 2][:, expert % 2, 2 * P * nt : 2 * P * (nt + 1)].bitcast(FP4X4),
-                        lhsT_scale=w_scales["w2"][:, expert, P * nt : P * (nt + 1)],
-                        rhs=h_codes[expert][:, lo % C : lo % C + hi - lo].bitcast(FP8X4),
-                        rhs_scale=h_scales[expert][:, lo % C : lo % C + hi - lo],
-                        start=True,
-                        stop=True,
-                    )
-                at = at + s1 - s0
-            at = 0
-            for nt, s0, s1 in pieces:
-                copy(y[nt][:, s0:s1], bank[:, at : at + s1 - s0])
-                at = at + s1 - s0
+        def second_layer(nt, expert, bank, half):
+            nc.tensor.matmul_mx(
+                banks[bank][:, half * C : (half + 1) * C],
+                lhsT=w_codes["w2", expert // 2 * 2][:, expert % 2, 2 * P * nt : 2 * P * (nt + 1)].bitcast(FP4X4),
+                lhsT_scale=w_scales["w2"][:, expert, P * nt : P * (nt + 1)],
+                rhs=h_codes[expert][:].bitcast(FP8X4),
+                rhs_scale=h_scales[expert][:],
+                start=True,
+                stop=True,
+            )
+
+        def copy_y(copy, nt, e0, count, bank, half):
+            copy(y[nt][:, e0 * C : (e0 + count) * C], banks[bank][:, half * C : (half + count) * C])
 
         on_s, on_v = nc.scalar.copy, nc.vector.tensor_copy
 
-        gather_gated(0, 0, CHUNK)
-        gather_gated(0, CHUNK, V_SLOTS)
-        for t in range(1, PACK):
-            gather_gated(t, 0, V_SLOTS)
-        late = tile("late_stage", PACK * (groups[2] + groups[3]), F32, tag="gate_first")
-        stage[2] = late[:, 0 : PACK * groups[2]]
-        stage[3] = late[:, PACK * groups[2] : PACK * (groups[2] + groups[3])]
-        for g in (1, 2, 3):
-            for t in range(PACK):
-                gather_plain(g, t)
-        round_x(0)
-        for r, (c0, n) in enumerate(ROUNDS):
-            if r + 1 < len(ROUNDS):
-                round_x(r + 1)
-            quantize_x(r)
-            for c in range(c0, c0 + n):
-                product_a(c)
-                sigmoid(c)
-        for c in range(3):
-            product_b(c)
-        multiply(0)
+        for t in range(PACK):
+            nc.vector.tensor_tensor(staged(0, t), picked_x(0, t), gate_first[:], MULT)
+        for t in range(PACK):
+            nc.scalar.activation(staged(1, t), picked_x(1, t), COPY)
+        stage[2] = tile("late_stage", PACK * (S - S_END), F32, tag="gate_first")[:]
+        for t in range(PACK):
+            nc.scalar.activation(staged(2, t), picked_x(2, t), COPY)
+
+        round_gated(0, CHUNK)
+        round_gated(CHUNK, V_END)
+        quantize_x(0, 1)
+        gate_and_round(V_END, 4 * CHUNK)
+        quantize_x(1, 1)
+        gate_and_round(4 * CHUNK, 5 * CHUNK)
+        quantize_x(2, 2)
+        gate_and_round(5 * CHUNK, 6 * CHUNK)
+        quantize_x(4, 1)
+        quantize_x(5, 1)
+        gate_and_round_on_gpsimd(6)
+
+        product_a(0)
+        product_a(1)
+        product_b(0)
+        product_a(2)
+        product_b(1)
+        product_a(3)
+        product_b(2)
+        product_a(4)
+        sigmoid(0)
+        product_a(5)
+        sigmoid(1)
         product_b(3)
-        multiply(1)
-        turn_h(0, on_s)
+        sigmoid(2)
         product_b(4)
-        multiply(2)
+        sigmoid(3)
+        sigmoid(4)
+        sigmoid(5)
+        multiply(0)
         product_b(5)
-        multiply(3)
-        turn_h(1, on_s)
+        multiply(1)
+        turn_h(0, 2, 4)
+        quantize_x(6, 1, tag="sig0")
+        gate_and_round_on_gpsimd(7)
+        product_a(6)
         product_b(6)
+        sigmoid(6)
+        copy_turned(0, 2, 4)
+        multiply(2)
+        multiply(3)
+        turn_h(2, 2, 5)
+        copy_turned(2, 2, 5)
         multiply(4)
+        quantize_x(7, 1, tag="sig3")
+        product_a(7)
         product_b(7)
+        sigmoid(7)
         multiply(5)
-        turn_h(2, on_s)
+        turn_h(4, 2, 2)
+        quantize_h(0, 2)
+        second_layer(0, 0, 3, 0)
+        second_layer(1, 0, 0, 0)
+        copy_turned(4, 2, 2, tag="sig3")
         multiply(6)
-        turn_h(3, on_s)
+        turn_h(6, 1, 7)
+        copy_turned(6, 1, 7)
+        quantize_h(2, 2)
+        second_layer(0, 1, 3, 1)
+        second_layer(1, 1, 0, 1)
+        copy_y(on_s, 0, 0, 2, 3, 0)
         multiply(7)
-        for e in (0, 1):
-            h_codes[e] = tile(f"h_codes{e}", C, U32, tag=f"sig{6 + e}")
-            quantize_h(e)
-        turn_h(4, on_s)
-        quantize_h(2)
-        quantize_h(3)
-        quantize_h(4)
-        half = S // 2
-        second_layer(((0, 0, half),), banks[1], on_s)
-        second_layer(((0, half, half + C),), banks[5], on_v)
-        second_layer(((0, half + C, S),), banks[4], on_v)
-        second_layer(((1, 0, half),), banks[2], on_s)
-        second_layer(((1, half, S),), banks[6], on_v)
-        second_layer(((2, half, S),), banks[7], on_v)
-        second_layer(((3, 0, half),), banks[1], on_v)
-        second_layer(((3, half, S),), banks[0], on_v)
+        turn_h(7, 1, 4)
+        copy_turned(7, 1, 4)
+        quantize_h(4, 2)
+        for nt, bank in ((2, 1), (3, 3)):
+            second_layer(nt, 0, bank, 0)
+            second_layer(nt, 1, bank, 1)
+        second_layer(0, 2, 2, 0)
+        second_layer(1, 2, 5, 0)
+        second_layer(2, 2, 5, 1)
+        y[1] = tile("y1", S, F32, tag="sig7")
+        copy_y(on_v, 1, 0, 2, 0, 0)
+        copy_y(on_s, 2, 0, 2, 1, 0)
+        copy_y(on_s, 0, 2, 1, 2, 0)
+        copy_y(on_s, 1, 2, 1, 5, 0)
+        copy_y(on_s, 2, 2, 1, 5, 1)
+        quantize_h(6, 1)
+        quantize_h(7, 1)
+        second_layer(0, 3, 6, 0)
+        second_layer(1, 3, 7, 0)
+        second_layer(2, 3, 7, 1)
+        second_layer(3, 2, 4, 0)
+        second_layer(3, 3, 4, 1)
+        y[3] = tile("y3", S, F32, tag="h_turned6")
+        copy_y(on_v, 3, 0, 2, 3, 0)
+        copy_y(on_v, 0, 3, 1, 6, 0)
+        copy_y(on_v, 1, 3, 1, 7, 0)
+        copy_y(on_v, 2, 3, 1, 7, 1)
+        copy_y(on_v, 3, 2, 2, 4, 0)
 
         def picked(nt, pos_sb, t0, t1):
             return y[nt][:].indirect(pos_sb[:, t0 // STRIPE : t1 // STRIPE])
 
-        def first_on_s(nt, t0, t1):
-            nc.scalar.activation(first[nt][:, t0:t1], picked(nt, pos1_sb, t0, t1), COPY)
-
-        def add_second(nt, t0, t1, queue=nc.sync):
+        def add_second(nt, t0, t1):
             nc.vector.tensor_tensor(total[nt][:, t0:t1], picked(nt, pos2_sb, t0, t1), first[nt][:, t0:t1], ADD)
-            queue.dma_start(out[nt * P : (nt + 1) * P, t0:t1], total[nt][:, t0:t1])
+            nc.sync.dma_start(out[nt * P : (nt + 1) * P, t0:t1], total[nt][:, t0:t1])
 
-        first_on_s(0, 0, T)
-        second_layer(((2, 0, half),), banks[3], on_s)
-        first_on_s(1, 0, T)
-        first_on_s(2, 0, T)
-        first_on_s(3, 0, T)
+        for nt in range(Y_TILES):
+            nc.scalar.activation(first[nt][:], picked(nt, pos1_sb, 0, T), COPY)
         second = tile("second", T // 2, F32)
         nc.scalar.activation(second[:], picked(3, pos2_sb, 0, T // 2), COPY)
         for nt in range(3):

@@ -37,8 +37,8 @@ Y_TILES = N // P
 V_END = 352
 S_END = 768
 
-A_BANKS = (0, 1, 2, 6, 7, 0, 6, 0)
-B_BANKS = (3, 4, 5, 1, 2, 3, 7, 1)
+A_BANKS = (0, 1, 2, 6, 7, 5, 4, 5)
+B_BANKS = (3, 0, 1, 2, 6, 7, 0, 2)
 
 
 def tile_moe_pre_glu_sigmoid_kernel(
@@ -76,7 +76,7 @@ def tile_moe_pre_glu_sigmoid_kernel(
         h_turned = {}
         h_codes = [tile(f"h_codes{e}", C, U32) for e in range(E)]
         h_scales = [tile(f"h_scales{e}", C, U8) for e in range(E)]
-        y = {nt: tile(f"y{nt}", S, F32) for nt in (0, 2)}
+        y = {nt: tile(f"y{nt}", S, F32) for nt in (0, 1, 3)}
         first = [tile(f"first{nt}", T, F32) for nt in range(Y_TILES)]
         total = [tile(f"total{nt}", T, F32) for nt in range(Y_TILES)]
         banks = [psum.tile([P, BANK], F32, name=f"bank{j}") for j in range(BANKS)]
@@ -108,10 +108,10 @@ def tile_moe_pre_glu_sigmoid_kernel(
             nc.sync.dma_start(x_phase[t][:], x_rows[t])
         nc.sync.dma_start(gate_rest[:], gate[0:P, V_END:S])
         load_scales("w1", "w3")
-        load_codes("w1", 0)
         load_codes("w3", 0)
-        load_codes("w1", E // 2)
+        load_codes("w1", 0)
         load_codes("w3", E // 2)
+        load_codes("w1", E // 2)
         load_scales("w2")
         load_codes("w2", 0)
         load_codes("w2", E // 2)
@@ -236,94 +236,95 @@ def tile_moe_pre_glu_sigmoid_kernel(
 
         round_gated(0, CHUNK)
         round_gated(CHUNK, V_END)
+        gate_and_round(V_END, 3 * CHUNK)
         quantize_x(0, 1)
-        gate_and_round(V_END, 4 * CHUNK)
-        quantize_x(1, 1)
+        gate_and_round(3 * CHUNK, 4 * CHUNK)
+        quantize_x(1, 2)
         gate_and_round(4 * CHUNK, 5 * CHUNK)
-        quantize_x(2, 2)
+        quantize_x(3, 1)
         gate_and_round(5 * CHUNK, 6 * CHUNK)
         quantize_x(4, 1)
         quantize_x(5, 1)
         gate_and_round_on_gpsimd(6)
 
-        product_a(0)
-        product_a(1)
         product_b(0)
-        product_a(2)
-        product_b(1)
-        product_a(3)
-        product_b(2)
-        product_a(4)
+        for c in range(4):
+            product_a(c)
         sigmoid(0)
-        product_a(5)
+        product_b(1)
+        product_a(4)
         sigmoid(1)
-        product_b(3)
+        product_b(2)
+        product_a(5)
         sigmoid(2)
-        product_b(4)
+        product_b(3)
         sigmoid(3)
+        product_b(4)
         sigmoid(4)
+        product_b(5)
         sigmoid(5)
         multiply(0)
-        product_b(5)
         multiply(1)
-        turn_h(0, 2, 4)
-        quantize_x(6, 1, tag="sig0")
+        turn_h(0, 2, 3)
+        multiply(2)
+        quantize_x(6, 1, tag="sig1")
         gate_and_round_on_gpsimd(7)
         product_a(6)
         product_b(6)
+        copy_turned(0, 2, 3)
         sigmoid(6)
-        copy_turned(0, 2, 4)
-        multiply(2)
         multiply(3)
-        turn_h(2, 2, 5)
-        copy_turned(2, 2, 5)
+        turn_h(2, 2, 1)
+        copy_turned(2, 2, 1)
         multiply(4)
-        quantize_x(7, 1, tag="sig3")
+        multiply(5)
+        turn_h(4, 2, 6)
+        quantize_x(7, 1, tag="sig4")
         product_a(7)
         product_b(7)
         sigmoid(7)
-        multiply(5)
-        turn_h(4, 2, 2)
         quantize_h(0, 2)
         second_layer(0, 0, 3, 0)
-        second_layer(1, 0, 0, 0)
-        copy_turned(4, 2, 2, tag="sig3")
+        second_layer(2, 0, 1, 0)
+        copy_turned(4, 2, 6, tag="sig4")
         multiply(6)
-        turn_h(6, 1, 7)
-        copy_turned(6, 1, 7)
+        turn_h(6, 1, 4)
+        copy_turned(6, 1, 4)
+        second_layer(1, 0, 5, 0)
         quantize_h(2, 2)
+        copy_y(on_v, 0, 0, 1, 3, 0)
+        second_layer(1, 1, 5, 1)
+        second_layer(2, 1, 1, 1)
         second_layer(0, 1, 3, 1)
-        second_layer(1, 1, 0, 1)
-        copy_y(on_s, 0, 0, 2, 3, 0)
+        copy_y(on_s, 0, 1, 1, 3, 1)
+        copy_y(on_s, 1, 0, 2, 5, 0)
         multiply(7)
-        turn_h(7, 1, 4)
-        copy_turned(7, 1, 4)
+        turn_h(7, 1, 7)
+        copy_turned(7, 1, 7)
         quantize_h(4, 2)
-        for nt, bank in ((2, 1), (3, 3)):
-            second_layer(nt, 0, bank, 0)
-            second_layer(nt, 1, bank, 1)
-        second_layer(0, 2, 2, 0)
-        second_layer(1, 2, 5, 0)
-        second_layer(2, 2, 5, 1)
-        y[1] = tile("y1", S, F32, tag="sig7")
-        copy_y(on_v, 1, 0, 2, 0, 0)
-        copy_y(on_s, 2, 0, 2, 1, 0)
-        copy_y(on_s, 0, 2, 1, 2, 0)
-        copy_y(on_s, 1, 2, 1, 5, 0)
-        copy_y(on_s, 2, 2, 1, 5, 1)
-        quantize_h(6, 1)
-        quantize_h(7, 1)
-        second_layer(0, 3, 6, 0)
-        second_layer(1, 3, 7, 0)
-        second_layer(2, 3, 7, 1)
+        second_layer(0, 2, 6, 0)
+        second_layer(3, 0, 2, 0)
+        second_layer(3, 1, 2, 1)
+        second_layer(1, 2, 0, 0)
+        second_layer(2, 2, 0, 1)
         second_layer(3, 2, 4, 0)
-        second_layer(3, 3, 4, 1)
-        y[3] = tile("y3", S, F32, tag="h_turned6")
-        copy_y(on_v, 3, 0, 2, 3, 0)
-        copy_y(on_v, 0, 3, 1, 6, 0)
-        copy_y(on_v, 1, 3, 1, 7, 0)
-        copy_y(on_v, 2, 3, 1, 7, 1)
-        copy_y(on_v, 3, 2, 2, 4, 0)
+        quantize_h(6, 1)
+        y[2] = tile("y2", S, F32, tag="sig7")
+        copy_y(on_v, 2, 0, 2, 1, 0)
+        copy_y(on_v, 0, 2, 1, 6, 0)
+        copy_y(on_s, 3, 0, 2, 2, 0)
+        copy_y(on_s, 1, 2, 1, 0, 0)
+        copy_y(on_s, 2, 2, 1, 0, 1)
+        quantize_h(7, 1)
+        second_layer(0, 3, 3, 0)
+        second_layer(1, 3, 5, 0)
+        second_layer(2, 3, 5, 1)
+        second_layer(3, 3, 1, 0)
+        copy_y(on_v, 3, 2, 1, 4, 0)
+        copy_y(on_v, 0, 3, 1, 3, 0)
+        copy_y(on_v, 1, 3, 1, 5, 0)
+        copy_y(on_v, 2, 3, 1, 5, 1)
+        copy_y(on_v, 3, 3, 1, 1, 0)
 
         def picked(nt, pos_sb, t0, t1):
             return y[nt][:].indirect(pos_sb[:, t0 // STRIPE : t1 // STRIPE])

@@ -36,9 +36,10 @@ Y_TILES = N // P
 
 V_END = 352
 S_END = 768
+S_SECOND = 384
 
-A_BANKS = (0, 1, 2, 6, 7, 5, 4, 5)
-B_BANKS = (3, 0, 1, 2, 6, 7, 0, 2)
+A_BANKS = (0, 1, 2, 1, 7, 5, 1, 7)
+B_BANKS = (3, 0, 6, 2, 4, 3, 6, 5)
 
 
 def tile_moe_pre_glu_sigmoid_kernel(
@@ -62,11 +63,7 @@ def tile_moe_pre_glu_sigmoid_kernel(
         gate_first = tile("gate_first", V_END, F32)
         gate_rest = tile("gate_rest", S - V_END, F32)
         stage = {g: tile(f"stage{g}", PACK * (groups[g][1] - groups[g][0]), F32)[:] for g in range(2)}
-        w_codes = {
-            (m, e0): keep.tile([P, E // 2, 2 * H], U8, name=f"{m}_codes{e0}", align_bytes=MX_ALIGN)
-            for m in weights
-            for e0 in (0, E // 2)
-        }
+        w_codes = {}
         w_scales = {m: keep.tile([P, E, H], U8, name=f"{m}_scale_bytes", align_bytes=MX_ALIGN) for m in weights}
         identity = tile("identity", P, F32)
         x_bf16 = tile("x_bf16", PACK * S_END, BF16)
@@ -90,9 +87,12 @@ def tile_moe_pre_glu_sigmoid_kernel(
 
         x_rows = xT.rearrange("(p t) n -> t p n", t=PACK)
 
-        def load_codes(m, e0):
+        def load_codes(m, e0, count):
+            held = keep.tile([P, count, 2 * H], U8, name=f"{m}_codes{e0}", align_bytes=MX_ALIGN)
             src = weights[m][0].rearrange("e s p b -> p (e s) b")
-            nc.sync.dma_start(w_codes[m, e0][:].bitcast(I32), src[:, e0 : e0 + E // 2, :].bitcast(I32))
+            nc.sync.dma_start(held[:].bitcast(I32), src[:, e0 : e0 + count, :].bitcast(I32))
+            for j in range(count):
+                w_codes[m, e0 + j] = held[:, j, :]
 
         def load_scales(*names):
             for q in (0, 2, 1, 3):
@@ -108,13 +108,15 @@ def tile_moe_pre_glu_sigmoid_kernel(
             nc.sync.dma_start(x_phase[t][:], x_rows[t])
         nc.sync.dma_start(gate_rest[:], gate[0:P, V_END:S])
         load_scales("w1", "w3")
-        load_codes("w3", 0)
-        load_codes("w1", 0)
-        load_codes("w3", E // 2)
-        load_codes("w1", E // 2)
+        load_codes("w3", 0, 1)
+        load_codes("w1", 0, 1)
+        load_codes("w1", 1, 1)
+        load_codes("w3", 1, 1)
+        load_codes("w1", 2, 2)
+        load_codes("w3", 2, 2)
         load_scales("w2")
-        load_codes("w2", 0)
-        load_codes("w2", E // 2)
+        load_codes("w2", 0, 2)
+        load_codes("w2", 2, 2)
         nc.sync.dma_start(pos1_sb[:], pos1)
         nc.sync.dma_start(pos2_sb[:], pos2)
 
@@ -172,7 +174,7 @@ def tile_moe_pre_glu_sigmoid_kernel(
                 bank[:],
                 lhsT=x_codes[c].bitcast(FP8X4),
                 lhsT_scale=x_scales[c],
-                rhs=w_codes[m, expert // 2 * 2][:, expert % 2, :].bitcast(FP4X4),
+                rhs=w_codes[m, expert].bitcast(FP4X4),
                 rhs_scale=w_scales[m][:, expert, :],
                 start=True,
                 stop=True,
@@ -213,7 +215,7 @@ def tile_moe_pre_glu_sigmoid_kernel(
         def second_layer(nt, expert, bank, half):
             nc.tensor.matmul_mx(
                 banks[bank][:, half * C : (half + 1) * C],
-                lhsT=w_codes["w2", expert // 2 * 2][:, expert % 2, 2 * P * nt : 2 * P * (nt + 1)].bitcast(FP4X4),
+                lhsT=w_codes["w2", expert][:, 2 * P * nt : 2 * P * (nt + 1)].bitcast(FP4X4),
                 lhsT_scale=w_scales["w2"][:, expert, P * nt : P * (nt + 1)],
                 rhs=h_codes[expert][:].bitcast(FP8X4),
                 rhs_scale=h_scales[expert][:],
@@ -226,8 +228,11 @@ def tile_moe_pre_glu_sigmoid_kernel(
 
         on_s, on_v = nc.scalar.copy, nc.vector.tensor_copy
 
-        for t in range(PACK):
+        for t in range(PACK - 1):
             nc.vector.tensor_tensor(staged(0, t), picked_x(0, t), gate_first[:], MULT)
+        for lo, hi in ((0, CHUNK), (CHUNK, V_END)):
+            picked = x_phase[PACK - 1][:].indirect(offs_sb[:, lo // STRIPE : hi // STRIPE])
+            nc.vector.tensor_tensor(staged(0, PACK - 1)[:, lo:hi], picked, gate_first[:, lo:hi], MULT)
         for t in range(PACK):
             nc.scalar.activation(staged(1, t), picked_x(1, t), COPY)
         stage[2] = tile("late_stage", PACK * (S - S_END), F32, tag="gate_first")[:]
@@ -235,9 +240,9 @@ def tile_moe_pre_glu_sigmoid_kernel(
             nc.scalar.activation(staged(2, t), picked_x(2, t), COPY)
 
         round_gated(0, CHUNK)
-        round_gated(CHUNK, V_END)
         gate_and_round(V_END, 3 * CHUNK)
         quantize_x(0, 1)
+        round_gated(CHUNK, V_END)
         gate_and_round(3 * CHUNK, 4 * CHUNK)
         quantize_x(1, 2)
         gate_and_round(4 * CHUNK, 5 * CHUNK)
@@ -248,99 +253,103 @@ def tile_moe_pre_glu_sigmoid_kernel(
         gate_and_round_on_gpsimd(6)
 
         product_b(0)
-        for c in range(4):
+        for c in range(3):
             product_a(c)
         sigmoid(0)
         product_b(1)
-        product_a(4)
-        sigmoid(1)
         product_b(2)
-        product_a(5)
+        sigmoid(1)
+        for c in range(3, 6):
+            product_a(c)
         sigmoid(2)
         product_b(3)
-        sigmoid(3)
         product_b(4)
-        sigmoid(4)
-        product_b(5)
-        sigmoid(5)
         multiply(0)
+        product_b(5)
+        for c in range(3, 6):
+            sigmoid(c)
         multiply(1)
-        turn_h(0, 2, 3)
+        turn_h(0, 2, 0)
         multiply(2)
         quantize_x(6, 1, tag="sig1")
         gate_and_round_on_gpsimd(7)
         product_a(6)
         product_b(6)
-        copy_turned(0, 2, 3)
+        copy_turned(0, 2, 0)
         sigmoid(6)
         multiply(3)
-        turn_h(2, 2, 1)
-        copy_turned(2, 2, 1)
+        turn_h(2, 2, 2)
+        copy_turned(2, 2, 2)
         multiply(4)
         multiply(5)
-        turn_h(4, 2, 6)
+        turn_h(4, 2, 4)
         quantize_x(7, 1, tag="sig4")
         product_a(7)
         product_b(7)
         sigmoid(7)
         quantize_h(0, 2)
-        second_layer(0, 0, 3, 0)
-        second_layer(2, 0, 1, 0)
-        copy_turned(4, 2, 6, tag="sig4")
+        second_layer(0, 0, 0, 0)
+        second_layer(2, 0, 2, 0)
+        copy_turned(4, 2, 4, tag="sig4")
         multiply(6)
-        turn_h(6, 1, 4)
-        copy_turned(6, 1, 4)
-        second_layer(1, 0, 5, 0)
+        turn_h(6, 1, 6)
+        copy_turned(6, 1, 6)
+        second_layer(1, 0, 7, 0)
         quantize_h(2, 2)
-        copy_y(on_v, 0, 0, 1, 3, 0)
-        second_layer(1, 1, 5, 1)
-        second_layer(2, 1, 1, 1)
-        second_layer(0, 1, 3, 1)
-        copy_y(on_s, 0, 1, 1, 3, 1)
-        copy_y(on_s, 1, 0, 2, 5, 0)
+        copy_y(on_v, 0, 0, 1, 0, 0)
+        second_layer(1, 1, 7, 1)
+        second_layer(2, 1, 2, 1)
+        second_layer(0, 1, 0, 1)
+        copy_y(on_s, 0, 1, 1, 0, 1)
+        copy_y(on_s, 1, 0, 2, 7, 0)
         multiply(7)
-        turn_h(7, 1, 7)
-        copy_turned(7, 1, 7)
+        turn_h(7, 1, 3)
+        copy_turned(7, 1, 3)
         quantize_h(4, 2)
-        second_layer(0, 2, 6, 0)
-        second_layer(3, 0, 2, 0)
-        second_layer(3, 1, 2, 1)
-        second_layer(1, 2, 0, 0)
-        second_layer(2, 2, 0, 1)
-        second_layer(3, 2, 4, 0)
+        second_layer(0, 2, 4, 0)
+        second_layer(3, 0, 5, 0)
+        second_layer(3, 1, 5, 1)
+        second_layer(1, 2, 1, 0)
+        second_layer(2, 2, 1, 1)
+        second_layer(3, 2, 6, 0)
         quantize_h(6, 1)
         y[2] = tile("y2", S, F32, tag="sig7")
-        copy_y(on_v, 2, 0, 2, 1, 0)
-        copy_y(on_v, 0, 2, 1, 6, 0)
-        copy_y(on_s, 3, 0, 2, 2, 0)
-        copy_y(on_s, 1, 2, 1, 0, 0)
-        copy_y(on_s, 2, 2, 1, 0, 1)
+        copy_y(on_v, 2, 0, 2, 2, 0)
+        copy_y(on_v, 0, 2, 1, 4, 0)
+        copy_y(on_s, 3, 0, 2, 5, 0)
+        copy_y(on_s, 1, 2, 1, 1, 0)
+        copy_y(on_s, 2, 2, 1, 1, 1)
         quantize_h(7, 1)
-        second_layer(0, 3, 3, 0)
-        second_layer(1, 3, 5, 0)
-        second_layer(2, 3, 5, 1)
-        second_layer(3, 3, 1, 0)
-        copy_y(on_v, 3, 2, 1, 4, 0)
-        copy_y(on_v, 0, 3, 1, 3, 0)
-        copy_y(on_v, 1, 3, 1, 5, 0)
-        copy_y(on_v, 2, 3, 1, 5, 1)
-        copy_y(on_v, 3, 3, 1, 1, 0)
+        second_layer(0, 3, 0, 0)
+        second_layer(1, 3, 7, 0)
+        second_layer(2, 3, 7, 1)
+        second_layer(3, 3, 2, 0)
+        copy_y(on_v, 3, 2, 1, 6, 0)
+        copy_y(on_v, 0, 3, 1, 0, 0)
+        copy_y(on_v, 1, 3, 1, 7, 0)
+        copy_y(on_v, 2, 3, 1, 7, 1)
+        copy_y(on_v, 3, 3, 1, 2, 0)
 
-        def picked(nt, pos_sb, t0, t1):
+        def picked_y(nt, pos_sb, t0, t1):
             return y[nt][:].indirect(pos_sb[:, t0 // STRIPE : t1 // STRIPE])
 
         def add_second(nt, t0, t1):
-            nc.vector.tensor_tensor(total[nt][:, t0:t1], picked(nt, pos2_sb, t0, t1), first[nt][:, t0:t1], ADD)
+            nc.vector.tensor_tensor(total[nt][:, t0:t1], picked_y(nt, pos2_sb, t0, t1), first[nt][:, t0:t1], ADD)
             nc.sync.dma_start(out[nt * P : (nt + 1) * P, t0:t1], total[nt][:, t0:t1])
 
-        for nt in range(Y_TILES):
-            nc.scalar.activation(first[nt][:], picked(nt, pos1_sb, 0, T), COPY)
-        second = tile("second", T // 2, F32)
-        nc.scalar.activation(second[:], picked(3, pos2_sb, 0, T // 2), COPY)
+        def first_on_s(nt, t0, t1):
+            nc.scalar.activation(first[nt][:, t0:t1], picked_y(nt, pos1_sb, t0, t1), COPY)
+
+        first_on_s(0, 0, T)
+        nc.vector.tensor_copy(first[1][:, 0 : T // 2], picked_y(1, pos1_sb, 0, T // 2))
+        first_on_s(1, T // 2, T)
+        first_on_s(2, 0, T)
+        first_on_s(3, 0, T)
+        second = tile("second", S_SECOND, F32)
+        nc.scalar.activation(second[:], picked_y(3, pos2_sb, 0, S_SECOND), COPY)
         for nt in range(3):
             add_second(nt, 0, T)
-        add_second(3, T // 2, T)
-        for t0, queue in ((T // 4, nc.sync), (0, nc.scalar)):
-            cols = slice(t0, t0 + T // 4)
-            nc.vector.tensor_tensor(total[3][:, cols], first[3][:, cols], second[:, cols], ADD)
-            queue.dma_start(out[3 * P : 4 * P, cols], total[3][:, cols])
+        add_second(3, S_SECOND, T)
+        for t0, t1, queue in ((T // 4, S_SECOND, nc.sync), (0, T // 4, nc.scalar)):
+            nc.vector.tensor_tensor(total[3][:, t0:t1], first[3][:, t0:t1], second[:, t0:t1], ADD)
+            queue.dma_start(out[3 * P : 4 * P, t0:t1], total[3][:, t0:t1])

@@ -39,7 +39,7 @@ S_END = 768
 S_SECOND = 384
 
 A_BANKS = (0, 1, 2, 1, 7, 5, 1, 7)
-B_BANKS = (3, 0, 6, 2, 4, 3, 6, 5)
+B_BANKS = (3, 0, 6, 2, 4, 3, 2, 5)
 
 
 def tile_moe_pre_glu_sigmoid_kernel(
@@ -274,12 +274,12 @@ def tile_moe_pre_glu_sigmoid_kernel(
         quantize_x(6, 1, tag="sig1")
         gate_and_round_on_gpsimd(7)
         product_a(6)
-        product_b(6)
         copy_turned(0, 2, 0)
         sigmoid(6)
         multiply(3)
-        turn_h(2, 2, 2)
-        copy_turned(2, 2, 2)
+        turn_h(2, 2, 6)
+        product_b(6)
+        copy_turned(2, 2, 6)
         multiply(4)
         multiply(5)
         turn_h(4, 2, 4)
@@ -289,16 +289,16 @@ def tile_moe_pre_glu_sigmoid_kernel(
         sigmoid(7)
         quantize_h(0, 2)
         second_layer(0, 0, 0, 0)
-        second_layer(2, 0, 2, 0)
+        second_layer(2, 0, 6, 0)
         copy_turned(4, 2, 4, tag="sig4")
         multiply(6)
-        turn_h(6, 1, 6)
-        copy_turned(6, 1, 6)
+        turn_h(6, 1, 2)
+        copy_turned(6, 1, 2)
         second_layer(1, 0, 7, 0)
         quantize_h(2, 2)
         copy_y(on_v, 0, 0, 1, 0, 0)
         second_layer(1, 1, 7, 1)
-        second_layer(2, 1, 2, 1)
+        second_layer(2, 1, 6, 1)
         second_layer(0, 1, 0, 1)
         copy_y(on_s, 0, 1, 1, 0, 1)
         copy_y(on_s, 1, 0, 2, 7, 0)
@@ -311,10 +311,10 @@ def tile_moe_pre_glu_sigmoid_kernel(
         second_layer(3, 1, 5, 1)
         second_layer(1, 2, 1, 0)
         second_layer(2, 2, 1, 1)
-        second_layer(3, 2, 6, 0)
+        second_layer(3, 2, 2, 0)
         quantize_h(6, 1)
         y[2] = tile("y2", S, F32, tag="sig7")
-        copy_y(on_v, 2, 0, 2, 2, 0)
+        copy_y(on_v, 2, 0, 2, 6, 0)
         copy_y(on_v, 0, 2, 1, 4, 0)
         copy_y(on_s, 3, 0, 2, 5, 0)
         copy_y(on_s, 1, 2, 1, 1, 0)
@@ -323,12 +323,12 @@ def tile_moe_pre_glu_sigmoid_kernel(
         second_layer(0, 3, 0, 0)
         second_layer(1, 3, 7, 0)
         second_layer(2, 3, 7, 1)
-        second_layer(3, 3, 2, 0)
-        copy_y(on_v, 3, 2, 1, 6, 0)
+        second_layer(3, 3, 6, 0)
+        copy_y(on_v, 3, 2, 1, 2, 0)
         copy_y(on_v, 0, 3, 1, 0, 0)
         copy_y(on_v, 1, 3, 1, 7, 0)
         copy_y(on_v, 2, 3, 1, 7, 1)
-        copy_y(on_v, 3, 3, 1, 2, 0)
+        copy_y(on_v, 3, 3, 1, 6, 0)
 
         def picked_y(nt, pos_sb, t0, t1):
             return y[nt][:].indirect(pos_sb[:, t0 // STRIPE : t1 // STRIPE])

@@ -66,7 +66,7 @@ def tile_moe_pre_glu_sigmoid_kernel(
         w_codes = {}
         w_scales = {m: keep.tile([P, E, H], U8, name=f"{m}_scale_bytes", align_bytes=MX_ALIGN) for m in weights}
         identity = tile("identity", P, F32)
-        x_bf16 = tile("x_bf16", PACK * S_END, BF16)
+        x_bf16 = tile("x_bf16", PACK * (S - CHUNK), BF16)
         x_codes, x_scales = {}, {}
         sig = [tile(f"sig{c}", H, F32)[:] for c in range(CHUNKS)]
         h_rows = [tile(f"h_rows{c}", WORDS, F32)[:] for c in range(CHUNKS)]
@@ -141,7 +141,7 @@ def tile_moe_pre_glu_sigmoid_kernel(
             row = gate_rest[:, lo - V_END : hi - V_END].rearrange("p (s o i) -> p s o i", o=1, i=2)
             nc.vector.tensor_tensor(dst, src, row.broadcast_to([P, (hi - lo) // 2, PACK, 2]), MULT)
 
-        last_room = x_bf16[:, PACK * (S_END - CHUNK) : PACK * S_END]
+        last_room = x_bf16[:, PACK * (S - 2 * CHUNK) : PACK * (S - CHUNK)]
 
         def gate_and_round_on_gpsimd(c):
             lo, hi = c * CHUNK, (c + 1) * CHUNK
@@ -249,8 +249,10 @@ def tile_moe_pre_glu_sigmoid_kernel(
         quantize_x(3, 1)
         gate_and_round(5 * CHUNK, 6 * CHUNK)
         quantize_x(4, 1)
+        gate_and_round(6 * CHUNK, 7 * CHUNK)
         quantize_x(5, 1)
-        gate_and_round_on_gpsimd(6)
+        quantize_x(6, 1)
+        gate_and_round_on_gpsimd(7)
 
         product_b(0)
         for c in range(3):
@@ -271,8 +273,6 @@ def tile_moe_pre_glu_sigmoid_kernel(
         multiply(1)
         turn_h(0, 2, 0)
         multiply(2)
-        quantize_x(6, 1, tag="sig1")
-        gate_and_round_on_gpsimd(7)
         product_a(6)
         copy_turned(0, 2, 0)
         sigmoid(6)
@@ -280,17 +280,17 @@ def tile_moe_pre_glu_sigmoid_kernel(
         turn_h(2, 2, 6)
         product_b(6)
         copy_turned(2, 2, 6)
-        multiply(4)
-        multiply(5)
-        turn_h(4, 2, 4)
-        quantize_x(7, 1, tag="sig4")
+        quantize_x(7, 1, tag="sig2")
         product_a(7)
         product_b(7)
         sigmoid(7)
+        multiply(4)
+        multiply(5)
+        turn_h(4, 2, 4)
         quantize_h(0, 2)
         second_layer(0, 0, 0, 0)
         second_layer(2, 0, 6, 0)
-        copy_turned(4, 2, 4, tag="sig4")
+        copy_turned(4, 2, 4, tag="sig2")
         multiply(6)
         turn_h(6, 1, 2)
         copy_turned(6, 1, 2)

@@ -189,9 +189,12 @@ def tile_moe_pre_glu_sigmoid_kernel(
         def sigmoid(c):
             nc.scalar.activation(in_pair_order(sig[c]), pairs_of_bank(banks[A_BANKS[c]]), SIGMOID)
 
-        def multiply(c):
+        def multiply(c, us=slice(0, 2)):
             nc.vector.tensor_tensor(
-                in_pair_order(h_rows[c].bitcast(BF16)), pairs_of_bank(banks[B_BANKS[c]]), in_pair_order(sig[c]), MULT
+                in_pair_order(h_rows[c].bitcast(BF16))[:, us],
+                pairs_of_bank(banks[B_BANKS[c]])[:, us],
+                in_pair_order(sig[c])[:, us],
+                MULT,
             )
 
         def turn_view(count, bank):
@@ -240,17 +243,15 @@ def tile_moe_pre_glu_sigmoid_kernel(
             nc.scalar.activation(staged(2, t), picked_x(2, t), COPY)
 
         round_gated(0, CHUNK)
-        gate_and_round(V_END, 3 * CHUNK)
-        quantize_x(0, 1)
         round_gated(CHUNK, V_END)
-        gate_and_round(3 * CHUNK, 4 * CHUNK)
-        quantize_x(1, 2)
+        quantize_x(0, 1)
+        gate_and_round(V_END, 4 * CHUNK)
+        quantize_x(1, 1)
         gate_and_round(4 * CHUNK, 5 * CHUNK)
-        quantize_x(3, 1)
+        quantize_x(2, 2)
         gate_and_round(5 * CHUNK, 6 * CHUNK)
-        quantize_x(4, 1)
         gate_and_round(6 * CHUNK, 7 * CHUNK)
-        quantize_x(5, 1)
+        quantize_x(4, 2)
         quantize_x(6, 1)
         gate_and_round_on_gpsimd(7)
 
@@ -302,7 +303,8 @@ def tile_moe_pre_glu_sigmoid_kernel(
         second_layer(0, 1, 0, 1)
         copy_y(on_s, 0, 1, 1, 0, 1)
         copy_y(on_s, 1, 0, 2, 7, 0)
-        multiply(7)
+        multiply(7, slice(0, 1))
+        multiply(7, slice(1, 2))
         turn_h(7, 1, 3)
         copy_turned(7, 1, 3)
         quantize_h(4, 2)

@@ -36,7 +36,8 @@ Y_TILES = N // P
 
 V_END = 352
 S_END = 768
-S_SECOND = 384
+V_FIRST = 128
+S_SECOND = 320
 
 A_BANKS = (0, 1, 2, 1, 7, 5, 1, 7)
 B_BANKS = (3, 0, 6, 2, 4, 3, 2, 5)
@@ -68,12 +69,13 @@ def tile_moe_pre_glu_sigmoid_kernel(
         identity = tile("identity", P, F32)
         x_bf16 = tile("x_bf16", PACK * (S - CHUNK), BF16)
         x_codes, x_scales = {}, {}
-        sig = [tile(f"sig{c}", H, F32)[:] for c in range(CHUNKS)]
+        sig = [tile(f"sig{c}", H, F32)[:] for c in range(CHUNKS - 1)]
+        last_sig = [tile(f"last_sig{u}", H // 2, F32)[:] for u in range(2)]
         h_rows = [tile(f"h_rows{c}", WORDS, F32)[:] for c in range(CHUNKS)]
         h_turned = {}
         h_codes = [tile(f"h_codes{e}", C, U32) for e in range(E)]
         h_scales = [tile(f"h_scales{e}", C, U8) for e in range(E)]
-        y = {nt: tile(f"y{nt}", S, F32) for nt in (0, 1, 3)}
+        y = {nt: tile(f"y{nt}", S, F32) for nt in (1, 3)}
         first = [tile(f"first{nt}", T, F32) for nt in range(Y_TILES)]
         total = [tile(f"total{nt}", T, F32) for nt in range(Y_TILES)]
         banks = [psum.tile([P, BANK], F32, name=f"bank{j}") for j in range(BANKS)]
@@ -189,11 +191,20 @@ def tile_moe_pre_glu_sigmoid_kernel(
         def sigmoid(c):
             nc.scalar.activation(in_pair_order(sig[c]), pairs_of_bank(banks[A_BANKS[c]]), SIGMOID)
 
-        def multiply(c, us=slice(0, 2)):
+        def multiply(c):
             nc.vector.tensor_tensor(
-                in_pair_order(h_rows[c].bitcast(BF16))[:, us],
-                pairs_of_bank(banks[B_BANKS[c]])[:, us],
-                in_pair_order(sig[c])[:, us],
+                in_pair_order(h_rows[c].bitcast(BF16)), pairs_of_bank(banks[B_BANKS[c]]), in_pair_order(sig[c]), MULT
+            )
+
+        def last_sigmoid(u):
+            pairs = last_sig[u].rearrange("s (q e) -> s q e", e=2)
+            nc.scalar.activation(pairs, pairs_of_bank(banks[A_BANKS[-1]])[:, u], SIGMOID)
+
+        def last_multiply(u):
+            nc.vector.tensor_tensor(
+                in_pair_order(h_rows[-1].bitcast(BF16))[:, u],
+                pairs_of_bank(banks[B_BANKS[-1]])[:, u],
+                last_sig[u].rearrange("s (q e) -> s q e", e=2),
                 MULT,
             )
 
@@ -284,7 +295,8 @@ def tile_moe_pre_glu_sigmoid_kernel(
         quantize_x(7, 1, tag="sig2")
         product_a(7)
         product_b(7)
-        sigmoid(7)
+        last_sigmoid(0)
+        last_sigmoid(1)
         multiply(4)
         multiply(5)
         turn_h(4, 2, 4)
@@ -295,42 +307,41 @@ def tile_moe_pre_glu_sigmoid_kernel(
         multiply(6)
         turn_h(6, 1, 2)
         copy_turned(6, 1, 2)
-        second_layer(1, 0, 7, 0)
         quantize_h(2, 2)
-        copy_y(on_v, 0, 0, 1, 0, 0)
-        second_layer(1, 1, 7, 1)
-        second_layer(2, 1, 6, 1)
         second_layer(0, 1, 0, 1)
+        second_layer(2, 1, 6, 1)
+        last_multiply(0)
+        last_multiply(1)
+        y[0] = tile("y0", S, F32, tag="last_sig0")
         copy_y(on_s, 0, 1, 1, 0, 1)
-        copy_y(on_s, 1, 0, 2, 7, 0)
-        multiply(7, slice(0, 1))
-        multiply(7, slice(1, 2))
         turn_h(7, 1, 3)
         copy_turned(7, 1, 3)
+        second_layer(1, 0, 2, 0)
+        second_layer(1, 1, 2, 1)
         quantize_h(4, 2)
         second_layer(0, 2, 4, 0)
         second_layer(3, 0, 5, 0)
         second_layer(3, 1, 5, 1)
+        second_layer(3, 2, 7, 0)
         second_layer(1, 2, 1, 0)
-        second_layer(2, 2, 1, 1)
-        second_layer(3, 2, 2, 0)
         quantize_h(6, 1)
-        y[2] = tile("y2", S, F32, tag="sig7")
+        y[2] = tile("y2", S, F32, tag="last_sig1")
         copy_y(on_v, 2, 0, 2, 6, 0)
-        copy_y(on_v, 0, 2, 1, 4, 0)
+        second_layer(2, 2, 6, 0)
+        copy_y(on_s, 1, 0, 2, 2, 0)
+        copy_y(on_s, 0, 2, 1, 4, 0)
         copy_y(on_s, 3, 0, 2, 5, 0)
-        copy_y(on_s, 1, 2, 1, 1, 0)
-        copy_y(on_s, 2, 2, 1, 1, 1)
         quantize_h(7, 1)
-        second_layer(0, 3, 0, 0)
-        second_layer(1, 3, 7, 0)
-        second_layer(2, 3, 7, 1)
-        second_layer(3, 3, 6, 0)
-        copy_y(on_v, 3, 2, 1, 2, 0)
-        copy_y(on_v, 0, 3, 1, 0, 0)
-        copy_y(on_v, 1, 3, 1, 7, 0)
-        copy_y(on_v, 2, 3, 1, 7, 1)
-        copy_y(on_v, 3, 3, 1, 6, 0)
+        second_layer(0, 3, 3, 0)
+        second_layer(1, 3, 1, 1)
+        second_layer(2, 3, 6, 1)
+        second_layer(3, 3, 2, 0)
+        copy_y(on_v, 0, 0, 1, 0, 0)
+        copy_y(on_v, 3, 2, 1, 7, 0)
+        copy_y(on_v, 0, 3, 1, 3, 0)
+        copy_y(on_v, 1, 2, 2, 1, 0)
+        copy_y(on_v, 2, 2, 2, 6, 0)
+        copy_y(on_v, 3, 3, 1, 2, 0)
 
         def picked_y(nt, pos_sb, t0, t1):
             return y[nt][:].indirect(pos_sb[:, t0 // STRIPE : t1 // STRIPE])
@@ -343,8 +354,8 @@ def tile_moe_pre_glu_sigmoid_kernel(
             nc.scalar.activation(first[nt][:, t0:t1], picked_y(nt, pos1_sb, t0, t1), COPY)
 
         first_on_s(0, 0, T)
-        nc.vector.tensor_copy(first[1][:, 0 : T // 2], picked_y(1, pos1_sb, 0, T // 2))
-        first_on_s(1, T // 2, T)
+        nc.vector.tensor_copy(first[1][:, 0:V_FIRST], picked_y(1, pos1_sb, 0, V_FIRST))
+        first_on_s(1, V_FIRST, T)
         first_on_s(2, 0, T)
         first_on_s(3, 0, T)
         second = tile("second", S_SECOND, F32)

@@ -25,7 +25,7 @@ P = 128
 PACK = 4
 QUAD = 32
 STRIPE = 16
-MX_ALIGN = 64
+MX_ALIGN = 256
 CHUNK = 128
 CHUNKS = S // CHUNK
 BANK = 512

from contextlib import ExitStack

import concourse.mybir as mybir
from concourse.masks import make_identity

K, T, E, C, H, N = 512, 512, 4, 256, 512, 512
S = E * C
FLOPS = 2 * S * (2 * K * H + H * N)
BYTES = 4 * (K * T + N * T + S) + E * (2 * K * H + H * N) * 17 // 32 + 2 * 8 * (S + 2 * T)

F32 = mybir.dt.float32
BF16 = mybir.dt.bfloat16
I32 = mybir.dt.int32
U32 = mybir.dt.uint32
U16 = mybir.dt.uint16
U8 = mybir.dt.uint8
FP8X4 = mybir.dt.float8_e4m3fn_x4
FP4X4 = mybir.dt.float4_e2m1fn_x4
MULT = mybir.AluOpType.mult
ADD = mybir.AluOpType.add
SIGMOID = mybir.ActivationFunctionType.Sigmoid
COPY = mybir.ActivationFunctionType.Copy

P = 128
PACK = 4
QUAD = 32
STRIPE = 16
MX_ALIGN = 256
CHUNK = 128
CHUNKS = S // CHUNK
BANK = 512
BANKS = 8
WORDS = H // 2
Y_TILES = N // P


V_END = 352
S_END = 768
V_FIRST = 128
S_SECOND = 320

A_BANKS = (0, 1, 2, 1, 7, 5, 1, 7)
B_BANKS = (3, 0, 6, 2, 4, 3, 2, 5)


def tile_moe_pre_glu_sigmoid_kernel(
    tc, xT, w1_words, w1_scales, w3_words, w3_scales, w2_words, w2_scales, gate, offs, pos1, pos2, out
):
    nc = tc.nc
    weights = {"w1": (w1_words, w1_scales), "w3": (w3_words, w3_scales), "w2": (w2_words, w2_scales)}
    groups = ((0, V_END), (V_END, S_END), (S_END, S))

    with ExitStack() as ctx:
        keep = ctx.enter_context(tc.tile_pool(name="keep", bufs=1))
        psum = ctx.enter_context(tc.psum_pool(name="psum", bufs=1))

        def tile(name, width, dtype, tag=None):
            return keep.tile([P, width], dtype, name=name, tag=tag or name, align_bytes=MX_ALIGN)

        offs_sb = keep.tile([P, S // STRIPE], U16, name="offs_sb")
        pos1_sb = keep.tile([P, T // STRIPE], U16, name="pos1_sb")
        pos2_sb = keep.tile([P, T // STRIPE], U16, name="pos2_sb")
        x_phase = [tile(f"x_phase{t}", T, F32) for t in range(PACK)]
        gate_first = tile("gate_first", V_END, F32)
        gate_rest = tile("gate_rest", S - V_END, F32)
        stage = {g: tile(f"stage{g}", PACK * (groups[g][1] - groups[g][0]), F32)[:] for g in range(2)}
        w_codes = {}
        w_scales = {m: keep.tile([P, E, H], U8, name=f"{m}_scale_bytes", align_bytes=MX_ALIGN) for m in weights}
        identity = tile("identity", P, F32)
        x_bf16 = tile("x_bf16", PACK * (S - CHUNK), BF16)
        x_codes, x_scales = {}, {}
        sig = [tile(f"sig{c}", H, F32)[:] for c in range(CHUNKS - 1)]
        last_sig = [tile(f"last_sig{u}", H // 2, F32)[:] for u in range(2)]
        h_rows = [tile(f"h_rows{c}", WORDS, F32)[:] for c in range(CHUNKS)]
        h_turned = {}
        h_codes = [tile(f"h_codes{e}", C, U32) for e in range(E)]
        h_scales = [tile(f"h_scales{e}", C, U8) for e in range(E)]
        y = {nt: tile(f"y{nt}", S, F32) for nt in (1, 3)}
        first = [tile(f"first{nt}", T, F32) for nt in range(Y_TILES)]
        total = [tile(f"total{nt}", T, F32) for nt in range(Y_TILES)]
        banks = [psum.tile([P, BANK], F32, name=f"bank{j}") for j in range(BANKS)]

        warm_in = keep.tile([P, 8], F32, name="warm_in")
        warm_out = keep.tile([P, 8], F32, name="warm_out")
        nc.vector.memset(warm_in[:], 0.0)
        make_identity(nc, identity[:])
        for m in weights:
            nc.vector.memset(w_scales[m][:].rearrange("p e n -> p (e n)").bitcast(I32), 0)

        x_rows = xT.rearrange("(p t) n -> t p n", t=PACK)

        def load_codes(m, e0, count):
            held = keep.tile([P, count, 2 * H], U8, name=f"{m}_codes{e0}", align_bytes=MX_ALIGN)
            src = weights[m][0].rearrange("e s p b -> p (e s) b")
            nc.sync.dma_start(held[:].bitcast(I32), src[:, e0 : e0 + count, :].bitcast(I32))
            for j in range(count):
                w_codes[m, e0 + j] = held[:, j, :]

        def load_scales(*names):
            for q in (0, 2, 1, 3):
                for m in names:
                    src = weights[m][1].rearrange("e s (q r) n -> q r (e s) n", r=4)
                    nc.sync.dma_start(w_scales[m][QUAD * q : QUAD * q + 4, :, :].bitcast(I32), src[q].bitcast(I32))

        nc.scalar.activation(warm_out[:], warm_in[:], SIGMOID)
        nc.sync.dma_start(x_phase[0][:], x_rows[0])
        nc.sync.dma_start(offs_sb[:], offs)
        nc.sync.dma_start(gate_first[:], gate[0:P, 0:V_END])
        for t in range(1, PACK):
            nc.sync.dma_start(x_phase[t][:], x_rows[t])
        nc.sync.dma_start(gate_rest[:], gate[0:P, V_END:S])
        load_scales("w1", "w3")
        load_codes("w3", 0, 1)
        load_codes("w1", 0, 1)
        load_codes("w1", 1, 1)
        load_codes("w3", 1, 1)
        load_codes("w1", 2, 2)
        load_codes("w3", 2, 2)
        load_scales("w2")
        load_codes("w2", 0, 2)
        load_codes("w2", 2, 2)
        nc.sync.dma_start(pos1_sb[:], pos1)
        nc.sync.dma_start(pos2_sb[:], pos2)

        def picked_x(g, t):
            return x_phase[t][:].indirect(offs_sb[:, groups[g][0] // STRIPE : groups[g][1] // STRIPE])

        def staged(g, t):
            width = groups[g][1] - groups[g][0]
            return stage[g][:, t * width : (t + 1) * width]

        def staged_slots(lo, hi):
            g = max(j for j in range(len(groups)) if groups[j][0] <= lo)
            return stage[g].rearrange("p (t s) -> p t s", t=PACK)[:, :, lo - groups[g][0] : hi - groups[g][0]]

        def round_gated(lo, hi):
            src = staged_slots(lo, hi).rearrange("p t (s i) -> p s t i", i=4)
            nc.vector.tensor_copy(x_bf16[:, PACK * lo : PACK * hi].rearrange("p (s i t) -> p s t i", i=4, t=PACK), src)

        def gate_and_round(lo, hi):
            src = staged_slots(lo, hi).rearrange("p t (s i) -> p s t i", i=2)
            dst = x_bf16[:, PACK * lo : PACK * hi].rearrange("p (s i t) -> p s t i", i=2, t=PACK)
            row = gate_rest[:, lo - V_END : hi - V_END].rearrange("p (s o i) -> p s o i", o=1, i=2)
            nc.vector.tensor_tensor(dst, src, row.broadcast_to([P, (hi - lo) // 2, PACK, 2]), MULT)

        last_room = x_bf16[:, PACK * (S - 2 * CHUNK) : PACK * (S - CHUNK)]

        def gate_and_round_on_gpsimd(c):
            lo, hi = c * CHUNK, (c + 1) * CHUNK
            row = gate_rest[:, lo - V_END : hi - V_END].rearrange("p (s o) -> p s o", o=1)
            nc.gpsimd.tensor_tensor(
                last_room.rearrange("p (s t) -> p s t", t=PACK),
                staged_slots(lo, hi).rearrange("p t s -> p s t"),
                row.broadcast_to([P, CHUNK, PACK]),
                MULT,
            )

        def quantize_x(c0, count, tag=None):
            codes = tile(f"x_codes{c0}", count * CHUNK, U32, tag=tag)[:]
            scales = tile(f"x_scales{c0}", count * CHUNK, U8)[:]
            for j in range(count):
                x_codes[c0 + j] = codes[:, j * CHUNK : (j + 1) * CHUNK]
                x_scales[c0 + j] = scales[:, j * CHUNK : (j + 1) * CHUNK]
            src = last_room if c0 * CHUNK >= S_END else x_bf16[:, PACK * CHUNK * c0 : PACK * CHUNK * (c0 + count)]
            nc.vector.quantize_mx(codes.bitcast(FP8X4), scales, src)

        def pairs_of_bank(bank):
            return bank[:].rearrange("s (q u e) -> s u q e", u=2, e=2)

        def in_pair_order(rows):
            return rows.rearrange("s (u q e) -> s u q e", u=2, e=2)

        def first_layer(c, m, bank):
            expert = c * CHUNK // C
            nc.tensor.matmul_mx(
                bank[:],
                lhsT=x_codes[c].bitcast(FP8X4),
                lhsT_scale=x_scales[c],
                rhs=w_codes[m, expert].bitcast(FP4X4),
                rhs_scale=w_scales[m][:, expert, :],
                start=True,
                stop=True,
            )

        def product_a(c):
            first_layer(c, "w1", banks[A_BANKS[c]])

        def product_b(c):
            first_layer(c, "w3", banks[B_BANKS[c]])

        def sigmoid(c):
            nc.scalar.activation(in_pair_order(sig[c]), pairs_of_bank(banks[A_BANKS[c]]), SIGMOID)

        def multiply(c):
            nc.vector.tensor_tensor(
                in_pair_order(h_rows[c].bitcast(BF16)), pairs_of_bank(banks[B_BANKS[c]]), in_pair_order(sig[c]), MULT
            )

        def last_sigmoid(u):
            pairs = last_sig[u].rearrange("s (q e) -> s q e", e=2)
            nc.scalar.activation(pairs, pairs_of_bank(banks[A_BANKS[-1]])[:, u], SIGMOID)

        def last_multiply(u):
            nc.vector.tensor_tensor(
                in_pair_order(h_rows[-1].bitcast(BF16))[:, u],
                pairs_of_bank(banks[B_BANKS[-1]])[:, u],
                last_sig[u].rearrange("s (q e) -> s q e", e=2),
                MULT,
            )

        def turn_view(count, bank):
            return banks[bank][:, 0 : 2 * CHUNK * count].rearrange("q (c u s) -> q c u s", u=2, s=CHUNK)

        def turn_h(c0, count, bank):
            for j in range(count):
                for u in range(2):
                    nc.tensor.transpose(turn_view(count, bank)[:, j, u, :], h_rows[c0 + j][:, u * P : (u + 1) * P], identity[:])

        def copy_turned(c0, count, bank, tag=None):
            h_turned[c0] = tile(f"h_turned{c0}", count * CHUNK * PACK, BF16, tag=tag)
            dst = h_turned[c0][:].bitcast(F32).rearrange("q (c s u) -> q c s u", u=2, s=CHUNK)
            nc.scalar.copy(dst, turn_view(count, bank).rearrange("q c u s -> q c s u"))

        def quantize_h(c0, count):
            expert, lo = divmod(c0 * CHUNK, C)
            hi = lo + count * CHUNK
            nc.vector.quantize_mx(h_codes[expert][:, lo:hi].bitcast(FP8X4), h_scales[expert][:, lo:hi], h_turned[c0][:])

        def second_layer(nt, expert, bank, half):
            nc.tensor.matmul_mx(
                banks[bank][:, half * C : (half + 1) * C],
                lhsT=w_codes["w2", expert][:, 2 * P * nt : 2 * P * (nt + 1)].bitcast(FP4X4),
                lhsT_scale=w_scales["w2"][:, expert, P * nt : P * (nt + 1)],
                rhs=h_codes[expert][:].bitcast(FP8X4),
                rhs_scale=h_scales[expert][:],
                start=True,
                stop=True,
            )

        def copy_y(copy, nt, e0, count, bank, half):
            copy(y[nt][:, e0 * C : (e0 + count) * C], banks[bank][:, half * C : (half + count) * C])

        on_s, on_v = nc.scalar.copy, nc.vector.tensor_copy

        for t in range(PACK - 1):
            nc.vector.tensor_tensor(staged(0, t), picked_x(0, t), gate_first[:], MULT)
        for lo, hi in ((0, CHUNK), (CHUNK, V_END)):
            picked = x_phase[PACK - 1][:].indirect(offs_sb[:, lo // STRIPE : hi // STRIPE])
            nc.vector.tensor_tensor(staged(0, PACK - 1)[:, lo:hi], picked, gate_first[:, lo:hi], MULT)
        for t in range(PACK):
            nc.scalar.activation(staged(1, t), picked_x(1, t), COPY)
        stage[2] = tile("late_stage", PACK * (S - S_END), F32, tag="gate_first")[:]
        for t in range(PACK):
            nc.scalar.activation(staged(2, t), picked_x(2, t), COPY)

        round_gated(0, CHUNK)
        round_gated(CHUNK, V_END)
        quantize_x(0, 1)
        gate_and_round(V_END, 4 * CHUNK)
        quantize_x(1, 1)
        gate_and_round(4 * CHUNK, 5 * CHUNK)
        quantize_x(2, 2)
        gate_and_round(5 * CHUNK, 6 * CHUNK)
        gate_and_round(6 * CHUNK, 7 * CHUNK)
        quantize_x(4, 2)
        quantize_x(6, 1)
        gate_and_round_on_gpsimd(7)

        product_b(0)
        for c in range(3):
            product_a(c)
        sigmoid(0)
        product_b(1)
        product_b(2)
        sigmoid(1)
        for c in range(3, 6):
            product_a(c)
        sigmoid(2)
        product_b(3)
        product_b(4)
        multiply(0)
        product_b(5)
        for c in range(3, 6):
            sigmoid(c)
        multiply(1)
        turn_h(0, 2, 0)
        multiply(2)
        product_a(6)
        copy_turned(0, 2, 0)
        sigmoid(6)
        multiply(3)
        turn_h(2, 2, 6)
        product_b(6)
        copy_turned(2, 2, 6)
        quantize_x(7, 1, tag="sig2")
        product_a(7)
        product_b(7)
        last_sigmoid(0)
        last_sigmoid(1)
        multiply(4)
        multiply(5)
        turn_h(4, 2, 4)
        quantize_h(0, 2)
        second_layer(0, 0, 0, 0)
        second_layer(2, 0, 6, 0)
        copy_turned(4, 2, 4, tag="sig2")
        multiply(6)
        turn_h(6, 1, 2)
        copy_turned(6, 1, 2)
        quantize_h(2, 2)
        second_layer(0, 1, 0, 1)
        second_layer(2, 1, 6, 1)
        last_multiply(0)
        last_multiply(1)
        y[0] = tile("y0", S, F32, tag="last_sig0")
        copy_y(on_s, 0, 1, 1, 0, 1)
        turn_h(7, 1, 3)
        copy_turned(7, 1, 3)
        second_layer(1, 0, 2, 0)
        second_layer(1, 1, 2, 1)
        quantize_h(4, 2)
        second_layer(0, 2, 4, 0)
        second_layer(3, 0, 5, 0)
        second_layer(3, 1, 5, 1)
        second_layer(3, 2, 7, 0)
        second_layer(1, 2, 1, 0)
        quantize_h(6, 1)
        y[2] = tile("y2", S, F32, tag="last_sig1")
        copy_y(on_v, 2, 0, 2, 6, 0)
        second_layer(2, 2, 6, 0)
        copy_y(on_s, 1, 0, 2, 2, 0)
        copy_y(on_s, 0, 2, 1, 4, 0)
        copy_y(on_s, 3, 0, 2, 5, 0)
        quantize_h(7, 1)
        second_layer(0, 3, 3, 0)
        second_layer(1, 3, 1, 1)
        second_layer(2, 3, 6, 1)
        second_layer(3, 3, 2, 0)
        copy_y(on_v, 0, 0, 1, 0, 0)
        copy_y(on_v, 3, 2, 1, 7, 0)
        copy_y(on_v, 0, 3, 1, 3, 0)
        copy_y(on_v, 1, 2, 2, 1, 0)
        copy_y(on_v, 2, 2, 2, 6, 0)
        copy_y(on_v, 3, 3, 1, 2, 0)

        def picked_y(nt, pos_sb, t0, t1):
            return y[nt][:].indirect(pos_sb[:, t0 // STRIPE : t1 // STRIPE])

        def add_second(nt, t0, t1):
            nc.vector.tensor_tensor(total[nt][:, t0:t1], picked_y(nt, pos2_sb, t0, t1), first[nt][:, t0:t1], ADD)
            nc.sync.dma_start(out[nt * P : (nt + 1) * P, t0:t1], total[nt][:, t0:t1])

        def first_on_s(nt, t0, t1):
            nc.scalar.activation(first[nt][:, t0:t1], picked_y(nt, pos1_sb, t0, t1), COPY)

        first_on_s(0, 0, T)
        nc.vector.tensor_copy(first[1][:, 0:V_FIRST], picked_y(1, pos1_sb, 0, V_FIRST))
        first_on_s(1, V_FIRST, T)
        first_on_s(2, 0, T)
        first_on_s(3, 0, T)
        second = tile("second", S_SECOND, F32)
        nc.scalar.activation(second[:], picked_y(3, pos2_sb, 0, S_SECOND), COPY)
        for nt in range(3):
            add_second(nt, 0, T)
        add_second(3, S_SECOND, T)
        for t0, t1, queue in ((T // 4, S_SECOND, nc.sync), (0, T // 4, nc.scalar)):
            nc.vector.tensor_tensor(total[3][:, t0:t1], first[3][:, t0:t1], second[:, t0:t1], ADD)
            queue.dma_start(out[3 * P : 4 * P, t0:t1], total[3][:, t0:t1])
